import numpy as np
import ml_dtypes


def mxq(x, axis, fmt="e4m3"):
    dtype, down = {"e4m3": (ml_dtypes.float8_e4m3fn, 7), "e5m2": (ml_dtypes.float8_e5m2, 14)}[fmt]
    v = np.moveaxis(np.asarray(x, np.float32).astype(ml_dtypes.bfloat16).astype(np.float64), axis, -1)
    blocks = v.reshape(v.shape[:-1] + (-1, 32))
    amax = np.abs(blocks).max(-1, keepdims=True)
    byte = np.maximum(np.where(amax > 0, np.frexp(amax)[1] - 1 + 127, 0) - down, 1)
    scale = np.exp2(byte - 127.0)
    codes = (blocks / scale).astype(np.float32).astype(dtype).astype(np.float64)
    return np.moveaxis((codes * scale).reshape(v.shape), -1, axis)


WIDE = False


def mx_kscale(k):
    if not WIDE:
        return np.ones(k)
    levels = np.array([30, -30])
    if k % 512:
        return np.exp2(np.random.permutation(np.resize(levels, k // 32))).repeat(32)
    a = np.empty((k // 512, 16))
    for p in range(k // 512):
        a[p, :8] = np.random.permutation(np.resize(levels, 8))
        for g in range(8):
            far = levels[np.abs(levels - a[p, g]) >= 10]
            a[p, g + 8] = far[np.random.randint(len(far))]
    return np.exp2(a.ravel()).repeat(32)


def f64(x):
    return np.asarray(x).astype(np.float64)


def striped(idx):
    return np.tile(idx.reshape(-1, 16).T, (8, 1)).astype(np.uint16)


def unstriped(offs):
    return offs[:16].T.reshape(-1).astype(np.int64)


def bf(x):
    return np.asarray(x, np.float32).astype(ml_dtypes.bfloat16)


E2M1 = np.array([0.0, 0.5, 1.0, 1.5, 2.0, 3.0, 4.0, 6.0, -0.0, -0.5, -1.0, -1.5, -2.0, -3.0, -4.0, -6.0])


def pack_weight(w, fmt):
    k, n = w.shape
    w = f64(bf(w)).reshape(k // 32, 32, n)
    amax = np.abs(w).max(1)
    if fmt in ("e4m3", "e5m2"):
        byte = np.frexp(amax)[1] - 1 + 127 - (7 if fmt == "e4m3" else 14)
    else:
        mant, ex = np.frexp(amax / 6.0)
        byte = np.where(mant > 0.5, ex, ex - 1) + 127
    byte = np.clip(np.where(amax > 0, byte, 1), 1, 254)
    scaled = (w * np.exp2(127.0 - byte)[:, None, :]).reshape(k, n).astype(np.float32)
    by_word = np.ascontiguousarray(scaled.reshape(k // 512, 128, 4, n).transpose(0, 1, 3, 2))
    if fmt in ("e4m3", "e5m2"):
        words = by_word.astype(ml_dtypes.float8_e4m3fn if fmt == "e4m3" else ml_dtypes.float8_e5m2).view(np.uint8)
    else:
        c = by_word.astype(ml_dtypes.float4_e2m1fn).view(np.uint8) & 0xF
        words = c[..., 0::2] | (c[..., 1::2] << 4)
    return np.ascontiguousarray(words), np.ascontiguousarray(byte.astype(np.uint8).reshape(k // 512, 16, n))


def unpack_weight(words, scales, fmt):
    g, p, n, _ = words.shape
    if fmt in ("e4m3", "e5m2"):
        vals = np.ascontiguousarray(words).view(ml_dtypes.float8_e4m3fn if fmt == "e4m3" else ml_dtypes.float8_e5m2).astype(np.float64)
    else:
        nib = np.empty((g, p, n, 4), np.uint8)
        nib[..., 0::2] = words & 0xF
        nib[..., 1::2] = words >> 4
        vals = E2M1[nib]
    vals = vals * np.repeat(np.exp2(scales.astype(np.float64) - 127.0), 8, axis=1)[..., None]
    return vals.transpose(0, 1, 3, 2).reshape(g * 512, n)


def planes(Y):
    n, m = Y.shape
    b = f64(bf(Y)).reshape(n // 32, 32, m)
    amax = np.abs(b).max(1)
    byte = np.clip(np.where(amax > 0, np.frexp(amax)[1] - 1 + 127 - 7, 1), 1, 254)
    codes = (b * np.exp2(127.0 - byte)[:, None, :]).reshape(n, m).astype(np.float32).astype(ml_dtypes.float8_e4m3fn).view(np.uint8)
    words = codes.reshape(n // 512, 128, 4, m).transpose(0, 1, 3, 2)
    return np.ascontiguousarray(words), np.ascontiguousarray(byte.astype(np.uint8).reshape(n // 512, 16, m))


K, T, S, H, N, T2 = 1024, 2048, 1024, 1024, 512, 2048

def setup_inputs():
    n = np.random.standard_normal
    s = mx_kscale(K)[:, None]
    u = mx_kscale(H)[:, None]
    tab_words, tab_scales = pack_weight(n((K, T)) * np.exp(1.0 * n((1, T))) * s, "e5m2")
    w2_words, w2_scales = pack_weight(4.0 * n((H, N)) * np.exp(0.8 * n((1, N))) / np.sqrt(H) / u, "e4m3")
    return {
        "tab_words": tab_words, "tab_scales": tab_scales,
        "offs": striped(np.random.permutation(T)[:S]),
        "w1": (0.4 * n((K, H)) / np.sqrt(K) / s).astype(np.float32),
        "target": (0.5 * n(H)).astype(np.float32),
        "sT": (n((H, T)) * u).astype(np.float32),
        "w2_words": w2_words, "w2_scales": w2_scales,
        "wgo": np.exp(0.3 * n((128, S))).astype(np.float32),
        "offs2": striped(np.random.permutation(T2)[:S]),
    }

def reference(tab_words, tab_scales, offs, w1, target, sT, w2_words, w2_scales, wgo, offs2):
    v = unpack_weight(tab_words, tab_scales, "e5m2")[:, unstriped(offs)]
    h = mxq(f64(w1), 0, "e4m3").T @ v
    res = h - f64(target)[:, None]
    trusted = res * np.exp(-np.square(res))
    s_ = f64(sT)[:, unstriped(offs)]
    z = trusted * np.maximum(s_, 0.0)
    w2 = unpack_weight(w2_words, w2_scales, "e4m3")
    step = w2.T @ mxq(z, 0, "e4m3")
    y = np.zeros((N, T2))
    y[:, unstriped(offs2)] = np.tile(f64(wgo), (N // 128, 1)) * step
    words, scales = planes(y)
    return y, words, scales

@@ -1,0 +1,274 @@
+from contextlib import ExitStack
+
+import concourse.mybir as mybir
+
+K, T, S, H, N, T2 = 1024, 2048, 1024, 1024, 512, 2048
+FLOPS = 2 * K * H * S + 2 * H * N * S
+
+F32 = mybir.dt.float32
+BF16 = mybir.dt.bfloat16
+I32 = mybir.dt.int32
+U32 = mybir.dt.uint32
+U16 = mybir.dt.uint16
+U8 = mybir.dt.uint8
+E4M3 = mybir.dt.float8_e4m3fn_x4
+E5M2 = mybir.dt.float8_e5m2_x4
+ACT = mybir.ActivationFunctionType
+ALU = mybir.AluOpType
+
+P = 128
+PACK = 4
+KP = P * PACK
+HALF = 512
+LCOL = HALF // 16
+CHUNK = 512
+
+
+def tile_list_coil_trust_weighting_kernel(
+    tc, tab_words, tab_scales, offs, w1, target, sT, w2_words, w2_scales, wgo, offs2, out_0, out_1, out_2
+):
+    nc = tc.nc
+    with ExitStack() as ctx:
+        keep = ctx.enter_context(tc.tile_pool(name="keep", bufs=1))
+        ring = ctx.enter_context(tc.tile_pool(name="ring", bufs=1))
+        psum = ctx.enter_context(tc.psum_pool(name="psum", bufs=4))
+
+        def stream(shape, dtype, name):
+            return ring.tile(shape, dtype, name=name, tag="stream", bufs=8, align_bytes=64)
+
+        def grouped(name):
+            return ring.tile([P, PACK * HALF], BF16, name=name, tag="grouped", bufs=4, align_bytes=64)
+
+        pick = keep.tile([P, S // 16], U16, name="pick")
+        place = keep.tile([P, S // 16], U16, name="place")
+        tsc = keep.tile([P, 2, T], U8, name="tsc", align_bytes=64)
+        vsc = [keep.tile([P, S], U8, name="vsc%d" % a, align_bytes=64) for a in range(2)]
+        vw = [keep.tile([P, S], U32, name="vw%d" % a, align_bytes=64) for a in range(2)]
+        w2sc_raw = keep.tile([P, N], U8, name="w2sc_raw", align_bytes=64)
+        w2sc = keep.tile([P, N], U8, name="w2sc", align_bytes=64)
+        w2w = keep.tile([P, 2, N], I32, name="w2w", align_bytes=64)
+        tgt = keep.tile([P, 2, PACK], F32, name="tgt")
+        ntgt = keep.tile([P, 2 * PACK], F32, name="ntgt")
+        gain = keep.tile([P, PACK, S], F32, name="gain")
+        pages = {t: keep.tile([P, T2], F32, name="page%d" % t) for t in range(2)}
+        ycodes = keep.tile([P, T2], U32, name="ycodes", align_bytes=64)
+        yscales = keep.tile([P, T2], U8, name="yscales", align_bytes=64)
+
+        nc.vector.memset(tsc[:].rearrange("p a t -> p (a t)").bitcast(I32), 0)
+        nc.vector.memset(w2sc_raw[:].bitcast(I32), 0)
+        for t in range(2):
+            nc.vector.memset(pages[t][:], 0.0)
+
+        nc.sync.dma_start(pick[:], offs)
+        tabw = {}
+        w1raw = {}
+        margins = {}
+
+        def load_tab(a):
+            tabw[a] = stream([P, T], U32, "tabw")
+            nc.sync.dma_start(tabw[a][:].bitcast(I32), tab_words[a].rearrange("p t i -> p (t i)").bitcast(I32))
+
+        def load_w1(a, b):
+            w1raw[a, b] = stream([P, PACK, KP], F32, "w1raw")
+            rows = w1[KP * a : KP * (a + 1), KP * b : KP * (b + 1)]
+            nc.sync.dma_start(w1raw[a, b][:], rows.rearrange("(p j) c -> p j c", j=PACK))
+
+        sT_v = sT.rearrange("(b p t) c -> b t p c", b=2, t=PACK)
+
+        def load_margins(b, t):
+            if b == 0 and t < 2:
+                margins[b, t] = ring.tile([P, T], F32, name="margins", tag="then_page%d" % t, bufs=1)
+            else:
+                margins[b, t] = stream([P, T], F32, "margins")
+            nc.sync.dma_start(margins[b, t][:], sT_v[b, t])
+
+        load_tab(0)
+        for q in range(4):
+            nc.sync.dma_start(
+                tsc[32 * q : 32 * q + 4].bitcast(I32),
+                tab_scales[:, 4 * q : 4 * q + 4, :].rearrange("a r t -> r a t").bitcast(I32),
+            )
+        load_w1(0, 0)
+        load_w1(1, 0)
+        load_tab(1)
+        nc.sync.dma_start(tgt[:], target.rearrange("(b p t) -> p b t", b=2, t=PACK))
+        for t in range(PACK):
+            load_margins(0, t)
+
+        nc.scalar.mul(ntgt[:], tgt[:].rearrange("p b t -> p (b t)"), -1.0)
+
+        nc.vector.tensor_copy(vw[0][:], tabw[0][:].indirect(pick[:]))
+        for a in range(2):
+            nc.vector.tensor_copy(vsc[a][:], tsc[:, a, :].indirect(pick[:]))
+
+        w1c = {}
+        w1s = {}
+
+        def quant_w1(a, b, scalar_m):
+            g = grouped("w1bf")
+            dst = g[:].rearrange("p (t m j) -> p m j t", t=PACK, j=PACK)
+            src = w1raw[a, b][:].rearrange("p j (m t) -> p m j t", t=PACK)
+            if scalar_m > 0:
+                nc.scalar.copy(dst[:, :scalar_m], src[:, :scalar_m])
+            if scalar_m < P:
+                nc.vector.tensor_copy(dst[:, scalar_m:], src[:, scalar_m:])
+            w1c[a, b] = keep.tile([P, KP], U32, name="w1c%d%d" % (a, b), align_bytes=64)
+            w1s[a, b] = keep.tile([P, KP], U8, name="w1s%d%d" % (a, b), align_bytes=64)
+            nc.vector.quantize_mx(out=w1c[a, b][:].bitcast(E4M3), scales=w1s[a, b][:], in_=g[:])
+
+        quant_w1(0, 0, P)
+        quant_w1(1, 0, P // 2)
+        for h in range(2):
+            nc.vector.tensor_copy(
+                vw[1][:, HALF * h : HALF * (h + 1)], tabw[1][:].indirect(pick[:, LCOL * h : LCOL * (h + 1)])
+            )
+
+        res = {}
+        gated = {}
+        zc = {}
+        zs = {}
+
+        def unit(b, t, h):
+            cols = slice(HALF * h, HALF * (h + 1))
+            if t == 0:
+                res[b, h] = ring.tile([P, PACK, HALF], F32, name="res", tag="res", bufs=3)
+                gated[b, h] = ring.tile([P, PACK, HALF], F32, name="gated", tag="gated", bufs=2)
+            acc = psum.tile([P, HALF], F32, name="acc", tag="acc")
+            for a in range(2):
+                nc.tensor.matmul_mx(
+                    out=acc[:],
+                    lhsT=w1c[a, b][:, P * t : P * (t + 1)].bitcast(E4M3),
+                    lhsT_scale=w1s[a, b][:, P * t : P * (t + 1)],
+                    rhs=vw[a][:, cols].bitcast(E5M2),
+                    rhs_scale=vsc[a][:, cols],
+                    start=(a == 0),
+                    stop=(a == 1),
+                )
+            bias = ntgt[:, PACK * b + t : PACK * b + t + 1]
+            trust = ring.tile([P, HALF], F32, name="trust", tag="trust", bufs=6)
+            nc.scalar.activation(trust[:], acc[:], ACT.Square, bias=bias)
+            nc.scalar.activation(res[b, h][:, t, :], acc[:], ACT.Identity, bias=bias)
+            nc.scalar.activation(trust[:], trust[:], ACT.Exp, scale=-1.0)
+            nc.vector.tensor_tensor(
+                gated[b, h][:, t, :], margins[b, t][:].indirect(pick[:, LCOL * h : LCOL * (h + 1)]), trust[:], ALU.mult
+            )
+
+        def make_z(b, h):
+            z = grouped("zbf")
+            nc.vector.scalar_tensor_tensor(
+                z[:].rearrange("p (c t) -> p c t", t=PACK),
+                gated[b, h][:].rearrange("p t c -> p c t"),
+                0.0,
+                res[b, h][:].rearrange("p t c -> p c t"),
+                ALU.max,
+                ALU.mult,
+            )
+            return z
+
+        def quant_z(b, h, z):
+            zc[b, h] = keep.tile([P, HALF], U32, name="zc%d%d" % (b, h), align_bytes=64)
+            zs[b, h] = keep.tile([P, HALF], U8, name="zs%d%d" % (b, h), align_bytes=64)
+            nc.vector.quantize_mx(out=zc[b, h][:].bitcast(E4M3), scales=zs[b, h][:], in_=z[:])
+
+        load_w1(0, 1)
+        load_w1(1, 1)
+        for t in range(PACK):
+            for h in range(2):
+                unit(0, t, h)
+        for t in range(2):
+            pages[2 + t] = ring.tile([P, T2], F32, name="page", tag="then_page%d" % t, bufs=1)
+            for c in range(T2 // CHUNK):
+                nc.gpsimd.memset(pages[2 + t][:, CHUNK * c : CHUNK * (c + 1)], 0.0)
+        quant_w1(0, 1, 0)
+        quant_w1(1, 1, 0)
+        for t in range(PACK):
+            load_margins(1, t)
+        w2raw = stream([P, 2, N], I32, "w2raw")
+        nc.sync.dma_start(w2raw[:], w2_words.rearrange("a p c i -> p a (c i)").bitcast(I32))
+        for q in range(4):
+            nc.sync.dma_start(
+                w2sc_raw[32 * q : 32 * q + 8, :].bitcast(I32), w2_scales[:, 4 * q : 4 * q + 4, :].bitcast(I32)
+            )
+        nc.sync.dma_start(place[:], offs2)
+        wgo_v = wgo.rearrange("(r t) s -> r t s", t=PACK)
+        for q in range(4):
+            nc.sync.dma_start(gain[32 * q : 32 * (q + 1)], wgo_v)
+
+        z00 = make_z(0, 0)
+        z01 = make_z(0, 1)
+        quant_z(0, 0, z00)
+        quant_z(0, 1, z01)
+        for t in range(PACK):
+            unit(1, t, 0)
+        nc.vector.tensor_copy(
+            w2w[:].rearrange("p a (t m) -> p a m t", t=PACK), w2raw[:].rearrange("p a (m t) -> p a m t", t=PACK)
+        )
+        nc.vector.tensor_copy(
+            w2sc[:].rearrange("p (t m) -> p m t", t=PACK), w2sc_raw[:].rearrange("p (m t) -> p m t", t=PACK)
+        )
+        z10 = make_z(1, 0)
+        unit(1, 0, 1)
+        quant_z(1, 0, z10)
+        for t in range(1, PACK):
+            unit(1, t, 1)
+
+        steps = [stream([P, S], F32, "step") for t in range(PACK)]
+
+        def second(t, h):
+            acc2 = psum.tile([P, HALF], F32, name="acc2", tag="acc2")
+            for b in range(2):
+                nc.tensor.matmul_mx(
+                    out=acc2[:],
+                    lhsT=w2w[:, b, P * t : P * (t + 1)].bitcast(E4M3),
+                    lhsT_scale=w2sc[4 * b :, P * t : P * (t + 1)],
+                    rhs=zc[b, h][:].bitcast(E4M3),
+                    rhs_scale=zs[b, h][:],
+                    start=(b == 0),
+                    stop=(b == 1),
+                )
+            nc.scalar.copy(steps[t][:, HALF * h : HALF * (h + 1)], acc2[:])
+
+        def scatter(t, lo, hi):
+            nc.vector.tensor_tensor(
+                pages[t][:].indirect(place[:, lo // 16 : hi // 16]), steps[t][:, lo:hi], gain[:, t, lo:hi], ALU.mult
+            )
+
+        for t in range(PACK):
+            second(t, 0)
+        z11 = make_z(1, 1)
+        quant_z(1, 1, z11)
+        scatter(0, 0, HALF)
+        for t in range(PACK):
+            second(t, 1)
+        scatter(0, HALF, S)
+
+        out_v = out_0.rearrange("(p t) m -> p t m", t=PACK)
+        n_chunks = T2 // CHUNK
+        ybf = [grouped("ybf") for c in range(n_chunks)]
+
+        def ycol(c):
+            return ybf[c][:].rearrange("p (c t) -> p c t", t=PACK)
+
+        for t in range(PACK):
+            if t > 0:
+                scatter(t, 0, S)
+            nc.sync.dma_start(out_v[:, t, :], pages[t][:])
+            for c in range(n_chunks):
+                src = pages[t][:, CHUNK * c : CHUNK * (c + 1)]
+                if t < 2:
+                    nc.scalar.copy(ycol(c)[:, :, t], src)
+                elif t == 2:
+                    nc.scalar.copy(ycol(c)[:, :, 2:4], src.unsqueeze(2).to_broadcast([P, CHUNK, 2]))
+                elif c < n_chunks // 2:
+                    nc.vector.tensor_copy(ycol(c)[:, :, t], src)
+                else:
+                    nc.scalar.copy(ycol(c)[:, :, t], src)
+
+        words_v = out_1[0].rearrange("p m t -> p (m t)").bitcast(I32)
+        for c in range(n_chunks):
+            cols = slice(CHUNK * c, CHUNK * (c + 1))
+            nc.vector.quantize_mx(out=ycodes[:, cols].bitcast(E4M3), scales=yscales[:, cols], in_=ybf[c][:])
+            nc.sync.dma_start(words_v[:, cols], ycodes[:, cols].bitcast(I32))
+        for q in range(4):
+            queue = nc.sync if q % 2 == 0 else nc.scalar
+            queue.dma_start(out_2[0, 4 * q : 4 * q + 4, :].bitcast(I32), yscales[32 * q : 32 * q + 4, :].bitcast(I32))

@@ -31,42 +31,46 @@ def tile_list_coil_trust_weighting_kernel(
     with ExitStack() as ctx:
         keep = ctx.enter_context(tc.tile_pool(name="keep", bufs=1))
         ring = ctx.enter_context(tc.tile_pool(name="ring", bufs=1))
+        shared = ctx.enter_context(tc.tile_pool(name="shared", bufs=1))
         psum = ctx.enter_context(tc.psum_pool(name="psum", bufs=4))
 
         def stream(shape, dtype, name):
-            return ring.tile(shape, dtype, name=name, tag="stream", bufs=8, align_bytes=64)
+            return ring.tile(shape, dtype, name=name, tag="stream", bufs=7, align_bytes=64)
 
         def grouped(name):
-            return ring.tile([P, PACK * HALF], BF16, name=name, tag="grouped", bufs=4, align_bytes=64)
+            return ring.tile([P, PACK * HALF], BF16, name=name, tag="grouped", bufs=3, align_bytes=64)
+
+        def gated_slot(shape, name, n):
+            return ring.tile(shape, F32, name=name, tag="gated%d" % (n % 2), bufs=1)
+
+        def half_list(offsets, h):
+            return offsets[:, LCOL * h : LCOL * (h + 1)]
 
         pick = keep.tile([P, S // 16], U16, name="pick")
         place = keep.tile([P, S // 16], U16, name="place")
         tsc = keep.tile([P, 2, T], U8, name="tsc", align_bytes=64)
-        vsc = [keep.tile([P, S], U8, name="vsc%d" % a, align_bytes=64) for a in range(2)]
-        vw = [keep.tile([P, S], U32, name="vw%d" % a, align_bytes=64) for a in range(2)]
         w2sc_raw = keep.tile([P, N], U8, name="w2sc_raw", align_bytes=64)
         w2sc = keep.tile([P, N], U8, name="w2sc", align_bytes=64)
         w2w = keep.tile([P, 2, N], I32, name="w2w", align_bytes=64)
         tgt = keep.tile([P, 2, PACK], F32, name="tgt")
         ntgt = keep.tile([P, 2 * PACK], F32, name="ntgt")
         gain = keep.tile([P, PACK, S], F32, name="gain")
-        pages = {t: keep.tile([P, T2], F32, name="page%d" % t) for t in range(2)}
+        pages = [keep.tile([P, T2], F32, name="page%d" % t) for t in range(PACK)]
         ycodes = keep.tile([P, T2], U32, name="ycodes", align_bytes=64)
         yscales = keep.tile([P, T2], U8, name="yscales", align_bytes=64)
 
         nc.vector.memset(tsc[:].rearrange("p a t -> p (a t)").bitcast(I32), 0)
         nc.vector.memset(w2sc_raw[:].bitcast(I32), 0)
-        for t in range(2):
-            nc.vector.memset(pages[t][:], 0.0)
+        for t in range(PACK):
+            nc.vector.memset(pages[t][:].bitcast(I32), 0)
 
-        nc.sync.dma_start(pick[:], offs)
         tabw = {}
         w1raw = {}
         margins = {}
 
-        def load_tab(a):
-            tabw[a] = stream([P, T], U32, "tabw")
-            nc.sync.dma_start(tabw[a][:].bitcast(I32), tab_words[a].rearrange("p t i -> p (t i)").bitcast(I32))
+        def load_tab(a, tile):
+            tabw[a] = tile
+            nc.sync.dma_start(tile[:].bitcast(I32), tab_words[a].rearrange("p t i -> p (t i)").bitcast(I32))
 
         def load_w1(a, b):
             w1raw[a, b] = stream([P, PACK, KP], F32, "w1raw")
@@ -76,13 +80,14 @@ def tile_list_coil_trust_weighting_kernel(
         sT_v = sT.rearrange("(b p t) c -> b t p c", b=2, t=PACK)
 
         def load_margins(b, t):
-            if b == 0 and t < 2:
-                margins[b, t] = ring.tile([P, T], F32, name="margins", tag="then_page%d" % t, bufs=1)
+            if (b, t) == (1, 2):
+                margins[b, t] = ring.tile([P, T], F32, name="margins", tag="then_step0", bufs=1)
             else:
                 margins[b, t] = stream([P, T], F32, "margins")
             nc.sync.dma_start(margins[b, t][:], sT_v[b, t])
 
-        load_tab(0)
+        nc.sync.dma_start(pick[:], offs)
+        load_tab(0, stream([P, T], U32, "tabw0"))
         for q in range(4):
             nc.sync.dma_start(
                 tsc[32 * q : 32 * q + 4].bitcast(I32),
@@ -90,97 +95,111 @@ def tile_list_coil_trust_weighting_kernel(
             )
         load_w1(0, 0)
         load_w1(1, 0)
-        load_tab(1)
+        load_tab(1, shared.tile([P, T], U32, name="tabw1", align_bytes=64, offset=0))
         nc.sync.dma_start(tgt[:], target.rearrange("(b p t) -> p b t", b=2, t=PACK))
         for t in range(PACK):
             load_margins(0, t)
 
         nc.scalar.mul(ntgt[:], tgt[:].rearrange("p b t -> p (b t)"), -1.0)
 
-        nc.vector.tensor_copy(vw[0][:], tabw[0][:].indirect(pick[:]))
-        for a in range(2):
-            nc.vector.tensor_copy(vsc[a][:], tsc[:, a, :].indirect(pick[:]))
+        vw = {}
+        vsc = {}
+
+        def gather_words(a, h, tile):
+            vw[a, h] = tile
+            nc.vector.tensor_copy(tile[:], tabw[a][:].indirect(half_list(pick, h)))
+
+        def gather_scales(a, h, tile):
+            vsc[a, h] = tile
+            nc.vector.tensor_copy(tile[:], tsc[:, a, :].indirect(half_list(pick, h)))
 
         w1c = {}
         w1s = {}
 
         def quant_w1(a, b, scalar_m):
             g = grouped("w1bf")
-            dst = g[:].rearrange("p (t m j) -> p m j t", t=PACK, j=PACK)
-            src = w1raw[a, b][:].rearrange("p j (m t) -> p m j t", t=PACK)
+            dst = g[:].rearrange("p (u e m j) -> p u m j e", u=2, e=2, j=PACK)
+            src = w1raw[a, b][:].rearrange("p j (m u e) -> p u m j e", u=2, e=2)
             if scalar_m > 0:
-                nc.scalar.copy(dst[:, :scalar_m], src[:, :scalar_m])
+                nc.scalar.copy(dst[:, :, :scalar_m], src[:, :, :scalar_m])
             if scalar_m < P:
-                nc.vector.tensor_copy(dst[:, scalar_m:], src[:, scalar_m:])
+                nc.vector.tensor_copy(dst[:, :, scalar_m:], src[:, :, scalar_m:])
             w1c[a, b] = keep.tile([P, KP], U32, name="w1c%d%d" % (a, b), align_bytes=64)
             w1s[a, b] = keep.tile([P, KP], U8, name="w1s%d%d" % (a, b), align_bytes=64)
             nc.vector.quantize_mx(out=w1c[a, b][:].bitcast(E4M3), scales=w1s[a, b][:], in_=g[:])
 
+        gather_words(0, 0, keep.tile([P, HALF], U32, name="vw00", align_bytes=64))
+        for a in range(2):
+            gather_scales(a, 0, keep.tile([P, HALF], U8, name="vsc%d0" % a, align_bytes=64))
         quant_w1(0, 0, P)
-        quant_w1(1, 0, P // 2)
+        quant_w1(1, 0, P // 4)
         for h in range(2):
-            nc.vector.tensor_copy(
-                vw[1][:, HALF * h : HALF * (h + 1)], tabw[1][:].indirect(pick[:, LCOL * h : LCOL * (h + 1)])
+            gather_words(1, h, keep.tile([P, HALF], U32, name="vw1%d" % h, align_bytes=64))
+        gather_words(0, 1, shared.tile([P, HALF], U32, name="vw01", align_bytes=64, offset=0))
+        for a in range(2):
+            gather_scales(
+                a, 1, shared.tile([P, HALF], U8, name="vsc%d1" % a, align_bytes=64, offset=4 * HALF + a * HALF)
             )
 
+        groups = [(0, 0), (0, 1), (1, 0), (1, 1)]
         res = {}
         gated = {}
+        zpairs = {}
+        zbf = {}
         zc = {}
         zs = {}
 
-        def unit(b, t, h):
-            cols = slice(HALF * h, HALF * (h + 1))
+        def unit(n, t):
+            b, h = groups[n]
             if t == 0:
-                res[b, h] = ring.tile([P, PACK, HALF], F32, name="res", tag="res", bufs=3)
-                gated[b, h] = ring.tile([P, PACK, HALF], F32, name="gated", tag="gated", bufs=2)
+                res[n] = ring.tile([P, PACK, HALF], F32, name="res", tag="res", bufs=3)
+                gated[n] = gated_slot([P, PACK, HALF], "gated", n)
             acc = psum.tile([P, HALF], F32, name="acc", tag="acc")
             for a in range(2):
                 nc.tensor.matmul_mx(
                     out=acc[:],
                     lhsT=w1c[a, b][:, P * t : P * (t + 1)].bitcast(E4M3),
                     lhsT_scale=w1s[a, b][:, P * t : P * (t + 1)],
-                    rhs=vw[a][:, cols].bitcast(E5M2),
-                    rhs_scale=vsc[a][:, cols],
+                    rhs=vw[a, h][:].bitcast(E5M2),
+                    rhs_scale=vsc[a, h][:],
                     start=(a == 0),
                     stop=(a == 1),
                 )
             bias = ntgt[:, PACK * b + t : PACK * b + t + 1]
-            trust = ring.tile([P, HALF], F32, name="trust", tag="trust", bufs=6)
+            trust = ring.tile([P, HALF], F32, name="trust", tag="trust", bufs=4)
             nc.scalar.activation(trust[:], acc[:], ACT.Square, bias=bias)
-            nc.scalar.activation(res[b, h][:, t, :], acc[:], ACT.Identity, bias=bias)
+            nc.scalar.activation(res[n][:, t, :], acc[:], ACT.Identity, bias=bias)
             nc.scalar.activation(trust[:], trust[:], ACT.Exp, scale=-1.0)
-            nc.vector.tensor_tensor(
-                gated[b, h][:, t, :], margins[b, t][:].indirect(pick[:, LCOL * h : LCOL * (h + 1)]), trust[:], ALU.mult
-            )
+            nc.vector.tensor_tensor(gated[n][:, t, :], margins[b, t][:].indirect(half_list(pick, h)), trust[:], ALU.mult)
 
-        def make_z(b, h):
-            z = grouped("zbf")
+        def weave(copy, pair_tile, name):
+            tile = grouped(name)
+            copy(
+                tile[:].bitcast(F32).rearrange("p (c u) -> p c u", u=2),
+                pair_tile[:].rearrange("p u c e -> p u (c e)").bitcast(F32).rearrange("p u c -> p c u"),
+            )
+            return tile
+
+        def z_pair(n, u):
+            if u == 0:
+                zpairs[n] = ring.tile([P, 2, HALF, 2], BF16, name="zpairs", tag="zpairs", bufs=2)
             nc.vector.scalar_tensor_tensor(
-                z[:].rearrange("p (c t) -> p c t", t=PACK),
-                gated[b, h][:].rearrange("p t c -> p c t"),
+                zpairs[n][:, u],
+                gated[n][:, 2 * u : 2 * u + 2, :].rearrange("p e c -> p c e"),
                 0.0,
-                res[b, h][:].rearrange("p t c -> p c t"),
+                res[n][:, 2 * u : 2 * u + 2, :].rearrange("p e c -> p c e"),
                 ALU.max,
                 ALU.mult,
             )
-            return z
 
-        def quant_z(b, h, z):
-            zc[b, h] = keep.tile([P, HALF], U32, name="zc%d%d" % (b, h), align_bytes=64)
-            zs[b, h] = keep.tile([P, HALF], U8, name="zs%d%d" % (b, h), align_bytes=64)
-            nc.vector.quantize_mx(out=zc[b, h][:].bitcast(E4M3), scales=zs[b, h][:], in_=z[:])
+        def make_z(n):
+            zbf[n] = weave(nc.scalar.copy if n < 3 else nc.vector.tensor_copy, zpairs[n], "zbf")
+            zc[groups[n]] = keep.tile([P, HALF], U32, name="zc%d" % n, align_bytes=64)
+            zs[groups[n]] = keep.tile([P, HALF], U8, name="zs%d" % n, align_bytes=64)
+            nc.vector.quantize_mx(out=zc[groups[n]][:].bitcast(E4M3), scales=zs[groups[n]][:], in_=zbf[n][:])
 
         load_w1(0, 1)
         load_w1(1, 1)
-        for t in range(PACK):
-            for h in range(2):
-                unit(0, t, h)
-        for t in range(2):
-            pages[2 + t] = ring.tile([P, T2], F32, name="page", tag="then_page%d" % t, bufs=1)
-            for c in range(T2 // CHUNK):
-                nc.gpsimd.memset(pages[2 + t][:, CHUNK * c : CHUNK * (c + 1)], 0.0)
-        quant_w1(0, 1, 0)
-        quant_w1(1, 1, 0)
         for t in range(PACK):
             load_margins(1, t)
         w2raw = stream([P, 2, N], I32, "w2raw")
@@ -194,25 +213,29 @@ def tile_list_coil_trust_weighting_kernel(
         for q in range(4):
             nc.sync.dma_start(gain[32 * q : 32 * (q + 1)], wgo_v)
 
-        z00 = make_z(0, 0)
-        z01 = make_z(0, 1)
-        quant_z(0, 0, z00)
-        quant_z(0, 1, z01)
-        for t in range(PACK):
-            unit(1, t, 0)
-        nc.vector.tensor_copy(
-            w2w[:].rearrange("p a (t m) -> p a m t", t=PACK), w2raw[:].rearrange("p a (m t) -> p a m t", t=PACK)
-        )
-        nc.vector.tensor_copy(
-            w2sc[:].rearrange("p (t m) -> p m t", t=PACK), w2sc_raw[:].rearrange("p (m t) -> p m t", t=PACK)
-        )
-        z10 = make_z(1, 0)
-        unit(1, 0, 1)
-        quant_z(1, 0, z10)
-        for t in range(1, PACK):
-            unit(1, t, 1)
+        for n in range(len(groups)):
+            if n == 1:
+                quant_w1(0, 1, P)
+                quant_w1(1, 1, 0)
+            for t in range(PACK):
+                unit(n, t)
+                if t % 2 == 1:
+                    z_pair(n, t // 2)
+                if n > 0 and t == 2:
+                    make_z(n - 1)
+            if n == 2:
+                nc.vector.tensor_copy(
+                    w2w[:].rearrange("p a (t m) -> p a m t", t=PACK),
+                    w2raw[:].rearrange("p a (m t) -> p a m t", t=PACK),
+                )
+                nc.vector.tensor_copy(
+                    w2sc[:].rearrange("p (t m) -> p m t", t=PACK), w2sc_raw[:].rearrange("p (m t) -> p m t", t=PACK)
+                )
 
-        steps = [stream([P, S], F32, "step") for t in range(PACK)]
+        steps = {}
+        step0 = ring.tile([P, S], F32, name="step0", tag="then_step0", bufs=1)
+        steps[0] = step0[:]
+        steps[3] = stream([P, S], F32, "step3")[:]
 
         def second(t, h):
             acc2 = psum.tile([P, HALF], F32, name="acc2", tag="acc2")
@@ -233,39 +256,39 @@ def tile_list_coil_trust_weighting_kernel(
                 pages[t][:].indirect(place[:, lo // 16 : hi // 16]), steps[t][:, lo:hi], gain[:, t, lo:hi], ALU.mult
             )
 
-        for t in range(PACK):
-            second(t, 0)
-        z11 = make_z(1, 1)
-        quant_z(1, 1, z11)
+        make_z(3)
+        second(0, 0)
         scatter(0, 0, HALF)
-        for t in range(PACK):
+        step21 = gated_slot([P, 2, S], "step21", 3)
+        steps[2] = step21[:, 0, :]
+        steps[1] = step21[:, 1, :]
+        for t in (2, 1):
+            second(t, 0)
+            scatter(t, 0, HALF)
+        second(3, 0)
+        for t in (0, 2, 1, 3):
             second(t, 1)
-        scatter(0, HALF, S)
 
         out_v = out_0.rearrange("(p t) m -> p t m", t=PACK)
         n_chunks = T2 // CHUNK
-        ybf = [grouped("ybf") for c in range(n_chunks)]
-
-        def ycol(c):
-            return ybf[c][:].rearrange("p (c t) -> p c t", t=PACK)
-
-        for t in range(PACK):
-            if t > 0:
-                scatter(t, 0, S)
+        pairs = [stream([P, 2, CHUNK, 2], BF16, "pairs") for c in range(n_chunks)]
+        for t in (0, 2, 1, 3):
+            scatter(t, HALF if t < 3 else 0, S)
             nc.sync.dma_start(out_v[:, t, :], pages[t][:])
             for c in range(n_chunks):
                 src = pages[t][:, CHUNK * c : CHUNK * (c + 1)]
-                if t < 2:
-                    nc.scalar.copy(ycol(c)[:, :, t], src)
-                elif t == 2:
-                    nc.scalar.copy(ycol(c)[:, :, 2:4], src.unsqueeze(2).to_broadcast([P, CHUNK, 2]))
-                elif c < n_chunks // 2:
-                    nc.vector.tensor_copy(ycol(c)[:, :, t], src)
-                else:
-                    nc.scalar.copy(ycol(c)[:, :, t], src)
+                on_vector = c < n_chunks // 2
+                if t == 2 and on_vector:
+                    nc.scalar.copy(pairs[c][:, 1], src.unsqueeze(2).to_broadcast([P, CHUNK, 2]))
+                elif t < 3:
+                    nc.scalar.copy(pairs[c][:, t // 2, :, t % 2], src)
 
         words_v = out_1[0].rearrange("p m t -> p (m t)").bitcast(I32)
-        for c in range(n_chunks):
+        ybf = {}
+        for c in (0, 2, 1, 3):
+            copy = nc.vector.tensor_copy if c < n_chunks // 2 else nc.scalar.copy
+            copy(pairs[c][:, 1, :, 1], pages[3][:, CHUNK * c : CHUNK * (c + 1)])
+            ybf[c] = weave(copy, pairs[c], "ybf")
             cols = slice(CHUNK * c, CHUNK * (c + 1))
             nc.vector.quantize_mx(out=ycodes[:, cols].bitcast(E4M3), scales=yscales[:, cols], in_=ybf[c][:])
             nc.sync.dma_start(words_v[:, cols], ycodes[:, cols].bitcast(I32))

@@ -22,6 +22,8 @@ KP = P * PACK
 HALF = 512
 LCOL = HALF // 16
 CHUNK = 512
+SLOT = 8192
+QUARTER = SLOT // 4
 
 
 def tile_list_coil_trust_weighting_kernel(
@@ -31,74 +33,81 @@ def tile_list_coil_trust_weighting_kernel(
     with ExitStack() as ctx:
         keep = ctx.enter_context(tc.tile_pool(name="keep", bufs=1))
         ring = ctx.enter_context(tc.tile_pool(name="ring", bufs=1))
-        shared = ctx.enter_context(tc.tile_pool(name="shared", bufs=1))
-        psum = ctx.enter_context(tc.psum_pool(name="psum", bufs=4))
+        slots = ctx.enter_context(tc.tile_pool(name="slots", bufs=1))
+        psum = ctx.enter_context(tc.psum_pool(name="psum", bufs=1))
 
-        def stream(shape, dtype, name):
-            return ring.tile(shape, dtype, name=name, tag="stream", bufs=7, align_bytes=64)
+        def in_slot(shape, dtype, name, slot, quarter=0):
+            return slots.tile(shape, dtype, name=name, align_bytes=64, offset=SLOT * slot + QUARTER * quarter)
 
         def grouped(name):
             return ring.tile([P, PACK * HALF], BF16, name=name, tag="grouped", bufs=3, align_bytes=64)
-
-        def gated_slot(shape, name, n):
-            return ring.tile(shape, F32, name=name, tag="gated%d" % (n % 2), bufs=1)
 
         def half_list(offsets, h):
             return offsets[:, LCOL * h : LCOL * (h + 1)]
 
         pick = keep.tile([P, S // 16], U16, name="pick")
         place = keep.tile([P, S // 16], U16, name="place")
-        tsc = keep.tile([P, 2, T], U8, name="tsc", align_bytes=64)
+        tsc = [keep.tile([P, T], U8, name="tsc%d" % a, align_bytes=64) for a in range(2)]
         w2sc_raw = keep.tile([P, N], U8, name="w2sc_raw", align_bytes=64)
         w2sc = keep.tile([P, N], U8, name="w2sc", align_bytes=64)
+        w2raw = keep.tile([P, 2, N], I32, name="w2raw", align_bytes=64)
         w2w = keep.tile([P, 2, N], I32, name="w2w", align_bytes=64)
         tgt = keep.tile([P, 2, PACK], F32, name="tgt")
         ntgt = keep.tile([P, 2 * PACK], F32, name="ntgt")
-        gain = keep.tile([P, PACK, S], F32, name="gain")
-        pages = [keep.tile([P, T2], F32, name="page%d" % t) for t in range(PACK)]
         ycodes = keep.tile([P, T2], U32, name="ycodes", align_bytes=64)
         yscales = keep.tile([P, T2], U8, name="yscales", align_bytes=64)
 
-        nc.vector.memset(tsc[:].rearrange("p a t -> p (a t)").bitcast(I32), 0)
+        for a in range(2):
+            nc.gpsimd.memset(tsc[a][:].bitcast(I32), 0)
         nc.vector.memset(w2sc_raw[:].bitcast(I32), 0)
-        for t in range(PACK):
-            nc.vector.memset(pages[t][:].bitcast(I32), 0)
 
         tabw = {}
         w1raw = {}
         margins = {}
 
-        def load_tab(a, tile):
-            tabw[a] = tile
-            nc.sync.dma_start(tile[:].bitcast(I32), tab_words[a].rearrange("p t i -> p (t i)").bitcast(I32))
+        def load_tab(a):
+            tabw[a] = in_slot([P, T], U32, "tabw%d" % a, a)
+            nc.sync.dma_start(tabw[a][:].bitcast(I32), tab_words[a].rearrange("p t i -> p (t i)").bitcast(I32))
+
+        def load_scales(a):
+            for q in range(4):
+                nc.sync.dma_start(
+                    tsc[a][32 * q : 32 * q + 4, :].bitcast(I32), tab_scales[a, 4 * q : 4 * q + 4, :].bitcast(I32)
+                )
 
         def load_w1(a, b):
-            w1raw[a, b] = stream([P, PACK, KP], F32, "w1raw")
+            w1raw[a, b] = in_slot([P, PACK, KP], F32, "w1raw%d%d" % (a, b), 2 + 2 * b + a)
             rows = w1[KP * a : KP * (a + 1), KP * b : KP * (b + 1)]
             nc.sync.dma_start(w1raw[a, b][:], rows.rearrange("(p j) c -> p j c", j=PACK))
 
         sT_v = sT.rearrange("(b p t) c -> b t p c", b=2, t=PACK)
 
         def load_margins(b, t):
-            if (b, t) == (1, 2):
-                margins[b, t] = ring.tile([P, T], F32, name="margins", tag="then_step0", bufs=1)
-            else:
-                margins[b, t] = stream([P, T], F32, "margins")
+            margins[b, t] = in_slot([P, T], F32, "margins%d%d" % (b, t), 6 + PACK * b + t)
             nc.sync.dma_start(margins[b, t][:], sT_v[b, t])
 
         nc.sync.dma_start(pick[:], offs)
-        load_tab(0, stream([P, T], U32, "tabw0"))
+        nc.sync.dma_start(tgt[:], target.rearrange("(b p t) -> p b t", b=2, t=PACK))
+        load_scales(0)
+        load_w1(0, 0)
+        load_scales(1)
+        load_w1(1, 0)
+        load_tab(0)
+        load_tab(1)
+        load_margins(0, 0)
+        load_margins(0, 1)
+        load_w1(0, 1)
+        load_w1(1, 1)
+        load_margins(0, 2)
+        load_margins(0, 3)
+        load_margins(1, 0)
+        load_margins(1, 1)
+        nc.sync.dma_start(w2raw[:], w2_words.rearrange("a p c i -> p a (c i)").bitcast(I32))
         for q in range(4):
             nc.sync.dma_start(
-                tsc[32 * q : 32 * q + 4].bitcast(I32),
-                tab_scales[:, 4 * q : 4 * q + 4, :].rearrange("a r t -> r a t").bitcast(I32),
+                w2sc_raw[32 * q : 32 * q + 8, :].bitcast(I32), w2_scales[:, 4 * q : 4 * q + 4, :].bitcast(I32)
             )
-        load_w1(0, 0)
-        load_w1(1, 0)
-        load_tab(1, shared.tile([P, T], U32, name="tabw1", align_bytes=64, offset=0))
-        nc.sync.dma_start(tgt[:], target.rearrange("(b p t) -> p b t", b=2, t=PACK))
-        for t in range(PACK):
-            load_margins(0, t)
+        nc.sync.dma_start(place[:], offs2)
 
         nc.scalar.mul(ntgt[:], tgt[:].rearrange("p b t -> p (b t)"), -1.0)
 
@@ -109,52 +118,58 @@ def tile_list_coil_trust_weighting_kernel(
             vw[a, h] = tile
             nc.vector.tensor_copy(tile[:], tabw[a][:].indirect(half_list(pick, h)))
 
-        def gather_scales(a, h, tile):
-            vsc[a, h] = tile
-            nc.vector.tensor_copy(tile[:], tsc[:, a, :].indirect(half_list(pick, h)))
+        def gather_scales(a, h):
+            vsc[a, h] = keep.tile([P, HALF], U8, name="vsc%d%d" % (a, h), align_bytes=64)
+            nc.vector.tensor_copy(vsc[a, h][:], tsc[a][:].indirect(half_list(pick, h)))
 
         w1c = {}
         w1s = {}
 
-        def quant_w1(a, b, scalar_m):
+        def quant_w1(a, b, copy):
             g = grouped("w1bf")
-            dst = g[:].rearrange("p (u e m j) -> p u m j e", u=2, e=2, j=PACK)
-            src = w1raw[a, b][:].rearrange("p j (m u e) -> p u m j e", u=2, e=2)
-            if scalar_m > 0:
-                nc.scalar.copy(dst[:, :, :scalar_m], src[:, :, :scalar_m])
-            if scalar_m < P:
-                nc.vector.tensor_copy(dst[:, :, scalar_m:], src[:, :, scalar_m:])
+            copy(
+                g[:].rearrange("p (u e m j) -> p u m j e", u=2, e=2, j=PACK),
+                w1raw[a, b][:].rearrange("p j (m u e) -> p u m j e", u=2, e=2),
+            )
             w1c[a, b] = keep.tile([P, KP], U32, name="w1c%d%d" % (a, b), align_bytes=64)
             w1s[a, b] = keep.tile([P, KP], U8, name="w1s%d%d" % (a, b), align_bytes=64)
             nc.vector.quantize_mx(out=w1c[a, b][:].bitcast(E4M3), scales=w1s[a, b][:], in_=g[:])
 
-        gather_words(0, 0, keep.tile([P, HALF], U32, name="vw00", align_bytes=64))
+        pages = {}
+
+        def clear_page(t, slot):
+            pages[t] = in_slot([P, T2], F32, "page%d" % t, slot)
+            for c in range(T2 // CHUNK):
+                nc.gpsimd.memset(pages[t][:, CHUNK * c : CHUNK * (c + 1)], 0.0)
+
         for a in range(2):
-            gather_scales(a, 0, keep.tile([P, HALF], U8, name="vsc%d0" % a, align_bytes=64))
-        quant_w1(0, 0, P)
-        quant_w1(1, 0, P // 4)
+            for h in range(2):
+                gather_scales(a, h)
+        quant_w1(0, 0, nc.scalar.copy)
+        gather_words(0, 0, keep.tile([P, HALF], U32, name="vw00", align_bytes=64))
+        quant_w1(1, 0, nc.scalar.copy)
         for h in range(2):
             gather_words(1, h, keep.tile([P, HALF], U32, name="vw1%d" % h, align_bytes=64))
-        gather_words(0, 1, shared.tile([P, HALF], U32, name="vw01", align_bytes=64, offset=0))
-        for a in range(2):
-            gather_scales(
-                a, 1, shared.tile([P, HALF], U8, name="vsc%d1" % a, align_bytes=64, offset=4 * HALF + a * HALF)
-            )
+        gather_words(0, 1, in_slot([P, HALF], U32, "vw01", 1))
+        clear_page(2, 2)
+        clear_page(3, 3)
+        clear_page(0, 0)
 
-        groups = [(0, 0), (0, 1), (1, 0), (1, 1)]
+        order = [(0, 0, 0), (0, 0, 1), (0, 1, 0), (0, 1, 1), (1, 0, 0), (1, 1, 0), (1, 0, 1), (1, 1, 1)]
+        zslot = {(0, 0): 0, (0, 1): 2, (1, 0): 4, (1, 1): 0}
         res = {}
-        gated = {}
+        trust = {}
         zpairs = {}
-        zbf = {}
         zc = {}
         zs = {}
 
-        def unit(n, t):
-            b, h = groups[n]
-            if t == 0:
-                res[n] = ring.tile([P, PACK, HALF], F32, name="res", tag="res", bufs=3)
-                gated[n] = gated_slot([P, PACK, HALF], "gated", n)
-            acc = psum.tile([P, HALF], F32, name="acc", tag="acc")
+        def residual(i, e):
+            b, u, h = order[i]
+            t = 2 * u + e
+            if e == 0:
+                res[i] = ring.tile([P, 2, HALF], F32, name="res", tag="res", bufs=4)
+                trust[i] = ring.tile([P, 2, HALF], F32, name="trust", tag="trust", bufs=3)
+            acc = psum.tile([P, HALF], F32, name="acc", tag="acc", bufs=6)
             for a in range(2):
                 nc.tensor.matmul_mx(
                     out=acc[:],
@@ -166,11 +181,33 @@ def tile_list_coil_trust_weighting_kernel(
                     stop=(a == 1),
                 )
             bias = ntgt[:, PACK * b + t : PACK * b + t + 1]
-            trust = ring.tile([P, HALF], F32, name="trust", tag="trust", bufs=4)
-            nc.scalar.activation(trust[:], acc[:], ACT.Square, bias=bias)
-            nc.scalar.activation(res[n][:, t, :], acc[:], ACT.Identity, bias=bias)
-            nc.scalar.activation(trust[:], trust[:], ACT.Exp, scale=-1.0)
-            nc.vector.tensor_tensor(gated[n][:, t, :], margins[b, t][:].indirect(half_list(pick, h)), trust[:], ALU.mult)
+            if i == 0:
+                nc.scalar.activation(trust[i][:, e, :], acc[:], ACT.Square, bias=bias)
+                nc.scalar.activation(trust[i][:, e, :], trust[i][:, e, :], ACT.Exp, scale=-1.0)
+            nc.scalar.activation(res[i][:, e, :], acc[:], ACT.Identity, bias=bias)
+
+        def square(i):
+            nc.scalar.activation(trust[i][:], res[i][:], ACT.Square)
+
+        def z_pair(i):
+            b, u, h = order[i]
+            if i > 0:
+                nc.scalar.activation(trust[i][:], trust[i][:], ACT.Exp, scale=-1.0)
+            gated = ring.tile([P, 2, HALF], F32, name="gated", tag="gated", bufs=2)
+            for e in range(2):
+                nc.vector.tensor_tensor(
+                    gated[:, e, :], margins[b, 2 * u + e][:].indirect(half_list(pick, h)), trust[i][:, e, :], ALU.mult
+                )
+            if u == 0:
+                zpairs[b, h] = in_slot([P, 2, HALF, 2], BF16, "zpairs%d%d" % (b, h), 14, zslot[b, h])
+            nc.vector.scalar_tensor_tensor(
+                zpairs[b, h][:, u],
+                gated[:].rearrange("p e c -> p c e"),
+                0.0,
+                res[i][:].rearrange("p e c -> p c e"),
+                ALU.max,
+                ALU.mult,
+            )
 
         def weave(copy, pair_tile, name):
             tile = grouped(name)
@@ -180,65 +217,22 @@ def tile_list_coil_trust_weighting_kernel(
             )
             return tile
 
-        def z_pair(n, u):
-            if u == 0:
-                zpairs[n] = ring.tile([P, 2, HALF, 2], BF16, name="zpairs", tag="zpairs", bufs=2)
-            nc.vector.scalar_tensor_tensor(
-                zpairs[n][:, u],
-                gated[n][:, 2 * u : 2 * u + 2, :].rearrange("p e c -> p c e"),
-                0.0,
-                res[n][:, 2 * u : 2 * u + 2, :].rearrange("p e c -> p c e"),
-                ALU.max,
-                ALU.mult,
-            )
+        def make_z(b, h):
+            zbf = weave(nc.scalar.copy, zpairs[b, h], "zbf")
+            zc[b, h] = keep.tile([P, HALF], U32, name="zc%d%d" % (b, h), align_bytes=64)
+            zs[b, h] = keep.tile([P, HALF], U8, name="zs%d%d" % (b, h), align_bytes=64)
+            nc.vector.quantize_mx(out=zc[b, h][:].bitcast(E4M3), scales=zs[b, h][:], in_=zbf[:])
 
-        def make_z(n):
-            zbf[n] = weave(nc.scalar.copy if n < 3 else nc.vector.tensor_copy, zpairs[n], "zbf")
-            zc[groups[n]] = keep.tile([P, HALF], U32, name="zc%d" % n, align_bytes=64)
-            zs[groups[n]] = keep.tile([P, HALF], U8, name="zs%d" % n, align_bytes=64)
-            nc.vector.quantize_mx(out=zc[groups[n]][:].bitcast(E4M3), scales=zs[groups[n]][:], in_=zbf[n][:])
-
-        load_w1(0, 1)
-        load_w1(1, 1)
-        for t in range(PACK):
-            load_margins(1, t)
-        w2raw = stream([P, 2, N], I32, "w2raw")
-        nc.sync.dma_start(w2raw[:], w2_words.rearrange("a p c i -> p a (c i)").bitcast(I32))
-        for q in range(4):
-            nc.sync.dma_start(
-                w2sc_raw[32 * q : 32 * q + 8, :].bitcast(I32), w2_scales[:, 4 * q : 4 * q + 4, :].bitcast(I32)
-            )
-        nc.sync.dma_start(place[:], offs2)
+        gain = {}
         wgo_v = wgo.rearrange("(r t) s -> r t s", t=PACK)
-        for q in range(4):
-            nc.sync.dma_start(gain[32 * q : 32 * (q + 1)], wgo_v)
 
-        for n in range(len(groups)):
-            if n == 1:
-                quant_w1(0, 1, P)
-                quant_w1(1, 1, 0)
-            for t in range(PACK):
-                unit(n, t)
-                if t % 2 == 1:
-                    z_pair(n, t // 2)
-                if n > 0 and t == 2:
-                    make_z(n - 1)
-            if n == 2:
-                nc.vector.tensor_copy(
-                    w2w[:].rearrange("p a (t m) -> p a m t", t=PACK),
-                    w2raw[:].rearrange("p a (m t) -> p a m t", t=PACK),
-                )
-                nc.vector.tensor_copy(
-                    w2sc[:].rearrange("p (t m) -> p m t", t=PACK), w2sc_raw[:].rearrange("p (m t) -> p m t", t=PACK)
-                )
+        def load_gain(h):
+            gain[h] = in_slot([P, PACK, HALF], F32, "gain%d" % h, 4 + h)
+            for q in range(4):
+                nc.sync.dma_start(gain[h][32 * q : 32 * (q + 1)], wgo_v[:, :, HALF * h : HALF * (h + 1)])
 
-        steps = {}
-        step0 = ring.tile([P, S], F32, name="step0", tag="then_step0", bufs=1)
-        steps[0] = step0[:]
-        steps[3] = stream([P, S], F32, "step3")[:]
-
-        def second(t, h):
-            acc2 = psum.tile([P, HALF], F32, name="acc2", tag="acc2")
+        def place_step(t, h, slot, quarter):
+            acc2 = psum.tile([P, HALF], F32, name="acc2", tag="acc2", bufs=2)
             for b in range(2):
                 nc.tensor.matmul_mx(
                     out=acc2[:],
@@ -249,31 +243,56 @@ def tile_list_coil_trust_weighting_kernel(
                     start=(b == 0),
                     stop=(b == 1),
                 )
-            nc.scalar.copy(steps[t][:, HALF * h : HALF * (h + 1)], acc2[:])
+            step = in_slot([P, HALF], F32, "step%d%d" % (t, h), slot, quarter)
+            nc.scalar.copy(step[:], acc2[:])
+            nc.vector.tensor_tensor(pages[t][:].indirect(half_list(place, h)), step[:], gain[h][:, t, :], ALU.mult)
 
-        def scatter(t, lo, hi):
-            nc.vector.tensor_tensor(
-                pages[t][:].indirect(place[:, lo // 16 : hi // 16]), steps[t][:, lo:hi], gain[:, t, lo:hi], ALU.mult
-            )
-
-        make_z(3)
-        second(0, 0)
-        scatter(0, 0, HALF)
-        step21 = gated_slot([P, 2, S], "step21", 3)
-        steps[2] = step21[:, 0, :]
-        steps[1] = step21[:, 1, :]
-        for t in (2, 1):
-            second(t, 0)
-            scatter(t, 0, HALF)
-        second(3, 0)
-        for t in (0, 2, 1, 3):
-            second(t, 1)
+        residual(0, 0)
+        residual(0, 1)
+        for i in range(len(order)):
+            if 0 < i < len(order) - 1:
+                residual(i + 1, 0)
+            if i > 0:
+                square(i)
+            if 0 < i < len(order) - 1:
+                residual(i + 1, 1)
+            z_pair(i)
+            if i == 0:
+                residual(1, 0)
+                residual(1, 1)
+            if i == 0:
+                quant_w1(0, 1, nc.vector.tensor_copy)
+            if i == 1:
+                quant_w1(1, 1, nc.scalar.copy)
+                load_gain(0)
+                load_margins(1, 2)
+                load_margins(1, 3)
+                load_gain(1)
+                clear_page(1, 6)
+            if i == 3:
+                make_z(0, 0)
+            if i == 4:
+                make_z(0, 1)
+                nc.vector.tensor_copy(
+                    w2w[:].rearrange("p a (t m) -> p a m t", t=PACK),
+                    w2raw[:].rearrange("p a (m t) -> p a m t", t=PACK),
+                )
+                nc.vector.tensor_copy(
+                    w2sc[:].rearrange("p (t m) -> p m t", t=PACK), w2sc_raw[:].rearrange("p (m t) -> p m t", t=PACK)
+                )
+            if i == 6:
+                make_z(1, 0)
+        place_step(0, 0, 1, 1)
+        place_step(1, 0, 13, 0)
+        make_z(1, 1)
+        place_step(2, 0, 14, zslot[1, 1])
+        place_step(3, 0, 14, zslot[1, 1] + 1)
 
         out_v = out_0.rearrange("(p t) m -> p t m", t=PACK)
         n_chunks = T2 // CHUNK
-        pairs = [stream([P, 2, CHUNK, 2], BF16, "pairs") for c in range(n_chunks)]
+        pairs = [in_slot([P, 2, CHUNK, 2], BF16, "pairs%d" % c, 8, 2 * c) for c in range(n_chunks)]
         for t in (0, 2, 1, 3):
-            scatter(t, HALF if t < 3 else 0, S)
+            place_step(t, 1, 7, t)
             nc.sync.dma_start(out_v[:, t, :], pages[t][:])
             for c in range(n_chunks):
                 src = pages[t][:, CHUNK * c : CHUNK * (c + 1)]
@@ -284,13 +303,12 @@ def tile_list_coil_trust_weighting_kernel(
                     nc.scalar.copy(pairs[c][:, t // 2, :, t % 2], src)
 
         words_v = out_1[0].rearrange("p m t -> p (m t)").bitcast(I32)
-        ybf = {}
         for c in (0, 2, 1, 3):
             copy = nc.vector.tensor_copy if c < n_chunks // 2 else nc.scalar.copy
             copy(pairs[c][:, 1, :, 1], pages[3][:, CHUNK * c : CHUNK * (c + 1)])
-            ybf[c] = weave(copy, pairs[c], "ybf")
+            ybf = weave(copy, pairs[c], "ybf")
             cols = slice(CHUNK * c, CHUNK * (c + 1))
-            nc.vector.quantize_mx(out=ycodes[:, cols].bitcast(E4M3), scales=yscales[:, cols], in_=ybf[c][:])
+            nc.vector.quantize_mx(out=ycodes[:, cols].bitcast(E4M3), scales=yscales[:, cols], in_=ybf[:])
             nc.sync.dma_start(words_v[:, cols], ycodes[:, cols].bitcast(I32))
         for q in range(4):
             queue = nc.sync if q % 2 == 0 else nc.scalar

@@ -40,7 +40,7 @@ def tile_list_coil_trust_weighting_kernel(
             return slots.tile(shape, dtype, name=name, align_bytes=64, offset=SLOT * slot + QUARTER * quarter)
 
         def grouped(name):
-            return ring.tile([P, PACK * HALF], BF16, name=name, tag="grouped", bufs=3, align_bytes=64)
+            return ring.tile([P, PACK * HALF], BF16, name=name, tag="grouped", bufs=4, align_bytes=64)
 
         def half_list(offsets, h):
             return offsets[:, LCOL * h : LCOL * (h + 1)]
@@ -57,9 +57,12 @@ def tile_list_coil_trust_weighting_kernel(
         ycodes = keep.tile([P, T2], U32, name="ycodes", align_bytes=64)
         yscales = keep.tile([P, T2], U8, name="yscales", align_bytes=64)
 
-        for a in range(2):
-            nc.gpsimd.memset(tsc[a][:].bitcast(I32), 0)
+        nc.gpsimd.memset(tsc[0][:].bitcast(I32), 0)
+        nc.vector.memset(tsc[1][:].bitcast(I32), 0)
         nc.vector.memset(w2sc_raw[:].bitcast(I32), 0)
+        pages = {t: in_slot([P, T2], F32, "page%d" % t, 10 + t) for t in range(2)}
+        for t in range(2):
+            nc.vector.memset(pages[t][:], 0.0)
 
         tabw = {}
         w1raw = {}
@@ -83,7 +86,7 @@ def tile_list_coil_trust_weighting_kernel(
         sT_v = sT.rearrange("(b p t) c -> b t p c", b=2, t=PACK)
 
         def load_margins(b, t):
-            margins[b, t] = in_slot([P, T], F32, "margins%d%d" % (b, t), 6 + PACK * b + t)
+            margins[b, t] = in_slot([P, T], F32, "margins%d%d" % (b, t), 6 + t if b == 0 else (0, 2, 12, 13)[t])
             nc.sync.dma_start(margins[b, t][:], sT_v[b, t])
 
         nc.sync.dma_start(pick[:], offs)
@@ -94,14 +97,14 @@ def tile_list_coil_trust_weighting_kernel(
         load_w1(1, 0)
         load_tab(0)
         load_tab(1)
+        load_w1(0, 1)
         load_margins(0, 0)
         load_margins(0, 1)
-        load_w1(0, 1)
         load_w1(1, 1)
         load_margins(0, 2)
         load_margins(0, 3)
-        load_margins(1, 0)
-        load_margins(1, 1)
+        for t in range(PACK):
+            load_margins(1, t)
         nc.sync.dma_start(w2raw[:], w2_words.rearrange("a p c i -> p a (c i)").bitcast(I32))
         for q in range(4):
             nc.sync.dma_start(
@@ -122,20 +125,23 @@ def tile_list_coil_trust_weighting_kernel(
             vsc[a, h] = keep.tile([P, HALF], U8, name="vsc%d%d" % (a, h), align_bytes=64)
             nc.vector.tensor_copy(vsc[a, h][:], tsc[a][:].indirect(half_list(pick, h)))
 
+        w1bf = {}
         w1c = {}
         w1s = {}
 
-        def quant_w1(a, b, copy):
-            g = grouped("w1bf")
-            copy(
-                g[:].rearrange("p (u e m j) -> p u m j e", u=2, e=2, j=PACK),
-                w1raw[a, b][:].rearrange("p j (m u e) -> p u m j e", u=2, e=2),
-            )
+        def round_w1(a, b, scalar_m):
+            g = w1bf[a, b] = grouped("w1bf")
+            dst = g[:].rearrange("p (u e m j) -> p u m j e", u=2, e=2, j=PACK)
+            src = w1raw[a, b][:].rearrange("p j (m u e) -> p u m j e", u=2, e=2)
+            if scalar_m > 0:
+                nc.scalar.copy(dst[:, :, :scalar_m], src[:, :, :scalar_m])
+            if scalar_m < P:
+                nc.vector.tensor_copy(dst[:, :, scalar_m:], src[:, :, scalar_m:])
+
+        def quant_w1(a, b):
             w1c[a, b] = keep.tile([P, KP], U32, name="w1c%d%d" % (a, b), align_bytes=64)
             w1s[a, b] = keep.tile([P, KP], U8, name="w1s%d%d" % (a, b), align_bytes=64)
-            nc.vector.quantize_mx(out=w1c[a, b][:].bitcast(E4M3), scales=w1s[a, b][:], in_=g[:])
-
-        pages = {}
+            nc.vector.quantize_mx(out=w1c[a, b][:].bitcast(E4M3), scales=w1s[a, b][:], in_=w1bf[a, b][:])
 
         def clear_page(t, slot):
             pages[t] = in_slot([P, T2], F32, "page%d" % t, slot)
@@ -145,34 +151,33 @@ def tile_list_coil_trust_weighting_kernel(
         for a in range(2):
             for h in range(2):
                 gather_scales(a, h)
-        quant_w1(0, 0, nc.scalar.copy)
+        round_w1(0, 0, P)
+        quant_w1(0, 0)
         gather_words(0, 0, keep.tile([P, HALF], U32, name="vw00", align_bytes=64))
-        quant_w1(1, 0, nc.scalar.copy)
+        round_w1(1, 0, P)
+        quant_w1(1, 0)
         for h in range(2):
             gather_words(1, h, keep.tile([P, HALF], U32, name="vw1%d" % h, align_bytes=64))
+        round_w1(0, 1, P // 2)
         gather_words(0, 1, in_slot([P, HALF], U32, "vw01", 1))
-        clear_page(2, 2)
-        clear_page(3, 3)
-        clear_page(0, 0)
+        quant_w1(0, 1)
 
         order = [(0, 0, 0), (0, 0, 1), (0, 1, 0), (0, 1, 1), (1, 0, 0), (1, 1, 0), (1, 0, 1), (1, 1, 1)]
         zslot = {(0, 0): 0, (0, 1): 2, (1, 0): 4, (1, 1): 0}
         res = {}
-        trust = {}
+        acc = {}
+        gated = {}
         zpairs = {}
         zc = {}
         zs = {}
 
-        def residual(i, e):
+        def product(i, e):
             b, u, h = order[i]
             t = 2 * u + e
-            if e == 0:
-                res[i] = ring.tile([P, 2, HALF], F32, name="res", tag="res", bufs=4)
-                trust[i] = ring.tile([P, 2, HALF], F32, name="trust", tag="trust", bufs=3)
-            acc = psum.tile([P, HALF], F32, name="acc", tag="acc", bufs=6)
+            acc[i, e] = psum.tile([P, HALF], F32, name="acc", tag="acc", bufs=8)
             for a in range(2):
                 nc.tensor.matmul_mx(
-                    out=acc[:],
+                    out=acc[i, e][:],
                     lhsT=w1c[a, b][:, P * t : P * (t + 1)].bitcast(E4M3),
                     lhsT_scale=w1s[a, b][:, P * t : P * (t + 1)],
                     rhs=vw[a, h][:].bitcast(E5M2),
@@ -180,37 +185,47 @@ def tile_list_coil_trust_weighting_kernel(
                     start=(a == 0),
                     stop=(a == 1),
                 )
-            bias = ntgt[:, PACK * b + t : PACK * b + t + 1]
-            if i == 0:
-                nc.scalar.activation(trust[i][:, e, :], acc[:], ACT.Square, bias=bias)
-                nc.scalar.activation(trust[i][:, e, :], trust[i][:, e, :], ACT.Exp, scale=-1.0)
-            nc.scalar.activation(res[i][:, e, :], acc[:], ACT.Identity, bias=bias)
 
-        def square(i):
-            nc.scalar.activation(trust[i][:], res[i][:], ACT.Square)
+        def leave_bank(func, tile, i, e):
+            b, u, h = order[i]
+            column = PACK * b + 2 * u + e
+            nc.scalar.activation(tile[:, e, :], acc[i, e][:], func, bias=ntgt[:, column : column + 1])
+
+        def mask(i):
+            b, u, h = order[i]
+            res[i] = ring.tile([P, 2, HALF], F32, name="res", tag="res", bufs=4)
+            trust = in_slot([P, 2, HALF], F32, "trust%d" % i, 16, 2 * (i % 4))
+            gated[i] = in_slot([P, 2, HALF], F32, "gated%d" % i, 16, 2 * ((i - 1) % 4))
+            for e in range(2):
+                product(i, e)
+                leave_bank(ACT.Square, trust, i, e)
+                if i == 0:
+                    nc.scalar.activation(trust[:, e, :], trust[:, e, :], ACT.Exp, scale=-1.0)
+            leave_bank(ACT.Identity, res[i], i, 0)
+            if i > 0:
+                nc.scalar.activation(trust[:], trust[:], ACT.Exp, scale=-1.0)
+            for e in range(2):
+                nc.vector.tensor_tensor(
+                    gated[i][:, e, :], margins[b, 2 * u + e][:].indirect(half_list(pick, h)), trust[:, e, :], ALU.mult
+                )
+                if e == 0 and i > 0:
+                    z_pair(i - 1)
 
         def z_pair(i):
             b, u, h = order[i]
-            if i > 0:
-                nc.scalar.activation(trust[i][:], trust[i][:], ACT.Exp, scale=-1.0)
-            gated = ring.tile([P, 2, HALF], F32, name="gated", tag="gated", bufs=2)
-            for e in range(2):
-                nc.vector.tensor_tensor(
-                    gated[:, e, :], margins[b, 2 * u + e][:].indirect(half_list(pick, h)), trust[i][:, e, :], ALU.mult
-                )
+            leave_bank(ACT.Identity, res[i], i, 1)
             if u == 0:
                 zpairs[b, h] = in_slot([P, 2, HALF, 2], BF16, "zpairs%d%d" % (b, h), 14, zslot[b, h])
             nc.vector.scalar_tensor_tensor(
                 zpairs[b, h][:, u],
-                gated[:].rearrange("p e c -> p c e"),
+                gated[i][:].rearrange("p e c -> p c e"),
                 0.0,
                 res[i][:].rearrange("p e c -> p c e"),
                 ALU.max,
                 ALU.mult,
             )
 
-        def weave(copy, pair_tile, name):
-            tile = grouped(name)
+        def weave(copy, pair_tile, tile):
             copy(
                 tile[:].bitcast(F32).rearrange("p (c u) -> p c u", u=2),
                 pair_tile[:].rearrange("p u c e -> p u (c e)").bitcast(F32).rearrange("p u c -> p c u"),
@@ -218,21 +233,27 @@ def tile_list_coil_trust_weighting_kernel(
             return tile
 
         def make_z(b, h):
-            zbf = weave(nc.scalar.copy, zpairs[b, h], "zbf")
-            zc[b, h] = keep.tile([P, HALF], U32, name="zc%d%d" % (b, h), align_bytes=64)
+            if h == 1:
+                zbf = in_slot([P, PACK * HALF], BF16, "zbf%d" % b, 12 + b)
+            else:
+                zbf = grouped("zbf")
+            weave(nc.scalar.copy, zpairs[b, h], zbf)
+            if (b, h) == (1, 1):
+                zc[b, h] = in_slot([P, HALF], U32, "zc_last", 1, 2)
+            else:
+                zc[b, h] = keep.tile([P, HALF], U32, name="zc%d%d" % (b, h), align_bytes=64)
             zs[b, h] = keep.tile([P, HALF], U8, name="zs%d%d" % (b, h), align_bytes=64)
             nc.vector.quantize_mx(out=zc[b, h][:].bitcast(E4M3), scales=zs[b, h][:], in_=zbf[:])
 
         gain = {}
         wgo_v = wgo.rearrange("(r t) s -> r t s", t=PACK)
 
-        def load_gain(h):
-            gain[h] = in_slot([P, PACK, HALF], F32, "gain%d" % h, 4 + h)
-            for q in range(4):
-                nc.sync.dma_start(gain[h][32 * q : 32 * (q + 1)], wgo_v[:, :, HALF * h : HALF * (h + 1)])
+        def load_gain(t):
+            gain[t] = in_slot([P, S], F32, "gain%d" % t, 4, 2 * t)
+            nc.sync.dma_start(gain[t][:], wgo_v[:, t, :].partition_broadcast(4))
 
-        def place_step(t, h, slot, quarter):
-            acc2 = psum.tile([P, HALF], F32, name="acc2", tag="acc2", bufs=2)
+        def make_step(t, h, step):
+            acc2 = psum.tile([P, HALF], F32, name="acc2", tag="acc", bufs=8)
             for b in range(2):
                 nc.tensor.matmul_mx(
                     out=acc2[:],
@@ -243,36 +264,23 @@ def tile_list_coil_trust_weighting_kernel(
                     start=(b == 0),
                     stop=(b == 1),
                 )
-            step = in_slot([P, HALF], F32, "step%d%d" % (t, h), slot, quarter)
-            nc.scalar.copy(step[:], acc2[:])
-            nc.vector.tensor_tensor(pages[t][:].indirect(half_list(place, h)), step[:], gain[h][:, t, :], ALU.mult)
+            nc.scalar.copy(step, acc2[:])
 
-        residual(0, 0)
-        residual(0, 1)
+        def place_step(t, lo, hi, step):
+            nc.vector.tensor_tensor(pages[t][:].indirect(place[:, lo // 16 : hi // 16]), step, gain[t][:, lo:hi], ALU.mult)
+
+        last = len(order) - 1
         for i in range(len(order)):
-            if 0 < i < len(order) - 1:
-                residual(i + 1, 0)
-            if i > 0:
-                square(i)
-            if 0 < i < len(order) - 1:
-                residual(i + 1, 1)
-            z_pair(i)
+            mask(i)
             if i == 0:
-                residual(1, 0)
-                residual(1, 1)
-            if i == 0:
-                quant_w1(0, 1, nc.vector.tensor_copy)
+                round_w1(1, 1, 0)
             if i == 1:
-                quant_w1(1, 1, nc.scalar.copy)
-                load_gain(0)
-                load_margins(1, 2)
-                load_margins(1, 3)
-                load_gain(1)
-                clear_page(1, 6)
-            if i == 3:
-                make_z(0, 0)
+                quant_w1(1, 1)
+                for t in range(PACK):
+                    load_gain(t)
             if i == 4:
-                make_z(0, 1)
+                make_z(0, 0)
+            if i == 5:
                 nc.vector.tensor_copy(
                     w2w[:].rearrange("p a (t m) -> p a m t", t=PACK),
                     w2raw[:].rearrange("p a (m t) -> p a m t", t=PACK),
@@ -280,19 +288,29 @@ def tile_list_coil_trust_weighting_kernel(
                 nc.vector.tensor_copy(
                     w2sc[:].rearrange("p (t m) -> p m t", t=PACK), w2sc_raw[:].rearrange("p (m t) -> p m t", t=PACK)
                 )
-            if i == 6:
-                make_z(1, 0)
-        place_step(0, 0, 1, 1)
-        place_step(1, 0, 13, 0)
+        make_z(1, 0)
+        z_pair(last)
+        make_z(0, 1)
+        clear_page(2, 12)
+        first_step = in_slot([P, HALF], F32, "first_step", 1, 2)
+        make_step(0, 0, first_step[:])
+        place_step(0, 0, HALF, first_step[:])
         make_z(1, 1)
-        place_step(2, 0, 14, zslot[1, 1])
-        place_step(3, 0, 14, zslot[1, 1] + 1)
+        clear_page(3, 13)
+        steps = [in_slot([P, S], F32, "step%d" % t, 6, 2 * t) for t in range(PACK)]
+        for t in range(1, PACK):
+            make_step(t, 0, steps[t][:, :HALF])
+            if t < 3:
+                place_step(t, 0, HALF, steps[t][:, :HALF])
+        for t in (0, 2, 1, 3):
+            make_step(t, 1, steps[t][:, HALF:])
 
         out_v = out_0.rearrange("(p t) m -> p t m", t=PACK)
         n_chunks = T2 // CHUNK
         pairs = [in_slot([P, 2, CHUNK, 2], BF16, "pairs%d" % c, 8, 2 * c) for c in range(n_chunks)]
         for t in (0, 2, 1, 3):
-            place_step(t, 1, 7, t)
+            lo = HALF if t < 3 else 0
+            place_step(t, lo, S, steps[t][:, lo:])
             nc.sync.dma_start(out_v[:, t, :], pages[t][:])
             for c in range(n_chunks):
                 src = pages[t][:, CHUNK * c : CHUNK * (c + 1)]
@@ -303,12 +321,15 @@ def tile_list_coil_trust_weighting_kernel(
                     nc.scalar.copy(pairs[c][:, t // 2, :, t % 2], src)
 
         words_v = out_1[0].rearrange("p m t -> p (m t)").bitcast(I32)
-        for c in (0, 2, 1, 3):
-            copy = nc.vector.tensor_copy if c < n_chunks // 2 else nc.scalar.copy
-            copy(pairs[c][:, 1, :, 1], pages[3][:, CHUNK * c : CHUNK * (c + 1)])
-            ybf = weave(copy, pairs[c], "ybf")
+        copies = [nc.vector.tensor_copy if c < n_chunks // 2 else nc.scalar.copy for c in range(n_chunks)]
+        for c in (0, 2, 1):
+            copies[c](pairs[c][:, 1, :, 1], pages[3][:, CHUNK * c : CHUNK * (c + 1)])
+        ybf = {c: weave(copies[c], pairs[c], grouped("ybf")) for c in (0, 2, 1)}
+        copies[3](pairs[3][:, 1, :, 1], pages[3][:, CHUNK * 3 :])
+        ybf[3] = weave(copies[3], pairs[3], grouped("ybf"))
+        for c in (0, 1, 2, 3):
             cols = slice(CHUNK * c, CHUNK * (c + 1))
-            nc.vector.quantize_mx(out=ycodes[:, cols].bitcast(E4M3), scales=yscales[:, cols], in_=ybf[:])
+            nc.vector.quantize_mx(out=ycodes[:, cols].bitcast(E4M3), scales=yscales[:, cols], in_=ybf[c][:])
             nc.sync.dma_start(words_v[:, cols], ycodes[:, cols].bitcast(I32))
         for q in range(4):
             queue = nc.sync if q % 2 == 0 else nc.scalar

@@ -24,6 +24,7 @@ LCOL = HALF // 16
 CHUNK = 512
 SLOT = 8192
 QUARTER = SLOT // 4
+SPLIT = 64
 
 
 def tile_list_coil_trust_weighting_kernel(
@@ -47,7 +48,7 @@ def tile_list_coil_trust_weighting_kernel(
 
         pick = keep.tile([P, S // 16], U16, name="pick")
         place = keep.tile([P, S // 16], U16, name="place")
-        tsc = [keep.tile([P, T], U8, name="tsc%d" % a, align_bytes=64) for a in range(2)]
+        tsc = [in_slot([P, T], U8, "tsc%d" % a, 18, a) for a in range(2)]
         w2sc_raw = keep.tile([P, N], U8, name="w2sc_raw", align_bytes=64)
         w2sc = keep.tile([P, N], U8, name="w2sc", align_bytes=64)
         w2raw = keep.tile([P, 2, N], I32, name="w2raw", align_bytes=64)
@@ -60,9 +61,8 @@ def tile_list_coil_trust_weighting_kernel(
         nc.gpsimd.memset(tsc[0][:].bitcast(I32), 0)
         nc.vector.memset(tsc[1][:].bitcast(I32), 0)
         nc.vector.memset(w2sc_raw[:].bitcast(I32), 0)
-        pages = {t: in_slot([P, T2], F32, "page%d" % t, 10 + t) for t in range(2)}
-        for t in range(2):
-            nc.vector.memset(pages[t][:], 0.0)
+        pages = {0: in_slot([P, T2], F32, "page0", 10)}
+        nc.vector.memset(pages[0][:], 0.0)
 
         tabw = {}
         w1raw = {}
@@ -78,24 +78,27 @@ def tile_list_coil_trust_weighting_kernel(
                     tsc[a][32 * q : 32 * q + 4, :].bitcast(I32), tab_scales[a, 4 * q : 4 * q + 4, :].bitcast(I32)
                 )
 
-        def load_w1(a, b):
-            w1raw[a, b] = in_slot([P, PACK, KP], F32, "w1raw%d%d" % (a, b), 2 + 2 * b + a)
-            rows = w1[KP * a : KP * (a + 1), KP * b : KP * (b + 1)]
-            nc.sync.dma_start(w1raw[a, b][:], rows.rearrange("(p j) c -> p j c", j=PACK))
+        def load_w1(a, b, lo=0, hi=P):
+            tile = in_slot([P, PACK, PACK * (hi - lo)], F32, "w1raw%d%d%d" % (a, b, lo), 2 + 2 * b + a, lo // 32)
+            w1raw[a, b, lo] = tile
+            rows = w1[KP * a : KP * (a + 1), KP * b + PACK * lo : KP * b + PACK * hi]
+            nc.sync.dma_start(tile[:], rows.rearrange("(p j) c -> p j c", j=PACK))
 
         sT_v = sT.rearrange("(b p t) c -> b t p c", b=2, t=PACK)
 
         def load_margins(b, t):
-            margins[b, t] = in_slot([P, T], F32, "margins%d%d" % (b, t), 6 + t if b == 0 else (0, 2, 12, 13)[t])
+            margins[b, t] = in_slot([P, T], F32, "margins%d%d" % (b, t), 6 + t if b == 0 else (1, 2, 12, 13)[t])
             nc.sync.dma_start(margins[b, t][:], sT_v[b, t])
 
         nc.sync.dma_start(pick[:], offs)
         nc.sync.dma_start(tgt[:], target.rearrange("(b p t) -> p b t", b=2, t=PACK))
         load_scales(0)
         load_w1(0, 0)
+        nc.sync.dma_start(place[:], offs2)
         load_scales(1)
-        load_w1(1, 0)
+        load_w1(1, 0, 0, SPLIT)
         load_tab(0)
+        load_w1(1, 0, SPLIT, P)
         load_tab(1)
         load_w1(0, 1)
         load_margins(0, 0)
@@ -103,23 +106,22 @@ def tile_list_coil_trust_weighting_kernel(
         load_w1(1, 1)
         load_margins(0, 2)
         load_margins(0, 3)
-        for t in range(PACK):
-            load_margins(1, t)
         nc.sync.dma_start(w2raw[:], w2_words.rearrange("a p c i -> p a (c i)").bitcast(I32))
         for q in range(4):
             nc.sync.dma_start(
                 w2sc_raw[32 * q : 32 * q + 8, :].bitcast(I32), w2_scales[:, 4 * q : 4 * q + 4, :].bitcast(I32)
             )
-        nc.sync.dma_start(place[:], offs2)
+        for t in range(PACK):
+            load_margins(1, t)
 
         nc.scalar.mul(ntgt[:], tgt[:].rearrange("p b t -> p (b t)"), -1.0)
 
         vw = {}
         vsc = {}
 
-        def gather_words(a, h, tile):
-            vw[a, h] = tile
-            nc.vector.tensor_copy(tile[:], tabw[a][:].indirect(half_list(pick, h)))
+        def gather_words(a, h):
+            vw[a, h] = keep.tile([P, HALF], U32, name="vw%d%d" % (a, h), align_bytes=64)
+            nc.vector.tensor_copy(vw[a, h][:], tabw[a][:].indirect(half_list(pick, h)))
 
         def gather_scales(a, h):
             vsc[a, h] = keep.tile([P, HALF], U8, name="vsc%d%d" % (a, h), align_bytes=64)
@@ -129,19 +131,22 @@ def tile_list_coil_trust_weighting_kernel(
         w1c = {}
         w1s = {}
 
-        def round_w1(a, b, scalar_m):
-            g = w1bf[a, b] = grouped("w1bf")
-            dst = g[:].rearrange("p (u e m j) -> p u m j e", u=2, e=2, j=PACK)
-            src = w1raw[a, b][:].rearrange("p j (m u e) -> p u m j e", u=2, e=2)
-            if scalar_m > 0:
-                nc.scalar.copy(dst[:, :, :scalar_m], src[:, :, :scalar_m])
-            if scalar_m < P:
-                nc.vector.tensor_copy(dst[:, :, scalar_m:], src[:, :, scalar_m:])
+        def round_w1(copy, a, b, lo=0, hi=P, piece=0):
+            if lo == 0:
+                w1bf[a, b] = grouped("w1bf")
+                if b == 0:
+                    w1c[a, b] = in_slot([P, KP], U32, "w1c%d0" % a, *((18, 1), (0, 0))[a])
+                else:
+                    w1c[a, b] = keep.tile([P, KP], U32, name="w1c%d%d" % (a, b), align_bytes=64)
+                w1s[a, b] = keep.tile([P, KP], U8, name="w1s%d%d" % (a, b), align_bytes=64)
+            dst = w1bf[a, b][:].rearrange("p (u e m j) -> p u m j e", u=2, e=2, j=PACK)
+            src = w1raw[a, b, piece][:].rearrange("p j (m u e) -> p u m j e", u=2, e=2)
+            copy(dst[:, :, lo:hi], src[:, :, lo - piece : hi - piece])
 
-        def quant_w1(a, b):
-            w1c[a, b] = keep.tile([P, KP], U32, name="w1c%d%d" % (a, b), align_bytes=64)
-            w1s[a, b] = keep.tile([P, KP], U8, name="w1s%d%d" % (a, b), align_bytes=64)
-            nc.vector.quantize_mx(out=w1c[a, b][:].bitcast(E4M3), scales=w1s[a, b][:], in_=w1bf[a, b][:])
+        def quant_w1(a, b, lo=0, hi=KP):
+            nc.vector.quantize_mx(
+                out=w1c[a, b][:, lo:hi].bitcast(E4M3), scales=w1s[a, b][:, lo:hi], in_=w1bf[a, b][:, PACK * lo : PACK * hi]
+            )
 
         def clear_page(t, slot):
             pages[t] = in_slot([P, T2], F32, "page%d" % t, slot)
@@ -151,21 +156,22 @@ def tile_list_coil_trust_weighting_kernel(
         for a in range(2):
             for h in range(2):
                 gather_scales(a, h)
-        round_w1(0, 0, P)
+        round_w1(nc.scalar.copy, 0, 0)
         quant_w1(0, 0)
-        gather_words(0, 0, keep.tile([P, HALF], U32, name="vw00", align_bytes=64))
-        round_w1(1, 0, P)
+        for h in range(2):
+            gather_words(0, h)
+        round_w1(nc.scalar.copy, 1, 0, 0, SPLIT)
+        round_w1(nc.scalar.copy, 1, 0, SPLIT, P, SPLIT)
         quant_w1(1, 0)
         for h in range(2):
-            gather_words(1, h, keep.tile([P, HALF], U32, name="vw1%d" % h, align_bytes=64))
-        round_w1(0, 1, P // 2)
-        gather_words(0, 1, in_slot([P, HALF], U32, "vw01", 1))
-        quant_w1(0, 1)
+            gather_words(1, h)
+        round_w1(nc.vector.tensor_copy, 0, 1)
 
         order = [(0, 0, 0), (0, 0, 1), (0, 1, 0), (0, 1, 1), (1, 0, 0), (1, 1, 0), (1, 0, 1), (1, 1, 1)]
         zslot = {(0, 0): 0, (0, 1): 2, (1, 0): 4, (1, 1): 0}
         res = {}
         acc = {}
+        trust = {}
         gated = {}
         zpairs = {}
         zc = {}
@@ -191,25 +197,43 @@ def tile_list_coil_trust_weighting_kernel(
             column = PACK * b + 2 * u + e
             nc.scalar.activation(tile[:, e, :], acc[i, e][:], func, bias=ntgt[:, column : column + 1])
 
-        def mask(i):
-            b, u, h = order[i]
+        def open_pair(i):
             res[i] = ring.tile([P, 2, HALF], F32, name="res", tag="res", bufs=4)
-            trust = in_slot([P, 2, HALF], F32, "trust%d" % i, 16, 2 * (i % 4))
-            gated[i] = in_slot([P, 2, HALF], F32, "gated%d" % i, 16, 2 * ((i - 1) % 4))
+            trust[i] = in_slot([P, 2, HALF], F32, "trust%d" % i, 16, 2 * (i % 4))
+            if i == 1:
+                gated[i] = in_slot([P, 2, HALF], F32, "gated1", 11)
+            else:
+                gated[i] = in_slot([P, 2, HALF], F32, "gated%d" % i, 16, 2 * ((i - 1) % 4))
+
+        def gate(i, e):
+            b, u, h = order[i]
+            nc.vector.tensor_tensor(
+                gated[i][:, e, :], margins[b, 2 * u + e][:].indirect(half_list(pick, h)), trust[i][:, e, :], ALU.mult
+            )
+
+        def first_pairs():
+            for i in range(2):
+                open_pair(i)
+            for e in range(2):
+                for i in range(2):
+                    product(i, e)
+                    leave_bank(ACT.Square, trust[i], i, e)
+                    nc.scalar.activation(trust[i][:, e, :], trust[i][:, e, :], ACT.Exp, scale=-1.0)
+                    gate(i, e)
+            leave_bank(ACT.Identity, res[0], 0, 0)
+            z_pair(0)
+            leave_bank(ACT.Identity, res[1], 1, 0)
+
+        def mask(i):
+            open_pair(i)
             for e in range(2):
                 product(i, e)
-                leave_bank(ACT.Square, trust, i, e)
-                if i == 0:
-                    nc.scalar.activation(trust[:, e, :], trust[:, e, :], ACT.Exp, scale=-1.0)
+                leave_bank(ACT.Square, trust[i], i, e)
             leave_bank(ACT.Identity, res[i], i, 0)
-            if i > 0:
-                nc.scalar.activation(trust[:], trust[:], ACT.Exp, scale=-1.0)
-            for e in range(2):
-                nc.vector.tensor_tensor(
-                    gated[i][:, e, :], margins[b, 2 * u + e][:].indirect(half_list(pick, h)), trust[:, e, :], ALU.mult
-                )
-                if e == 0 and i > 0:
-                    z_pair(i - 1)
+            nc.scalar.activation(trust[i][:], trust[i][:], ACT.Exp, scale=-1.0)
+            gate(i, 0)
+            z_pair(i - 1)
+            gate(i, 1)
 
         def z_pair(i):
             b, u, h = order[i]
@@ -233,8 +257,8 @@ def tile_list_coil_trust_weighting_kernel(
             return tile
 
         def make_z(b, h):
-            if h == 1:
-                zbf = in_slot([P, PACK * HALF], BF16, "zbf%d" % b, 12 + b)
+            if (b, h) != (1, 0):
+                zbf = in_slot([P, PACK * HALF], BF16, "zbf%d%d" % (b, h), 11 + b + h)
             else:
                 zbf = grouped("zbf")
             weave(nc.scalar.copy, zpairs[b, h], zbf)
@@ -270,17 +294,19 @@ def tile_list_coil_trust_weighting_kernel(
             nc.vector.tensor_tensor(pages[t][:].indirect(place[:, lo // 16 : hi // 16]), step, gain[t][:, lo:hi], ALU.mult)
 
         last = len(order) - 1
-        for i in range(len(order)):
+        quant_w1(0, 1)
+        first_pairs()
+        round_w1(nc.vector.tensor_copy, 1, 1)
+        for i in range(2, len(order)):
             mask(i)
-            if i == 0:
-                round_w1(1, 1, 0)
-            if i == 1:
+            if i == 2:
                 quant_w1(1, 1)
                 for t in range(PACK):
                     load_gain(t)
             if i == 4:
                 make_z(0, 0)
-            if i == 5:
+                clear_page(1, 11)
+            if i == 3:
                 nc.vector.tensor_copy(
                     w2w[:].rearrange("p a (t m) -> p a m t", t=PACK),
                     w2raw[:].rearrange("p a (m t) -> p a m t", t=PACK),
@@ -308,6 +334,7 @@ def tile_list_coil_trust_weighting_kernel(
         out_v = out_0.rearrange("(p t) m -> p t m", t=PACK)
         n_chunks = T2 // CHUNK
         pairs = [in_slot([P, 2, CHUNK, 2], BF16, "pairs%d" % c, 8, 2 * c) for c in range(n_chunks)]
+        ybf = {}
         for t in (0, 2, 1, 3):
             lo = HALF if t < 3 else 0
             place_step(t, lo, S, steps[t][:, lo:])
@@ -319,14 +346,17 @@ def tile_list_coil_trust_weighting_kernel(
                     nc.scalar.copy(pairs[c][:, 1], src.unsqueeze(2).to_broadcast([P, CHUNK, 2]))
                 elif t < 3:
                     nc.scalar.copy(pairs[c][:, t // 2, :, t % 2], src)
+                if t == 1 and on_vector:
+                    ybf[c] = weave(nc.scalar.copy, pairs[c], grouped("ybf"))
 
         words_v = out_1[0].rearrange("p m t -> p (m t)").bitcast(I32)
-        copies = [nc.vector.tensor_copy if c < n_chunks // 2 else nc.scalar.copy for c in range(n_chunks)]
-        for c in (0, 2, 1):
-            copies[c](pairs[c][:, 1, :, 1], pages[3][:, CHUNK * c : CHUNK * (c + 1)])
-        ybf = {c: weave(copies[c], pairs[c], grouped("ybf")) for c in (0, 2, 1)}
-        copies[3](pairs[3][:, 1, :, 1], pages[3][:, CHUNK * 3 :])
-        ybf[3] = weave(copies[3], pairs[3], grouped("ybf"))
+        for c in range(n_chunks):
+            src = pages[3][:, CHUNK * c : CHUNK * (c + 1)]
+            if c < n_chunks // 2:
+                nc.vector.tensor_copy(ybf[c][:].rearrange("p (m t) -> p m t", t=PACK)[:, :, 3], src)
+            else:
+                nc.scalar.copy(pairs[c][:, 1, :, 1], src)
+                ybf[c] = weave(nc.scalar.copy, pairs[c], grouped("ybf"))
         for c in (0, 1, 2, 3):
             cols = slice(CHUNK * c, CHUNK * (c + 1))
             nc.vector.quantize_mx(out=ycodes[:, cols].bitcast(E4M3), scales=yscales[:, cols], in_=ybf[c][:])

@@ -25,6 +25,8 @@ CHUNK = 512
 SLOT = 8192
 QUARTER = SLOT // 4
 SPLIT = 64
+EDGES = (0, 512, 1024, 1536, 1792, 2048)
+ON_VECTOR = 2
 
 
 def tile_list_coil_trust_weighting_kernel(
@@ -41,7 +43,7 @@ def tile_list_coil_trust_weighting_kernel(
             return slots.tile(shape, dtype, name=name, align_bytes=64, offset=SLOT * slot + QUARTER * quarter)
 
         def grouped(name):
-            return ring.tile([P, PACK * HALF], BF16, name=name, tag="grouped", bufs=4, align_bytes=64)
+            return ring.tile([P, PACK * HALF], BF16, name=name, tag="grouped", bufs=3, align_bytes=64)
 
         def half_list(offsets, h):
             return offsets[:, LCOL * h : LCOL * (h + 1)]
@@ -61,8 +63,9 @@ def tile_list_coil_trust_weighting_kernel(
         nc.gpsimd.memset(tsc[0][:].bitcast(I32), 0)
         nc.vector.memset(tsc[1][:].bitcast(I32), 0)
         nc.vector.memset(w2sc_raw[:].bitcast(I32), 0)
-        pages = {0: in_slot([P, T2], F32, "page0", 10)}
-        nc.vector.memset(pages[0][:], 0.0)
+        pages = {t: in_slot([P, T2], F32, "page%d" % t, 10 + t) for t in range(2)}
+        for t in range(2):
+            nc.vector.memset(pages[t][:], 0.0)
 
         tabw = {}
         w1raw = {}
@@ -123,9 +126,9 @@ def tile_list_coil_trust_weighting_kernel(
             vw[a, h] = keep.tile([P, HALF], U32, name="vw%d%d" % (a, h), align_bytes=64)
             nc.vector.tensor_copy(vw[a, h][:], tabw[a][:].indirect(half_list(pick, h)))
 
-        def gather_scales(a, h):
-            vsc[a, h] = keep.tile([P, HALF], U8, name="vsc%d%d" % (a, h), align_bytes=64)
-            nc.vector.tensor_copy(vsc[a, h][:], tsc[a][:].indirect(half_list(pick, h)))
+        def gather_scales(a):
+            vsc[a] = keep.tile([P, S], U8, name="vsc%d" % a, align_bytes=64)
+            nc.vector.tensor_copy(vsc[a][:], tsc[a][:].indirect(pick[:]))
 
         w1bf = {}
         w1c = {}
@@ -154,8 +157,7 @@ def tile_list_coil_trust_weighting_kernel(
                 nc.gpsimd.memset(pages[t][:, CHUNK * c : CHUNK * (c + 1)], 0.0)
 
         for a in range(2):
-            for h in range(2):
-                gather_scales(a, h)
+            gather_scales(a)
         round_w1(nc.scalar.copy, 0, 0)
         quant_w1(0, 0)
         for h in range(2):
@@ -187,7 +189,7 @@ def tile_list_coil_trust_weighting_kernel(
                     lhsT=w1c[a, b][:, P * t : P * (t + 1)].bitcast(E4M3),
                     lhsT_scale=w1s[a, b][:, P * t : P * (t + 1)],
                     rhs=vw[a, h][:].bitcast(E5M2),
-                    rhs_scale=vsc[a, h][:],
+                    rhs_scale=vsc[a][:, HALF * h : HALF * (h + 1)],
                     start=(a == 0),
                     stop=(a == 1),
                 )
@@ -201,7 +203,7 @@ def tile_list_coil_trust_weighting_kernel(
             res[i] = ring.tile([P, 2, HALF], F32, name="res", tag="res", bufs=4)
             trust[i] = in_slot([P, 2, HALF], F32, "trust%d" % i, 16, 2 * (i % 4))
             if i == 1:
-                gated[i] = in_slot([P, 2, HALF], F32, "gated1", 11)
+                gated[i] = in_slot([P, 2, HALF], F32, "gated1", 0, 2)
             else:
                 gated[i] = in_slot([P, 2, HALF], F32, "gated%d" % i, 16, 2 * ((i - 1) % 4))
 
@@ -232,7 +234,8 @@ def tile_list_coil_trust_weighting_kernel(
             leave_bank(ACT.Identity, res[i], i, 0)
             nc.scalar.activation(trust[i][:], trust[i][:], ACT.Exp, scale=-1.0)
             gate(i, 0)
-            z_pair(i - 1)
+            if i < len(order) - 1:
+                z_pair(i - 1)
             gate(i, 1)
 
         def z_pair(i):
@@ -249,19 +252,18 @@ def tile_list_coil_trust_weighting_kernel(
                 ALU.mult,
             )
 
-        def weave(copy, pair_tile, tile):
-            copy(
+        def weave(pair_tile, tile):
+            nc.scalar.copy(
                 tile[:].bitcast(F32).rearrange("p (c u) -> p c u", u=2),
                 pair_tile[:].rearrange("p u c e -> p u (c e)").bitcast(F32).rearrange("p u c -> p c u"),
             )
-            return tile
 
         def make_z(b, h):
-            if (b, h) != (1, 0):
-                zbf = in_slot([P, PACK * HALF], BF16, "zbf%d%d" % (b, h), 11 + b + h)
+            if h == 1:
+                zbf = in_slot([P, PACK * HALF], BF16, "zbf%d%d" % (b, h), 12 + b)
             else:
                 zbf = grouped("zbf")
-            weave(nc.scalar.copy, zpairs[b, h], zbf)
+            weave(zpairs[b, h], zbf)
             if (b, h) == (1, 1):
                 zc[b, h] = in_slot([P, HALF], U32, "zc_last", 1, 2)
             else:
@@ -305,7 +307,6 @@ def tile_list_coil_trust_weighting_kernel(
                     load_gain(t)
             if i == 4:
                 make_z(0, 0)
-                clear_page(1, 11)
             if i == 3:
                 nc.vector.tensor_copy(
                     w2w[:].rearrange("p a (t m) -> p a m t", t=PACK),
@@ -315,6 +316,7 @@ def tile_list_coil_trust_weighting_kernel(
                     w2sc[:].rearrange("p (t m) -> p m t", t=PACK), w2sc_raw[:].rearrange("p (m t) -> p m t", t=PACK)
                 )
         make_z(1, 0)
+        z_pair(last - 1)
         z_pair(last)
         make_z(0, 1)
         clear_page(2, 12)
@@ -332,33 +334,30 @@ def tile_list_coil_trust_weighting_kernel(
             make_step(t, 1, steps[t][:, HALF:])
 
         out_v = out_0.rearrange("(p t) m -> p t m", t=PACK)
-        n_chunks = T2 // CHUNK
-        pairs = [in_slot([P, 2, CHUNK, 2], BF16, "pairs%d" % c, 8, 2 * c) for c in range(n_chunks)]
-        ybf = {}
+        chunks = [slice(lo, hi) for lo, hi in zip(EDGES, EDGES[1:])]
+        pairs = [in_slot([P, 2, c.stop - c.start, 2], BF16, "pairs%d" % c.start, 8, c.start // 256) for c in chunks]
+        ybf = [in_slot([P, PACK * (c.stop - c.start)], BF16, "ybf%d" % c.start, 2, c.start // 256) for c in chunks]
         for t in (0, 2, 1, 3):
             lo = HALF if t < 3 else 0
             place_step(t, lo, S, steps[t][:, lo:])
             nc.sync.dma_start(out_v[:, t, :], pages[t][:])
-            for c in range(n_chunks):
-                src = pages[t][:, CHUNK * c : CHUNK * (c + 1)]
-                on_vector = c < n_chunks // 2
-                if t == 2 and on_vector:
-                    nc.scalar.copy(pairs[c][:, 1], src.unsqueeze(2).to_broadcast([P, CHUNK, 2]))
+            for c, cols in enumerate(chunks):
+                src = pages[t][:, cols]
+                if t == 2 and c < ON_VECTOR:
+                    nc.scalar.copy(pairs[c][:, 1], src.unsqueeze(2).to_broadcast([P, cols.stop - cols.start, 2]))
                 elif t < 3:
                     nc.scalar.copy(pairs[c][:, t // 2, :, t % 2], src)
-                if t == 1 and on_vector:
-                    ybf[c] = weave(nc.scalar.copy, pairs[c], grouped("ybf"))
+                if t == 1 and c < ON_VECTOR:
+                    weave(pairs[c], ybf[c])
 
         words_v = out_1[0].rearrange("p m t -> p (m t)").bitcast(I32)
-        for c in range(n_chunks):
-            src = pages[3][:, CHUNK * c : CHUNK * (c + 1)]
-            if c < n_chunks // 2:
-                nc.vector.tensor_copy(ybf[c][:].rearrange("p (m t) -> p m t", t=PACK)[:, :, 3], src)
+        for c, cols in enumerate(chunks):
+            if c < ON_VECTOR:
+                nc.vector.tensor_copy(ybf[c][:].rearrange("p (m t) -> p m t", t=PACK)[:, :, 3], pages[3][:, cols])
             else:
-                nc.scalar.copy(pairs[c][:, 1, :, 1], src)
-                ybf[c] = weave(nc.scalar.copy, pairs[c], grouped("ybf"))
-        for c in (0, 1, 2, 3):
-            cols = slice(CHUNK * c, CHUNK * (c + 1))
+                nc.scalar.copy(pairs[c][:, 1, :, 1], pages[3][:, cols])
+                weave(pairs[c], ybf[c])
+        for c, cols in enumerate(chunks):
             nc.vector.quantize_mx(out=ycodes[:, cols].bitcast(E4M3), scales=yscales[:, cols], in_=ybf[c][:])
             nc.sync.dma_start(words_v[:, cols], ycodes[:, cols].bitcast(I32))
         for q in range(4):

@@ -63,8 +63,8 @@ def tile_list_coil_trust_weighting_kernel(
         nc.gpsimd.memset(tsc[0][:].bitcast(I32), 0)
         nc.vector.memset(tsc[1][:].bitcast(I32), 0)
         nc.vector.memset(w2sc_raw[:].bitcast(I32), 0)
-        pages = {t: in_slot([P, T2], F32, "page%d" % t, 10 + t) for t in range(2)}
-        for t in range(2):
+        pages = {t: in_slot([P, T2], F32, "page%d" % t, 10 + t) for t in range(3)}
+        for t in range(3):
             nc.vector.memset(pages[t][:], 0.0)
 
         tabw = {}
@@ -90,7 +90,7 @@ def tile_list_coil_trust_weighting_kernel(
         sT_v = sT.rearrange("(b p t) c -> b t p c", b=2, t=PACK)
 
         def load_margins(b, t):
-            margins[b, t] = in_slot([P, T], F32, "margins%d%d" % (b, t), 6 + t if b == 0 else (1, 2, 12, 13)[t])
+            margins[b, t] = in_slot([P, T], F32, "margins%d%d" % (b, t), 6 + t if b == 0 else (1, 2, 3, 13)[t])
             nc.sync.dma_start(margins[b, t][:], sT_v[b, t])
 
         nc.sync.dma_start(pick[:], offs)
@@ -259,8 +259,8 @@ def tile_list_coil_trust_weighting_kernel(
             )
 
         def make_z(b, h):
-            if h == 1:
-                zbf = in_slot([P, PACK * HALF], BF16, "zbf%d%d" % (b, h), 12 + b)
+            if (b, h) == (1, 1):
+                zbf = in_slot([P, PACK * HALF], BF16, "zbf11", 13)
             else:
                 zbf = grouped("zbf")
             weave(zpairs[b, h], zbf)
@@ -319,13 +319,13 @@ def tile_list_coil_trust_weighting_kernel(
         z_pair(last - 1)
         z_pair(last)
         make_z(0, 1)
-        clear_page(2, 12)
         first_step = in_slot([P, HALF], F32, "first_step", 1, 2)
         make_step(0, 0, first_step[:])
         place_step(0, 0, HALF, first_step[:])
         make_z(1, 1)
         clear_page(3, 13)
-        steps = [in_slot([P, S], F32, "step%d" % t, 6, 2 * t) for t in range(PACK)]
+        steps = {t: in_slot([P, S], F32, "step%d" % t, 6, 2 * t) for t in (0, 1, 3)}
+        steps[2] = in_slot([P, S], F32, "step2", 14, zslot[1, 1])
         for t in range(1, PACK):
             make_step(t, 0, steps[t][:, :HALF])
             if t < 3:

@@ -35,15 +35,14 @@ def tile_list_coil_trust_weighting_kernel(
     nc = tc.nc
     with ExitStack() as ctx:
         keep = ctx.enter_context(tc.tile_pool(name="keep", bufs=1))
-        ring = ctx.enter_context(tc.tile_pool(name="ring", bufs=1))
         slots = ctx.enter_context(tc.tile_pool(name="slots", bufs=1))
         psum = ctx.enter_context(tc.psum_pool(name="psum", bufs=1))
 
         def in_slot(shape, dtype, name, slot, quarter=0):
             return slots.tile(shape, dtype, name=name, align_bytes=64, offset=SLOT * slot + QUARTER * quarter)
 
-        def grouped(name):
-            return ring.tile([P, PACK * HALF], BF16, name=name, tag="grouped", bufs=3, align_bytes=64)
+        def grouped(name, cell):
+            return in_slot([P, PACK * HALF], BF16, name, 18, 2 + 2 * cell)
 
         def half_list(offsets, h):
             return offsets[:, LCOL * h : LCOL * (h + 1)]
@@ -136,7 +135,7 @@ def tile_list_coil_trust_weighting_kernel(
 
         def round_w1(copy, a, b, lo=0, hi=P, piece=0):
             if lo == 0:
-                w1bf[a, b] = grouped("w1bf")
+                w1bf[a, b] = grouped("w1bf%d%d" % (a, b), (2 * b + a) % 3)
                 if b == 0:
                     w1c[a, b] = in_slot([P, KP], U32, "w1c%d0" % a, *((18, 1), (0, 0))[a])
                 else:
@@ -170,7 +169,8 @@ def tile_list_coil_trust_weighting_kernel(
         round_w1(nc.vector.tensor_copy, 0, 1)
 
         order = [(0, 0, 0), (0, 0, 1), (0, 1, 0), (0, 1, 1), (1, 0, 0), (1, 1, 0), (1, 0, 1), (1, 1, 1)]
-        zslot = {(0, 0): 0, (0, 1): 2, (1, 0): 4, (1, 1): 0}
+        zslot = {(0, 0): (14, 0), (0, 1): (14, 2), (1, 0): (14, 4), (1, 1): (16, 0)}
+        last = len(order) - 1
         res = {}
         acc = {}
         trust = {}
@@ -200,12 +200,17 @@ def tile_list_coil_trust_weighting_kernel(
             nc.scalar.activation(tile[:, e, :], acc[i, e][:], func, bias=ntgt[:, column : column + 1])
 
         def open_pair(i):
-            res[i] = ring.tile([P, 2, HALF], F32, name="res", tag="res", bufs=4)
-            trust[i] = in_slot([P, 2, HALF], F32, "trust%d" % i, 16, 2 * (i % 4))
+            if i < last - 1:
+                res[i] = in_slot([P, 2, HALF], F32, "res%d" % i, 20, 2 * (i % 4))
+            else:
+                res[i] = in_slot([P, 2, HALF], F32, "res%d" % i, 3, 2 * (i % 2))
+            trust[i] = in_slot([P, 2, HALF], F32, "trust%d" % i, 16, 2 * ((i + 1) % 4))
             if i == 1:
                 gated[i] = in_slot([P, 2, HALF], F32, "gated1", 0, 2)
+            elif i < last:
+                gated[i] = in_slot([P, 2, HALF], F32, "gated%d" % i, 16, 2 * (i % 4))
             else:
-                gated[i] = in_slot([P, 2, HALF], F32, "gated%d" % i, 16, 2 * ((i - 1) % 4))
+                gated[i] = in_slot([P, 2, HALF], F32, "gated%d" % i, *zslot[1, 0])
 
         def gate(i, e):
             b, u, h = order[i]
@@ -228,21 +233,37 @@ def tile_list_coil_trust_weighting_kernel(
 
         def mask(i):
             open_pair(i)
+            squares = trust[i] if i < last else in_slot([P, 2, HALF], F32, "squares", 18, 6)
             for e in range(2):
                 product(i, e)
-                leave_bank(ACT.Square, trust[i], i, e)
-            leave_bank(ACT.Identity, res[i], i, 0)
-            nc.scalar.activation(trust[i][:], trust[i][:], ACT.Exp, scale=-1.0)
+                leave_bank(ACT.Square, squares, i, e)
+            if i < last - 1:
+                leave_bank(ACT.Identity, res[i], i, 0)
+            nc.scalar.activation(trust[i][:], squares[:], ACT.Exp, scale=-1.0)
+            if i == last:
+                make_z(1, 0)
             gate(i, 0)
-            if i < len(order) - 1:
+            if i < last:
                 z_pair(i - 1)
             gate(i, 1)
 
         def z_pair(i):
             b, u, h = order[i]
+            if i >= last - 1:
+                leave_bank(ACT.Identity, res[i], i, 0)
             leave_bank(ACT.Identity, res[i], i, 1)
             if u == 0:
-                zpairs[b, h] = in_slot([P, 2, HALF, 2], BF16, "zpairs%d%d" % (b, h), 14, zslot[b, h])
+                zpairs[b, h] = in_slot([P, 2, HALF, 2], BF16, "zpairs%d%d" % (b, h), *zslot[b, h])
+            if i >= last - 1:
+                positive = gated[i]
+                nc.scalar.activation(positive[:], positive[:], ACT.Relu)
+                nc.gpsimd.tensor_tensor(
+                    zpairs[b, h][:, u],
+                    positive[:].rearrange("p e c -> p c e"),
+                    res[i][:].rearrange("p e c -> p c e"),
+                    ALU.mult,
+                )
+                return
             nc.vector.scalar_tensor_tensor(
                 zpairs[b, h][:, u],
                 gated[i][:].rearrange("p e c -> p c e"),
@@ -259,13 +280,13 @@ def tile_list_coil_trust_weighting_kernel(
             )
 
         def make_z(b, h):
-            if (b, h) == (1, 1):
-                zbf = in_slot([P, PACK * HALF], BF16, "zbf11", 13)
+            if h == 1:
+                zbf = in_slot([P, PACK * HALF], BF16, "zbf%d1" % b, (20, 13)[b])
             else:
-                zbf = grouped("zbf")
+                zbf = grouped("zbf%d0" % b, 1 + b)
             weave(zpairs[b, h], zbf)
-            if (b, h) == (1, 1):
-                zc[b, h] = in_slot([P, HALF], U32, "zc_last", 1, 2)
+            if (b, h) == (0, 1):
+                zc[b, h] = in_slot([P, HALF], U32, "zc01", 20, 2)
             else:
                 zc[b, h] = keep.tile([P, HALF], U32, name="zc%d%d" % (b, h), align_bytes=64)
             zs[b, h] = keep.tile([P, HALF], U8, name="zs%d%d" % (b, h), align_bytes=64)
@@ -278,7 +299,7 @@ def tile_list_coil_trust_weighting_kernel(
             gain[t] = in_slot([P, S], F32, "gain%d" % t, 4, 2 * t)
             nc.sync.dma_start(gain[t][:], wgo_v[:, t, :].partition_broadcast(4))
 
-        def make_step(t, h, step):
+        def make_step(t, h, step, with_gain=False):
             acc2 = psum.tile([P, HALF], F32, name="acc2", tag="acc", bufs=8)
             for b in range(2):
                 nc.tensor.matmul_mx(
@@ -290,12 +311,14 @@ def tile_list_coil_trust_weighting_kernel(
                     start=(b == 0),
                     stop=(b == 1),
                 )
-            nc.scalar.copy(step, acc2[:])
+            if with_gain:
+                nc.vector.tensor_tensor(step, acc2[:], gain[t][:, HALF * h : HALF * (h + 1)], ALU.mult)
+            else:
+                nc.scalar.copy(step, acc2[:])
 
         def place_step(t, lo, hi, step):
             nc.vector.tensor_tensor(pages[t][:].indirect(place[:, lo // 16 : hi // 16]), step, gain[t][:, lo:hi], ALU.mult)
 
-        last = len(order) - 1
         quant_w1(0, 1)
         first_pairs()
         round_w1(nc.vector.tensor_copy, 1, 1)
@@ -307,6 +330,8 @@ def tile_list_coil_trust_weighting_kernel(
                     load_gain(t)
             if i == 4:
                 make_z(0, 0)
+            if i == 6:
+                make_z(0, 1)
             if i == 3:
                 nc.vector.tensor_copy(
                     w2w[:].rearrange("p a (t m) -> p a m t", t=PACK),
@@ -315,18 +340,18 @@ def tile_list_coil_trust_weighting_kernel(
                 nc.vector.tensor_copy(
                     w2sc[:].rearrange("p (t m) -> p m t", t=PACK), w2sc_raw[:].rearrange("p (m t) -> p m t", t=PACK)
                 )
-        make_z(1, 0)
         z_pair(last - 1)
         z_pair(last)
-        make_z(0, 1)
-        first_step = in_slot([P, HALF], F32, "first_step", 1, 2)
-        make_step(0, 0, first_step[:])
-        place_step(0, 0, HALF, first_step[:])
+        gained = [in_slot([P, HALF], F32, "gained%d" % t, 1, 2 + t) for t in range(2)]
+        for t in range(2):
+            make_step(t, 0, gained[t][:], True)
+        for t in range(2):
+            nc.vector.tensor_copy(pages[t][:].indirect(half_list(place, 0)), gained[t][:])
         make_z(1, 1)
         clear_page(3, 13)
         steps = {t: in_slot([P, S], F32, "step%d" % t, 6, 2 * t) for t in (0, 1, 3)}
-        steps[2] = in_slot([P, S], F32, "step2", 14, zslot[1, 1])
-        for t in range(1, PACK):
+        steps[2] = in_slot([P, S], F32, "step2", *zslot[1, 1])
+        for t in range(2, PACK):
             make_step(t, 0, steps[t][:, :HALF])
             if t < 3:
                 place_step(t, 0, HALF, steps[t][:, :HALF])

@@ -49,18 +49,19 @@ def tile_list_coil_trust_weighting_kernel(
 
         pick = keep.tile([P, S // 16], U16, name="pick")
         place = keep.tile([P, S // 16], U16, name="place")
-        tsc = [in_slot([P, T], U8, "tsc%d" % a, 18, a) for a in range(2)]
+        tsc = in_slot([P, T], U8, "tsc", 18, 1)
+        moved = keep.tile([P, S], U8, name="moved", align_bytes=64)
         w2sc_raw = keep.tile([P, N], U8, name="w2sc_raw", align_bytes=64)
-        w2sc = keep.tile([P, N], U8, name="w2sc", align_bytes=64)
+        w2sc = in_slot([P, N], U8, "w2sc", 7, 2)
         w2raw = keep.tile([P, 2, N], I32, name="w2raw", align_bytes=64)
-        w2w = keep.tile([P, 2, N], I32, name="w2w", align_bytes=64)
+        w2w = in_slot([P, 2, N], I32, "w2w", 7)
         tgt = keep.tile([P, 2, PACK], F32, name="tgt")
         ntgt = keep.tile([P, 2 * PACK], F32, name="ntgt")
         ycodes = keep.tile([P, T2], U32, name="ycodes", align_bytes=64)
         yscales = keep.tile([P, T2], U8, name="yscales", align_bytes=64)
 
-        nc.gpsimd.memset(tsc[0][:].bitcast(I32), 0)
-        nc.vector.memset(tsc[1][:].bitcast(I32), 0)
+        nc.vector.memset(tsc[:].bitcast(I32), 0)
+        nc.vector.memset(moved[:].bitcast(I32), 0)
         nc.vector.memset(w2sc_raw[:].bitcast(I32), 0)
         pages = {t: in_slot([P, T2], F32, "page%d" % t, 10 + t) for t in range(3)}
         for t in range(3):
@@ -74,11 +75,10 @@ def tile_list_coil_trust_weighting_kernel(
             tabw[a] = in_slot([P, T], U32, "tabw%d" % a, a)
             nc.sync.dma_start(tabw[a][:].bitcast(I32), tab_words[a].rearrange("p t i -> p (t i)").bitcast(I32))
 
-        def load_scales(a):
-            for q in range(4):
-                nc.sync.dma_start(
-                    tsc[a][32 * q : 32 * q + 4, :].bitcast(I32), tab_scales[a, 4 * q : 4 * q + 4, :].bitcast(I32)
-                )
+        def load_scales():
+            rows = tab_scales.rearrange("a (q r) t -> r q a t", r=4)
+            for r in range(4):
+                nc.sync.dma_start(tsc[r:P:16, :].bitcast(I32), rows[r].bitcast(I32))
 
         def load_w1(a, b, lo=0, hi=P):
             tile = in_slot([P, PACK, PACK * (hi - lo)], F32, "w1raw%d%d%d" % (a, b, lo), 2 + 2 * b + a, lo // 32)
@@ -92,14 +92,13 @@ def tile_list_coil_trust_weighting_kernel(
             margins[b, t] = in_slot([P, T], F32, "margins%d%d" % (b, t), 6 + t if b == 0 else (1, 2, 3, 13)[t])
             nc.sync.dma_start(margins[b, t][:], sT_v[b, t])
 
-        nc.sync.dma_start(pick[:], offs)
-        nc.sync.dma_start(tgt[:], target.rearrange("(b p t) -> p b t", b=2, t=PACK))
-        load_scales(0)
         load_w1(0, 0)
-        nc.sync.dma_start(place[:], offs2)
-        load_scales(1)
+        nc.sync.dma_start(pick[:], offs)
+        load_scales()
         load_w1(1, 0, 0, SPLIT)
         load_tab(0)
+        nc.sync.dma_start(tgt[:], target.rearrange("(b p t) -> p b t", b=2, t=PACK))
+        nc.sync.dma_start(place[:], offs2)
         load_w1(1, 0, SPLIT, P)
         load_tab(1)
         load_w1(0, 1)
@@ -116,8 +115,6 @@ def tile_list_coil_trust_weighting_kernel(
         for t in range(PACK):
             load_margins(1, t)
 
-        nc.scalar.mul(ntgt[:], tgt[:].rearrange("p b t -> p (b t)"), -1.0)
-
         vw = {}
         vsc = {}
 
@@ -125,9 +122,10 @@ def tile_list_coil_trust_weighting_kernel(
             vw[a, h] = keep.tile([P, HALF], U32, name="vw%d%d" % (a, h), align_bytes=64)
             nc.vector.tensor_copy(vw[a, h][:], tabw[a][:].indirect(half_list(pick, h)))
 
-        def gather_scales(a):
-            vsc[a] = keep.tile([P, S], U8, name="vsc%d" % a, align_bytes=64)
-            nc.vector.tensor_copy(vsc[a][:], tsc[a][:].indirect(pick[:]))
+        def gather_scales():
+            vsc[0] = keep.tile([P, S], U8, name="vsc", align_bytes=64)
+            nc.vector.tensor_copy(vsc[0][:], tsc[:].indirect(pick[:]))
+            vsc[1] = moved
 
         w1bf = {}
         w1c = {}
@@ -135,7 +133,10 @@ def tile_list_coil_trust_weighting_kernel(
 
         def round_w1(copy, a, b, lo=0, hi=P, piece=0):
             if lo == 0:
-                w1bf[a, b] = grouped("w1bf%d%d" % (a, b), (2 * b + a) % 3)
+                if a + b < 2:
+                    w1bf[a, b] = grouped("w1bf%d%d" % (a, b), 2 * b + a)
+                else:
+                    w1bf[a, b] = in_slot([P, PACK * HALF], BF16, "w1bf11", 16, 2)
                 if b == 0:
                     w1c[a, b] = in_slot([P, KP], U32, "w1c%d0" % a, *((18, 1), (0, 0))[a])
                 else:
@@ -155,14 +156,15 @@ def tile_list_coil_trust_weighting_kernel(
             for c in range(T2 // CHUNK):
                 nc.gpsimd.memset(pages[t][:, CHUNK * c : CHUNK * (c + 1)], 0.0)
 
-        for a in range(2):
-            gather_scales(a)
+        gather_scales()
         round_w1(nc.scalar.copy, 0, 0)
+        nc.scalar.dma_start(moved[: P - 16, :].bitcast(I32), vsc[0][16:, :].bitcast(I32))
         quant_w1(0, 0)
         for h in range(2):
             gather_words(0, h)
         round_w1(nc.scalar.copy, 1, 0, 0, SPLIT)
         round_w1(nc.scalar.copy, 1, 0, SPLIT, P, SPLIT)
+        nc.scalar.mul(ntgt[:], tgt[:].rearrange("p b t -> p (b t)"), -1.0)
         quant_w1(1, 0)
         for h in range(2):
             gather_words(1, h)
@@ -349,7 +351,7 @@ def tile_list_coil_trust_weighting_kernel(
             nc.vector.tensor_copy(pages[t][:].indirect(half_list(place, 0)), gained[t][:])
         make_z(1, 1)
         clear_page(3, 13)
-        steps = {t: in_slot([P, S], F32, "step%d" % t, 6, 2 * t) for t in (0, 1, 3)}
+        steps = {t: in_slot([P, S], F32, "step%d" % t, *((6, 0), (6, 2), None, (16, 4))[t]) for t in (0, 1, 3)}
         steps[2] = in_slot([P, S], F32, "step2", *zslot[1, 1])
         for t in range(2, PACK):
             make_step(t, 0, steps[t][:, :HALF])

@@ -171,13 +171,14 @@ def tile_list_coil_trust_weighting_kernel(
         round_w1(nc.vector.tensor_copy, 0, 1)
 
         order = [(0, 0, 0), (0, 0, 1), (0, 1, 0), (0, 1, 1), (1, 0, 0), (1, 1, 0), (1, 0, 1), (1, 1, 1)]
-        zslot = {(0, 0): (14, 0), (0, 1): (14, 2), (1, 0): (14, 4), (1, 1): (16, 0)}
+        zslot = {(0, 0): (14, 0), (0, 1): (14, 2), (1, 0): (14, 4)}
         last = len(order) - 1
         res = {}
         acc = {}
         trust = {}
         gated = {}
         zpairs = {}
+        zbf = {}
         zc = {}
         zs = {}
 
@@ -205,7 +206,7 @@ def tile_list_coil_trust_weighting_kernel(
             if i < last - 1:
                 res[i] = in_slot([P, 2, HALF], F32, "res%d" % i, 20, 2 * (i % 4))
             else:
-                res[i] = in_slot([P, 2, HALF], F32, "res%d" % i, 3, 2 * (i % 2))
+                res[i] = in_slot([P, 2, HALF], F32, "res%d" % i, 2 + i % 2, 2)
             trust[i] = in_slot([P, 2, HALF], F32, "trust%d" % i, 16, 2 * ((i + 1) % 4))
             if i == 1:
                 gated[i] = in_slot([P, 2, HALF], F32, "gated1", 0, 2)
@@ -231,7 +232,6 @@ def tile_list_coil_trust_weighting_kernel(
                     gate(i, e)
             leave_bank(ACT.Identity, res[0], 0, 0)
             z_pair(0)
-            leave_bank(ACT.Identity, res[1], 1, 0)
 
         def mask(i):
             open_pair(i)
@@ -251,21 +251,23 @@ def tile_list_coil_trust_weighting_kernel(
 
         def z_pair(i):
             b, u, h = order[i]
-            if i >= last - 1:
+            if i == 1 or i >= last - 1:
                 leave_bank(ACT.Identity, res[i], i, 0)
             leave_bank(ACT.Identity, res[i], i, 1)
-            if u == 0:
-                zpairs[b, h] = in_slot([P, 2, HALF, 2], BF16, "zpairs%d%d" % (b, h), *zslot[b, h])
             if i >= last - 1:
+                if u == 0:
+                    zbf[b, h] = in_slot([P, PACK * HALF], BF16, "zbf11", 13)
                 positive = gated[i]
                 nc.scalar.activation(positive[:], positive[:], ACT.Relu)
                 nc.gpsimd.tensor_tensor(
-                    zpairs[b, h][:, u],
+                    zbf[b, h][:].rearrange("p (c u e) -> p u c e", u=2, e=2)[:, u],
                     positive[:].rearrange("p e c -> p c e"),
                     res[i][:].rearrange("p e c -> p c e"),
                     ALU.mult,
                 )
                 return
+            if u == 0:
+                zpairs[b, h] = in_slot([P, 2, HALF, 2], BF16, "zpairs%d%d" % (b, h), *zslot[b, h])
             nc.vector.scalar_tensor_tensor(
                 zpairs[b, h][:, u],
                 gated[i][:].rearrange("p e c -> p c e"),
@@ -282,17 +284,18 @@ def tile_list_coil_trust_weighting_kernel(
             )
 
         def make_z(b, h):
-            if h == 1:
-                zbf = in_slot([P, PACK * HALF], BF16, "zbf%d1" % b, (20, 13)[b])
-            else:
-                zbf = grouped("zbf%d0" % b, 1 + b)
-            weave(zpairs[b, h], zbf)
+            if h == 0:
+                zbf[b, h] = grouped("zbf%d0" % b, 1 + b)
+            elif b == 0:
+                zbf[b, h] = in_slot([P, PACK * HALF], BF16, "zbf01", 20)
+            if (b, h) in zpairs:
+                weave(zpairs[b, h], zbf[b, h])
             if (b, h) == (0, 1):
                 zc[b, h] = in_slot([P, HALF], U32, "zc01", 20, 2)
             else:
                 zc[b, h] = keep.tile([P, HALF], U32, name="zc%d%d" % (b, h), align_bytes=64)
             zs[b, h] = keep.tile([P, HALF], U8, name="zs%d%d" % (b, h), align_bytes=64)
-            nc.vector.quantize_mx(out=zc[b, h][:].bitcast(E4M3), scales=zs[b, h][:], in_=zbf[:])
+            nc.vector.quantize_mx(out=zc[b, h][:].bitcast(E4M3), scales=zs[b, h][:], in_=zbf[b, h][:])
 
         gain = {}
         wgo_v = wgo.rearrange("(r t) s -> r t s", t=PACK)
@@ -352,7 +355,7 @@ def tile_list_coil_trust_weighting_kernel(
         make_z(1, 1)
         clear_page(3, 13)
         steps = {t: in_slot([P, S], F32, "step%d" % t, *((6, 0), (6, 2), None, (16, 4))[t]) for t in (0, 1, 3)}
-        steps[2] = in_slot([P, S], F32, "step2", *zslot[1, 1])
+        steps[2] = in_slot([P, S], F32, "step2", *zslot[1, 0])
         for t in range(2, PACK):
             make_step(t, 0, steps[t][:, :HALF])
             if t < 3:

@@ -27,6 +27,9 @@ QUARTER = SLOT // 4
 SPLIT = 64
 EDGES = (0, 512, 1024, 1536, 1792, 2048)
 ON_VECTOR = 2
+RUN = 4
+EARLY = 256
+SPLIT_PAIRS = (0, 1, 5)
 
 
 def tile_list_coil_trust_weighting_kernel(
@@ -52,9 +55,9 @@ def tile_list_coil_trust_weighting_kernel(
         tsc = in_slot([P, T], U8, "tsc", 18, 1)
         moved = keep.tile([P, S], U8, name="moved", align_bytes=64)
         w2sc_raw = keep.tile([P, N], U8, name="w2sc_raw", align_bytes=64)
-        w2sc = in_slot([P, N], U8, "w2sc", 7, 2)
-        w2raw = keep.tile([P, 2, N], I32, name="w2raw", align_bytes=64)
-        w2w = in_slot([P, 2, N], I32, "w2w", 7)
+        w2sc = in_slot([P, N], U8, "w2sc", 16)
+        w2raw = in_slot([P, 2, N], I32, "w2raw", 4)
+        w2w = in_slot([P, 2, N], I32, "w2w", 17)
         tgt = keep.tile([P, 2, PACK], F32, name="tgt")
         ntgt = keep.tile([P, 2 * PACK], F32, name="ntgt")
         ycodes = keep.tile([P, T2], U32, name="ycodes", align_bytes=64)
@@ -89,7 +92,7 @@ def tile_list_coil_trust_weighting_kernel(
         sT_v = sT.rearrange("(b p t) c -> b t p c", b=2, t=PACK)
 
         def load_margins(b, t):
-            margins[b, t] = in_slot([P, T], F32, "margins%d%d" % (b, t), 6 + t if b == 0 else (1, 2, 3, 13)[t])
+            margins[b, t] = in_slot([P, T], F32, "margins%d%d" % (b, t), 6 + t if b == 0 else (13, 2, 3, 1)[t])
             nc.sync.dma_start(margins[b, t][:], sT_v[b, t])
 
         load_w1(0, 0)
@@ -107,13 +110,13 @@ def tile_list_coil_trust_weighting_kernel(
         load_w1(1, 1)
         load_margins(0, 2)
         load_margins(0, 3)
+        for t in range(PACK):
+            load_margins(1, t)
         nc.sync.dma_start(w2raw[:], w2_words.rearrange("a p c i -> p a (c i)").bitcast(I32))
         for q in range(4):
             nc.sync.dma_start(
                 w2sc_raw[32 * q : 32 * q + 8, :].bitcast(I32), w2_scales[:, 4 * q : 4 * q + 4, :].bitcast(I32)
             )
-        for t in range(PACK):
-            load_margins(1, t)
 
         vw = {}
         vsc = {}
@@ -136,11 +139,13 @@ def tile_list_coil_trust_weighting_kernel(
                 if a + b < 2:
                     w1bf[a, b] = grouped("w1bf%d%d" % (a, b), 2 * b + a)
                 else:
-                    w1bf[a, b] = in_slot([P, PACK * HALF], BF16, "w1bf11", 16, 2)
+                    w1bf[a, b] = in_slot([P, PACK * HALF], BF16, "w1bf11", 16, 6)
                 if b == 0:
                     w1c[a, b] = in_slot([P, KP], U32, "w1c%d0" % a, *((18, 1), (0, 0))[a])
+                elif a == 0:
+                    w1c[a, b] = keep.tile([P, KP], U32, name="w1c01", align_bytes=64)
                 else:
-                    w1c[a, b] = keep.tile([P, KP], U32, name="w1c%d%d" % (a, b), align_bytes=64)
+                    w1c[a, b] = keep.tile([P, KP], U32, name="w1c11", align_bytes=64)
                 w1s[a, b] = keep.tile([P, KP], U8, name="w1s%d%d" % (a, b), align_bytes=64)
             dst = w1bf[a, b][:].rearrange("p (u e m j) -> p u m j e", u=2, e=2, j=PACK)
             src = w1raw[a, b, piece][:].rearrange("p j (m u e) -> p u m j e", u=2, e=2)
@@ -171,21 +176,25 @@ def tile_list_coil_trust_weighting_kernel(
         round_w1(nc.vector.tensor_copy, 0, 1)
 
         order = [(0, 0, 0), (0, 0, 1), (0, 1, 0), (0, 1, 1), (1, 0, 0), (1, 1, 0), (1, 0, 1), (1, 1, 1)]
-        zslot = {(0, 0): (14, 0), (0, 1): (14, 2), (1, 0): (14, 4)}
         last = len(order) - 1
         res = {}
         acc = {}
         trust = {}
+        wide = {}
         gated = {}
         zpairs = {}
-        zbf = {}
+        late_res = {}
+        late_gated = {}
         zc = {}
         zs = {}
+
+        def bank(n):
+            return psum.tile([P, HALF], F32, name="bank%d" % n, tag="bank%d" % n, bufs=1)
 
         def product(i, e):
             b, u, h = order[i]
             t = 2 * u + e
-            acc[i, e] = psum.tile([P, HALF], F32, name="acc", tag="acc", bufs=8)
+            acc[i, e] = bank(len(acc) % 8)
             for a in range(2):
                 nc.tensor.matmul_mx(
                     out=acc[i, e][:],
@@ -197,29 +206,48 @@ def tile_list_coil_trust_weighting_kernel(
                     stop=(a == 1),
                 )
 
-        def leave_bank(func, tile, i, e):
+        def leave_bank(func, dst, i, e):
             b, u, h = order[i]
             column = PACK * b + 2 * u + e
-            nc.scalar.activation(tile[:, e, :], acc[i, e][:], func, bias=ntgt[:, column : column + 1])
+            nc.scalar.activation(dst, acc[i, e][:], func, bias=ntgt[:, column : column + 1])
+
+        def residual(i, e):
+            leave_bank(ACT.Identity, res[i][:, e, :], i, e)
+
+        def cell(n, half=0):
+            return 16, 2 * n + half
+
+        held = {6: (cell(2), cell(0, 1)), 7: ((21, 2), (8, 3))}
 
         def open_pair(i):
-            if i < last - 1:
-                res[i] = in_slot([P, 2, HALF], F32, "res%d" % i, 20, 2 * (i % 4))
+            b, u, h = order[i]
+            home = (i + 3) % 4
+            if i in held:
+                trust[i] = [in_slot([P, HALF], F32, "trust%d%d" % (i, e), *held[i][e])[:] for e in range(2)]
+            elif i in SPLIT_PAIRS:
+                trust[i] = [in_slot([P, HALF], F32, "trust%d%d" % (i, e), *cell(home, e))[:] for e in range(2)]
             else:
-                res[i] = in_slot([P, 2, HALF], F32, "res%d" % i, 2 + i % 2, 2)
-            trust[i] = in_slot([P, 2, HALF], F32, "trust%d" % i, 16, 2 * ((i + 1) % 4))
-            if i == 1:
-                gated[i] = in_slot([P, 2, HALF], F32, "gated1", 0, 2)
-            elif i < last:
-                gated[i] = in_slot([P, 2, HALF], F32, "gated%d" % i, 16, 2 * (i % 4))
-            else:
-                gated[i] = in_slot([P, 2, HALF], F32, "gated%d" % i, *zslot[1, 0])
+                wide[i] = in_slot([P, 2 * HALF], F32, "trust%d" % i, *cell(home))
+                trust[i] = [wide[i][:, HALF * e : HALF * (e + 1)] for e in range(2)]
+            if h == 0:
+                res[i] = in_slot([P, 2, HALF], F32, "res%d" % i, 20, 2 * u)[:]
+                gated[i] = in_slot([P, 2, HALF], F32, "gated%d" % i, 21, 2 * u)[:]
+                return
+            if u == 0:
+                late_res[b] = in_slot([P, PACK, HALF], F32, "late_res%d" % b, *((23, 0), (2, 2))[b])
+                late_gated[b] = in_slot([P, PACK, HALF], F32, "late_gated%d" % b, (22, 15)[b])
+            res[i] = late_res[b][:, 2 * u : 2 * u + 2, :]
+            gated[i] = late_gated[b][:, 2 * u : 2 * u + 2, :]
 
         def gate(i, e):
             b, u, h = order[i]
             nc.vector.tensor_tensor(
-                gated[i][:, e, :], margins[b, 2 * u + e][:].indirect(half_list(pick, h)), trust[i][:, e, :], ALU.mult
+                gated[i][:, e, :], margins[b, 2 * u + e][:].indirect(half_list(pick, h)), trust[i][e], ALU.mult
             )
+
+        def weigh(i, e, squares):
+            nc.scalar.activation(trust[i][e], squares, ACT.Exp, scale=-1.0)
+            gate(i, e)
 
         def first_pairs():
             for i in range(2):
@@ -227,52 +255,56 @@ def tile_list_coil_trust_weighting_kernel(
             for e in range(2):
                 for i in range(2):
                     product(i, e)
-                    leave_bank(ACT.Square, trust[i], i, e)
-                    nc.scalar.activation(trust[i][:, e, :], trust[i][:, e, :], ACT.Exp, scale=-1.0)
-                    gate(i, e)
-            leave_bank(ACT.Identity, res[0], 0, 0)
-            z_pair(0)
+                    leave_bank(ACT.Square, trust[i][e], i, e)
+                    weigh(i, e, trust[i][e])
 
-        def mask(i):
+        def mask(i, squares=None):
             open_pair(i)
-            squares = trust[i] if i < last else in_slot([P, 2, HALF], F32, "squares", 18, 6)
             for e in range(2):
                 product(i, e)
-                leave_bank(ACT.Square, squares, i, e)
-            if i < last - 1:
-                leave_bank(ACT.Identity, res[i], i, 0)
-            nc.scalar.activation(trust[i][:], squares[:], ACT.Exp, scale=-1.0)
-            if i == last:
-                make_z(1, 0)
-            gate(i, 0)
-            if i < last:
-                z_pair(i - 1)
-            gate(i, 1)
+                leave_bank(ACT.Square, trust[i][e] if squares is None else squares[:, HALF * e : HALF * (e + 1)], i, e)
+            if i in SPLIT_PAIRS:
+                for e in range(2):
+                    weigh(i, e, trust[i][e])
+                return
+            nc.scalar.activation(wide[i][:], wide[i][:] if squares is None else squares, ACT.Exp, scale=-1.0)
+            for e in range(2):
+                gate(i, e)
 
-        def z_pair(i):
+        def square(i, e, place):
+            squares = in_slot([P, HALF], F32, "squares%d%d" % (i, e), *place)
+            product(i, e)
+            leave_bank(ACT.Square, squares[:], i, e)
+            return squares[:]
+
+        def last_masks():
+            open_pair(6)
+            product(6, 0)
+            leave_bank(ACT.Square, trust[6][0], 6, 0)
+            weigh(6, 0, trust[6][0])
+            finish_pair(5)
+            weigh(6, 1, square(6, 1, cell(2, 1)))
+            sort_w2()
+            load_gain(2)
+            open_pair(7)
+            squares = [square(7, 0, (18, 6)), square(7, 1, cell(1, 1))]
+            weigh(7, 0, squares[0])
+            make_z(1)
+            weigh(7, 1, squares[1])
+
+        def finish_pair(i):
             b, u, h = order[i]
-            if i == 1 or i >= last - 1:
-                leave_bank(ACT.Identity, res[i], i, 0)
-            leave_bank(ACT.Identity, res[i], i, 1)
-            if i >= last - 1:
-                if u == 0:
-                    zbf[b, h] = in_slot([P, PACK * HALF], BF16, "zbf11", 13)
-                positive = gated[i]
-                nc.scalar.activation(positive[:], positive[:], ACT.Relu)
-                nc.gpsimd.tensor_tensor(
-                    zbf[b, h][:].rearrange("p (c u e) -> p u c e", u=2, e=2)[:, u],
-                    positive[:].rearrange("p e c -> p c e"),
-                    res[i][:].rearrange("p e c -> p c e"),
-                    ALU.mult,
-                )
+            for e in range(2):
+                residual(i, e)
+            if h == 1:
                 return
             if u == 0:
-                zpairs[b, h] = in_slot([P, 2, HALF, 2], BF16, "zpairs%d%d" % (b, h), *zslot[b, h])
+                zpairs[b] = in_slot([P, 2, HALF, 2], BF16, "zpairs%d" % b, *((14, 0), (8, 3))[b])
             nc.vector.scalar_tensor_tensor(
-                zpairs[b, h][:, u],
-                gated[i][:].rearrange("p e c -> p c e"),
+                zpairs[b][:, u],
+                gated[i].rearrange("p e c -> p c e"),
                 0.0,
-                res[i][:].rearrange("p e c -> p c e"),
+                res[i].rearrange("p e c -> p c e"),
                 ALU.max,
                 ALU.mult,
             )
@@ -283,85 +315,117 @@ def tile_list_coil_trust_weighting_kernel(
                 pair_tile[:].rearrange("p u c e -> p u (c e)").bitcast(F32).rearrange("p u c -> p c u"),
             )
 
-        def make_z(b, h):
-            if h == 0:
-                zbf[b, h] = grouped("zbf%d0" % b, 1 + b)
-            elif b == 0:
-                zbf[b, h] = in_slot([P, PACK * HALF], BF16, "zbf01", 20)
-            if (b, h) in zpairs:
-                weave(zpairs[b, h], zbf[b, h])
-            if (b, h) == (0, 1):
-                zc[b, h] = in_slot([P, HALF], U32, "zc01", 20, 2)
-            else:
-                zc[b, h] = keep.tile([P, HALF], U32, name="zc%d%d" % (b, h), align_bytes=64)
-            zs[b, h] = keep.tile([P, HALF], U8, name="zs%d%d" % (b, h), align_bytes=64)
-            nc.vector.quantize_mx(out=zc[b, h][:].bitcast(E4M3), scales=zs[b, h][:], in_=zbf[b, h][:])
+        def make_z(b):
+            zbf = grouped("zbf%d" % b, 1 + b)
+            weave(zpairs[b], zbf)
+            codes = in_slot([P, HALF], U32, "zc%d" % b, *(cell(3), (14, 2))[b])
+            scales = keep.tile([P, HALF], U8, name="zs%d" % b, align_bytes=64)
+            nc.vector.quantize_mx(out=codes[:].bitcast(E4M3), scales=scales[:], in_=zbf[:])
+            zc[b, 0] = codes[:]
+            zs[b, 0] = scales[:]
+
+        def late_products():
+            zbf = in_slot([P, 2, PACK * HALF], BF16, "late_zbf", 1)
+            for b in range(2):
+                if b == 1:
+                    for i in (last - 1, last):
+                        for e in range(2):
+                            residual(i, e)
+                positive = late_gated[b] if b == 1 else in_slot([P, PACK, HALF], F32, "positive", 9)
+                nc.scalar.activation(positive[:], late_gated[b][:], ACT.Relu)
+                nc.gpsimd.tensor_tensor(
+                    zbf[:, b, :].rearrange("p (c i t) -> p c t i", i=RUN, t=PACK),
+                    positive[:].rearrange("p t (c i) -> p c t i", i=RUN),
+                    late_res[b][:].rearrange("p t (c i) -> p c t i", i=RUN),
+                    ALU.mult,
+                )
+            return zbf
+
+        def make_late_z(zbf):
+            codes = in_slot([P, S], U32, "late_zc", 13, 2)
+            scales = keep.tile([P, S], U8, name="late_zs", align_bytes=64)
+            for b in range(2):
+                zc[b, 1] = codes[:, HALF * b : HALF * (b + 1)]
+                zs[b, 1] = scales[:, HALF * b : HALF * (b + 1)]
+                nc.vector.quantize_mx(out=zc[b, 1].bitcast(E4M3), scales=zs[b, 1], in_=zbf[:, b, :])
 
         gain = {}
         wgo_v = wgo.rearrange("(r t) s -> r t s", t=PACK)
 
         def load_gain(t):
-            gain[t] = in_slot([P, S], F32, "gain%d" % t, 4, 2 * t)
+            gain[t] = in_slot([P, S], F32, "gain%d" % t, *((5, 0), (5, 2), (4, 0), (4, 2))[t])
             nc.sync.dma_start(gain[t][:], wgo_v[:, t, :].partition_broadcast(4))
 
-        def make_step(t, h, step, with_gain=False):
-            acc2 = psum.tile([P, HALF], F32, name="acc2", tag="acc", bufs=8)
-            for b in range(2):
+        def make_step(t, h):
+            acc2 = bank(t if h == 0 else (PACK, PACK, 2, 2)[t])
+            passes = (1, 0) if h == 1 and t > 0 else (0, 1)
+            for b in passes:
                 nc.tensor.matmul_mx(
                     out=acc2[:],
                     lhsT=w2w[:, b, P * t : P * (t + 1)].bitcast(E4M3),
                     lhsT_scale=w2sc[4 * b :, P * t : P * (t + 1)],
-                    rhs=zc[b, h][:].bitcast(E4M3),
-                    rhs_scale=zs[b, h][:],
-                    start=(b == 0),
-                    stop=(b == 1),
+                    rhs=zc[b, h].bitcast(E4M3),
+                    rhs_scale=zs[b, h],
+                    start=(b == passes[0]),
+                    stop=(b == passes[1]),
                 )
-            if with_gain:
-                nc.vector.tensor_tensor(step, acc2[:], gain[t][:, HALF * h : HALF * (h + 1)], ALU.mult)
-            else:
-                nc.scalar.copy(step, acc2[:])
+            return acc2
 
         def place_step(t, lo, hi, step):
             nc.vector.tensor_tensor(pages[t][:].indirect(place[:, lo // 16 : hi // 16]), step, gain[t][:, lo:hi], ALU.mult)
 
+        def sort_w2():
+            nc.vector.tensor_copy(
+                w2w[:].rearrange("p a (t m) -> p a m t", t=PACK),
+                w2raw[:].rearrange("p a (m t) -> p a m t", t=PACK),
+            )
+            nc.vector.tensor_copy(
+                w2sc[:].rearrange("p (t m) -> p m t", t=PACK), w2sc_raw[:].rearrange("p (m t) -> p m t", t=PACK)
+            )
+
         quant_w1(0, 1)
         first_pairs()
+        finish_pair(0)
         round_w1(nc.vector.tensor_copy, 1, 1)
-        for i in range(2, len(order)):
-            mask(i)
-            if i == 2:
-                quant_w1(1, 1)
-                for t in range(PACK):
-                    load_gain(t)
-            if i == 4:
-                make_z(0, 0)
-            if i == 6:
-                make_z(0, 1)
-            if i == 3:
-                nc.vector.tensor_copy(
-                    w2w[:].rearrange("p a (t m) -> p a m t", t=PACK),
-                    w2raw[:].rearrange("p a (m t) -> p a m t", t=PACK),
-                )
-                nc.vector.tensor_copy(
-                    w2sc[:].rearrange("p (t m) -> p m t", t=PACK), w2sc_raw[:].rearrange("p (m t) -> p m t", t=PACK)
-                )
-        z_pair(last - 1)
-        z_pair(last)
-        gained = [in_slot([P, HALF], F32, "gained%d" % t, 1, 2 + t) for t in range(2)]
-        for t in range(2):
-            make_step(t, 0, gained[t][:], True)
-        for t in range(2):
-            nc.vector.tensor_copy(pages[t][:].indirect(half_list(place, 0)), gained[t][:])
-        make_z(1, 1)
-        clear_page(3, 13)
-        steps = {t: in_slot([P, S], F32, "step%d" % t, *((6, 0), (6, 2), None, (16, 4))[t]) for t in (0, 1, 3)}
-        steps[2] = in_slot([P, S], F32, "step2", *zslot[1, 0])
-        for t in range(2, PACK):
-            make_step(t, 0, steps[t][:, :HALF])
-            if t < 3:
-                place_step(t, 0, HALF, steps[t][:, :HALF])
+        mask(2)
+        quant_w1(1, 1)
+        for t in (3, 0, 1):
+            load_gain(t)
+        finish_pair(1)
+        mask(3)
+        finish_pair(2)
+        finish_pair(3)
+        mask(4, grouped("squares4", 1)[:].bitcast(F32))
+        make_z(0)
+        finish_pair(4)
+        mask(5)
+        last_masks()
+        late_zbf = late_products()
+
+        steps = {t: in_slot([P, S], F32, "step%d" % t, *((6, 0), (6, 2), (15, 0), (7, 0))[t]) for t in range(PACK)}
+        widths = (HALF, HALF, EARLY)
+        gained = [in_slot([P, widths[t]], F32, "gained%d" % t, *((0, 2), (0, 3), (13, 0))[t]) for t in range(3)]
+        banks = [make_step(t, 0) for t in range(PACK)]
+
+        def apply_gain(t):
+            nc.vector.tensor_tensor(gained[t][:], banks[t][:, : widths[t]], gain[t][:, : widths[t]], ALU.mult)
+
+        def place_gained(t):
+            nc.vector.tensor_copy(pages[t][:].indirect(place[:, : widths[t] // 16]), gained[t][:])
+
+        apply_gain(0)
+        apply_gain(1)
+        place_gained(0)
+        apply_gain(2)
+        place_gained(1)
+        place_gained(2)
+        nc.scalar.copy(steps[2][:, EARLY:HALF], banks[2][:, EARLY:])
+        nc.scalar.copy(steps[3][:, :HALF], banks[3][:])
+        make_late_z(late_zbf)
+        clear_page(3, 1)
+        place_step(2, EARLY, HALF, steps[2][:, EARLY:HALF])
         for t in (0, 2, 1, 3):
-            make_step(t, 1, steps[t][:, HALF:])
+            nc.scalar.copy(steps[t][:, HALF:], make_step(t, 1)[:])
 
         out_v = out_0.rearrange("(p t) m -> p t m", t=PACK)
         chunks = [slice(lo, hi) for lo, hi in zip(EDGES, EDGES[1:])]

@@ -29,7 +29,6 @@ EDGES = (0, 512, 1024, 1536, 1792, 2048)
 ON_VECTOR = 2
 RUN = 4
 EARLY = 256
-SPLIT_PAIRS = (0, 1, 5)
 
 
 def tile_list_coil_trust_weighting_kernel(
@@ -41,8 +40,8 @@ def tile_list_coil_trust_weighting_kernel(
         slots = ctx.enter_context(tc.tile_pool(name="slots", bufs=1))
         psum = ctx.enter_context(tc.psum_pool(name="psum", bufs=1))
 
-        def in_slot(shape, dtype, name, slot, quarter=0):
-            return slots.tile(shape, dtype, name=name, align_bytes=64, offset=SLOT * slot + QUARTER * quarter)
+        def in_slot(shape, dtype, name, slot, quarter=0, extra=0):
+            return slots.tile(shape, dtype, name=name, align_bytes=64, offset=SLOT * slot + QUARTER * quarter + extra)
 
         def grouped(name, cell):
             return in_slot([P, PACK * HALF], BF16, name, 18, 2 + 2 * cell)
@@ -55,9 +54,9 @@ def tile_list_coil_trust_weighting_kernel(
         tsc = in_slot([P, T], U8, "tsc", 18, 1)
         moved = keep.tile([P, S], U8, name="moved", align_bytes=64)
         w2sc_raw = keep.tile([P, N], U8, name="w2sc_raw", align_bytes=64)
-        w2sc = in_slot([P, N], U8, "w2sc", 16)
+        w2sc = in_slot([P, N], U8, "w2sc", 17, 2, N)
         w2raw = in_slot([P, 2, N], I32, "w2raw", 4)
-        w2w = in_slot([P, 2, N], I32, "w2w", 17)
+        w2w = in_slot([P, 2, N], I32, "w2w", 17, 0, N)
         tgt = keep.tile([P, 2, PACK], F32, name="tgt")
         ntgt = keep.tile([P, 2 * PACK], F32, name="ntgt")
         ycodes = keep.tile([P, T2], U32, name="ycodes", align_bytes=64)
@@ -139,7 +138,7 @@ def tile_list_coil_trust_weighting_kernel(
                 if a + b < 2:
                     w1bf[a, b] = grouped("w1bf%d%d" % (a, b), 2 * b + a)
                 else:
-                    w1bf[a, b] = in_slot([P, PACK * HALF], BF16, "w1bf11", 16, 6)
+                    w1bf[a, b] = in_slot([P, PACK * HALF], BF16, "w1bf11", 16)
                 if b == 0:
                     w1c[a, b] = in_slot([P, KP], U32, "w1c%d0" % a, *((18, 1), (0, 0))[a])
                 elif a == 0:
@@ -179,10 +178,11 @@ def tile_list_coil_trust_weighting_kernel(
         last = len(order) - 1
         res = {}
         acc = {}
-        trust = {}
-        wide = {}
+        squares = {}
         gated = {}
         zpairs = {}
+        zbf = {}
+        positive = {}
         late_res = {}
         late_gated = {}
         zc = {}
@@ -191,10 +191,30 @@ def tile_list_coil_trust_weighting_kernel(
         def bank(n):
             return psum.tile([P, HALF], F32, name="bank%d" % n, tag="bank%d" % n, bufs=1)
 
-        def product(i, e):
+        def leave_bank(func, dst, i, e):
+            b, u, h = order[i]
+            column = PACK * b + 2 * u + e
+            nc.scalar.activation(dst, acc[i, e][:], func, bias=ntgt[:, column : column + 1])
+
+        def open_pair(i):
+            b, u, h = order[i]
+            if h == 0:
+                res[i] = in_slot([P, 2, HALF], F32, "res%d" % i, 20, 2 * u)[:]
+                gated[i] = in_slot([P, 2, HALF], F32, "gated%d" % i, 21, 2 * u)[:]
+                return
+            if b not in late_res:
+                late_res[b] = in_slot([P, PACK, HALF], F32, "late_res%d" % b, *((23, 0), (8, 1))[b])
+                late_gated[b] = in_slot([P, PACK, HALF], F32, "late_gated%d" % b, (22, 15)[b])
+            res[i] = late_res[b][:, 2 * u : 2 * u + 2, :]
+            gated[i] = late_gated[b][:, 2 * u : 2 * u + 2, :]
+
+        def square(i, e, place=None):
             b, u, h = order[i]
             t = 2 * u + e
-            acc[i, e] = bank(len(acc) % 8)
+            n = len(acc) % 8
+            if i not in res:
+                open_pair(i)
+            acc[i, e] = bank(n)
             for a in range(2):
                 nc.tensor.matmul_mx(
                     out=acc[i, e][:],
@@ -205,101 +225,30 @@ def tile_list_coil_trust_weighting_kernel(
                     start=(a == 0),
                     stop=(a == 1),
                 )
+            squares[i, e] = in_slot([P, HALF], F32, "squares%d%d" % (i, e), *(place or (16, n)))
+            leave_bank(ACT.Square, squares[i, e][:], i, e)
 
-        def leave_bank(func, dst, i, e):
+        def gate(i, e, place=None):
             b, u, h = order[i]
-            column = PACK * b + 2 * u + e
-            nc.scalar.activation(dst, acc[i, e][:], func, bias=ntgt[:, column : column + 1])
-
-        def residual(i, e):
-            leave_bank(ACT.Identity, res[i][:, e, :], i, e)
-
-        def cell(n, half=0):
-            return 16, 2 * n + half
-
-        held = {6: (cell(2), cell(0, 1)), 7: ((21, 2), (8, 3))}
-
-        def open_pair(i):
-            b, u, h = order[i]
-            home = (i + 3) % 4
-            if i in held:
-                trust[i] = [in_slot([P, HALF], F32, "trust%d%d" % (i, e), *held[i][e])[:] for e in range(2)]
-            elif i in SPLIT_PAIRS:
-                trust[i] = [in_slot([P, HALF], F32, "trust%d%d" % (i, e), *cell(home, e))[:] for e in range(2)]
-            else:
-                wide[i] = in_slot([P, 2 * HALF], F32, "trust%d" % i, *cell(home))
-                trust[i] = [wide[i][:, HALF * e : HALF * (e + 1)] for e in range(2)]
-            if h == 0:
-                res[i] = in_slot([P, 2, HALF], F32, "res%d" % i, 20, 2 * u)[:]
-                gated[i] = in_slot([P, 2, HALF], F32, "gated%d" % i, 21, 2 * u)[:]
-                return
-            if u == 0:
-                late_res[b] = in_slot([P, PACK, HALF], F32, "late_res%d" % b, *((23, 0), (2, 2))[b])
-                late_gated[b] = in_slot([P, PACK, HALF], F32, "late_gated%d" % b, (22, 15)[b])
-            res[i] = late_res[b][:, 2 * u : 2 * u + 2, :]
-            gated[i] = late_gated[b][:, 2 * u : 2 * u + 2, :]
-
-        def gate(i, e):
-            b, u, h = order[i]
+            trust = squares[i, e] if place is None else in_slot([P, HALF], F32, "trust%d%d" % (i, e), *place)
+            nc.scalar.activation(trust[:], squares[i, e][:], ACT.Exp, scale=-1.0)
             nc.vector.tensor_tensor(
-                gated[i][:, e, :], margins[b, 2 * u + e][:].indirect(half_list(pick, h)), trust[i][e], ALU.mult
+                gated[i][:, e, :], margins[b, 2 * u + e][:].indirect(half_list(pick, h)), trust[:], ALU.mult
             )
 
-        def weigh(i, e, squares):
-            nc.scalar.activation(trust[i][e], squares, ACT.Exp, scale=-1.0)
-            gate(i, e)
-
-        def first_pairs():
-            for i in range(2):
-                open_pair(i)
-            for e in range(2):
-                for i in range(2):
-                    product(i, e)
-                    leave_bank(ACT.Square, trust[i][e], i, e)
-                    weigh(i, e, trust[i][e])
-
-        def mask(i, squares=None):
-            open_pair(i)
-            for e in range(2):
-                product(i, e)
-                leave_bank(ACT.Square, trust[i][e] if squares is None else squares[:, HALF * e : HALF * (e + 1)], i, e)
-            if i in SPLIT_PAIRS:
-                for e in range(2):
-                    weigh(i, e, trust[i][e])
-                return
-            nc.scalar.activation(wide[i][:], wide[i][:] if squares is None else squares, ACT.Exp, scale=-1.0)
-            for e in range(2):
+        def mask(*slices):
+            for i, e in slices:
+                square(i, e)
                 gate(i, e)
 
-        def square(i, e, place):
-            squares = in_slot([P, HALF], F32, "squares%d%d" % (i, e), *place)
-            product(i, e)
-            leave_bank(ACT.Square, squares[:], i, e)
-            return squares[:]
-
-        def last_masks():
-            open_pair(6)
-            product(6, 0)
-            leave_bank(ACT.Square, trust[6][0], 6, 0)
-            weigh(6, 0, trust[6][0])
-            finish_pair(5)
-            weigh(6, 1, square(6, 1, cell(2, 1)))
-            sort_w2()
-            load_gain(2)
-            open_pair(7)
-            squares = [square(7, 0, (18, 6)), square(7, 1, cell(1, 1))]
-            weigh(7, 0, squares[0])
-            make_z(1)
-            weigh(7, 1, squares[1])
-
-        def finish_pair(i):
-            b, u, h = order[i]
+        def residuals(i):
             for e in range(2):
-                residual(i, e)
-            if h == 1:
-                return
+                leave_bank(ACT.Identity, res[i][:, e, :], i, e)
+
+        def multiply(i):
+            b, u, h = order[i]
             if u == 0:
-                zpairs[b] = in_slot([P, 2, HALF, 2], BF16, "zpairs%d" % b, *((14, 0), (8, 3))[b])
+                zpairs[b] = in_slot([P, 2, HALF, 2], BF16, "zpairs%d" % b, (14, 8)[b])
             nc.vector.scalar_tensor_tensor(
                 zpairs[b][:, u],
                 gated[i].rearrange("p e c -> p c e"),
@@ -315,39 +264,41 @@ def tile_list_coil_trust_weighting_kernel(
                 pair_tile[:].rearrange("p u c e -> p u (c e)").bitcast(F32).rearrange("p u c -> p c u"),
             )
 
-        def make_z(b):
-            zbf = grouped("zbf%d" % b, 1 + b)
-            weave(zpairs[b], zbf)
-            codes = in_slot([P, HALF], U32, "zc%d" % b, *(cell(3), (14, 2))[b])
+        def weave_z(b):
+            zbf[b] = grouped("zbf%d" % b, 1 + b)
+            weave(zpairs[b], zbf[b])
+
+        def quant_z(b):
+            codes = in_slot([P, HALF], U32, "zc%d" % b, *((17, 2, 2 * N), (13, 1))[b])
             scales = keep.tile([P, HALF], U8, name="zs%d" % b, align_bytes=64)
-            nc.vector.quantize_mx(out=codes[:].bitcast(E4M3), scales=scales[:], in_=zbf[:])
+            nc.vector.quantize_mx(out=codes[:].bitcast(E4M3), scales=scales[:], in_=zbf[b][:])
             zc[b, 0] = codes[:]
             zs[b, 0] = scales[:]
 
-        def late_products():
-            zbf = in_slot([P, 2, PACK * HALF], BF16, "late_zbf", 1)
-            for b in range(2):
-                if b == 1:
-                    for i in (last - 1, last):
-                        for e in range(2):
-                            residual(i, e)
-                positive = late_gated[b] if b == 1 else in_slot([P, PACK, HALF], F32, "positive", 9)
-                nc.scalar.activation(positive[:], late_gated[b][:], ACT.Relu)
-                nc.gpsimd.tensor_tensor(
-                    zbf[:, b, :].rearrange("p (c i t) -> p c t i", i=RUN, t=PACK),
-                    positive[:].rearrange("p t (c i) -> p c t i", i=RUN),
-                    late_res[b][:].rearrange("p t (c i) -> p c t i", i=RUN),
-                    ALU.mult,
-                )
-            return zbf
+        def keep_positive(b):
+            positive[b] = late_gated[b] if b == 1 else in_slot([P, PACK, HALF], F32, "positive", 14)
+            nc.scalar.activation(positive[b][:], late_gated[b][:], ACT.Relu)
 
-        def make_late_z(zbf):
+        def late_product(tile, b):
+            nc.gpsimd.tensor_tensor(
+                tile[:, b, :].rearrange("p (c i t) -> p c t i", i=RUN, t=PACK),
+                positive[b][:].rearrange("p t (c i) -> p c t i", i=RUN),
+                late_res[b][:].rearrange("p t (c i) -> p c t i", i=RUN),
+                ALU.mult,
+            )
+
+        def make_late_z(tile):
             codes = in_slot([P, S], U32, "late_zc", 13, 2)
             scales = keep.tile([P, S], U8, name="late_zs", align_bytes=64)
             for b in range(2):
                 zc[b, 1] = codes[:, HALF * b : HALF * (b + 1)]
                 zs[b, 1] = scales[:, HALF * b : HALF * (b + 1)]
-                nc.vector.quantize_mx(out=zc[b, 1].bitcast(E4M3), scales=zs[b, 1], in_=zbf[:, b, :])
+                for lo, hi in ((0, HALF),) if b == 0 else ((0, EARLY), (EARLY, HALF)):
+                    nc.vector.quantize_mx(
+                        out=zc[b, 1][:, lo:hi].bitcast(E4M3),
+                        scales=zs[b, 1][:, lo:hi],
+                        in_=tile[:, b, PACK * lo : PACK * hi],
+                    )
 
         gain = {}
         wgo_v = wgo.rearrange("(r t) s -> r t s", t=PACK)
@@ -356,16 +307,16 @@ def tile_list_coil_trust_weighting_kernel(
             gain[t] = in_slot([P, S], F32, "gain%d" % t, *((5, 0), (5, 2), (4, 0), (4, 2))[t])
             nc.sync.dma_start(gain[t][:], wgo_v[:, t, :].partition_broadcast(4))
 
-        def make_step(t, h):
-            acc2 = bank(t if h == 0 else (PACK, PACK, 2, 2)[t])
-            passes = (1, 0) if h == 1 and t > 0 else (0, 1)
+        def make_step(t, h, n, lo=0, hi=HALF):
+            acc2 = bank(n)
+            passes = (0, 1) if t < 2 - h else (1, 0)
             for b in passes:
                 nc.tensor.matmul_mx(
-                    out=acc2[:],
+                    out=acc2[:, : hi - lo],
                     lhsT=w2w[:, b, P * t : P * (t + 1)].bitcast(E4M3),
                     lhsT_scale=w2sc[4 * b :, P * t : P * (t + 1)],
-                    rhs=zc[b, h].bitcast(E4M3),
-                    rhs_scale=zs[b, h],
+                    rhs=zc[b, h][:, lo:hi].bitcast(E4M3),
+                    rhs_scale=zs[b, h][:, lo:hi],
                     start=(b == passes[0]),
                     stop=(b == passes[1]),
                 )
@@ -384,28 +335,47 @@ def tile_list_coil_trust_weighting_kernel(
             )
 
         quant_w1(0, 1)
-        first_pairs()
-        finish_pair(0)
+        mask((0, 0), (1, 0), (0, 1), (1, 1))
+        residuals(0)
+        multiply(0)
         round_w1(nc.vector.tensor_copy, 1, 1)
-        mask(2)
         quant_w1(1, 1)
         for t in (3, 0, 1):
             load_gain(t)
-        finish_pair(1)
-        mask(3)
-        finish_pair(2)
-        finish_pair(3)
-        mask(4, grouped("squares4", 1)[:].bitcast(F32))
-        make_z(0)
-        finish_pair(4)
-        mask(5)
-        last_masks()
-        late_zbf = late_products()
+        mask((2, 0), (3, 0))
+        residuals(1)
+        mask((2, 1), (3, 1))
+        residuals(2)
+        multiply(2)
+        residuals(3)
+        mask((4, 0), (6, 0), (4, 1), (6, 1))
+        residuals(4)
+        multiply(4)
+        mask((5, 0), (5, 1))
+        square(7, 1, (18, 4))
+        gate(7, 1, (17, 2))
+        residuals(5)
+        multiply(5)
+        sort_w2()
+        load_gain(2)
+        weave_z(0)
+        quant_z(0)
+        square(7, 0, (18, 2))
+        keep_positive(0)
+        weave_z(1)
+        quant_z(1)
+        gate(7, 0, (8, 0))
+        late_zbf = in_slot([P, 2, PACK * HALF], BF16, "late_zbf", 3)
+        late_product(late_zbf, 0)
+        residuals(6)
+        residuals(7)
+        keep_positive(1)
+        late_product(late_zbf, 1)
 
         steps = {t: in_slot([P, S], F32, "step%d" % t, *((6, 0), (6, 2), (15, 0), (7, 0))[t]) for t in range(PACK)}
         widths = (HALF, HALF, EARLY)
         gained = [in_slot([P, widths[t]], F32, "gained%d" % t, *((0, 2), (0, 3), (13, 0))[t]) for t in range(3)]
-        banks = [make_step(t, 0) for t in range(PACK)]
+        banks = [make_step(t, 0, (0, 2, 4, 5)[t]) for t in range(PACK)]
 
         def apply_gain(t):
             nc.vector.tensor_tensor(gained[t][:], banks[t][:, : widths[t]], gain[t][:, : widths[t]], ALU.mult)
@@ -422,15 +392,18 @@ def tile_list_coil_trust_weighting_kernel(
         nc.scalar.copy(steps[2][:, EARLY:HALF], banks[2][:, EARLY:])
         nc.scalar.copy(steps[3][:, :HALF], banks[3][:])
         make_late_z(late_zbf)
-        clear_page(3, 1)
+        clear_page(3, 3)
         place_step(2, EARLY, HALF, steps[2][:, EARLY:HALF])
-        for t in (0, 2, 1, 3):
-            nc.scalar.copy(steps[t][:, HALF:], make_step(t, 1)[:])
+        for lo in (0, EARLY):
+            first = make_step(0, 1, 1 + 2 * (lo // EARLY), lo, lo + EARLY)
+            nc.scalar.copy(steps[0][:, HALF + lo : HALF + lo + EARLY], first[:, :EARLY])
+        for t in (2, 1, 3):
+            nc.scalar.copy(steps[t][:, HALF:], make_step(t, 1, (None, 7, 6, 1)[t])[:])
 
         out_v = out_0.rearrange("(p t) m -> p t m", t=PACK)
         chunks = [slice(lo, hi) for lo, hi in zip(EDGES, EDGES[1:])]
         pairs = [in_slot([P, 2, c.stop - c.start, 2], BF16, "pairs%d" % c.start, 8, c.start // 256) for c in chunks]
-        ybf = [in_slot([P, PACK * (c.stop - c.start)], BF16, "ybf%d" % c.start, 2, c.start // 256) for c in chunks]
+        ybf = [in_slot([P, PACK * (c.stop - c.start)], BF16, "ybf%d" % c.start, 1, c.start // 256) for c in chunks]
         for t in (0, 2, 1, 3):
             lo = HALF if t < 3 else 0
             place_step(t, lo, S, steps[t][:, lo:])

@@ -182,7 +182,6 @@ def tile_list_coil_trust_weighting_kernel(
         gated = {}
         zpairs = {}
         zbf = {}
-        positive = {}
         late_res = {}
         late_gated = {}
         zc = {}
@@ -203,7 +202,7 @@ def tile_list_coil_trust_weighting_kernel(
                 gated[i] = in_slot([P, 2, HALF], F32, "gated%d" % i, 21, 2 * u)[:]
                 return
             if b not in late_res:
-                late_res[b] = in_slot([P, PACK, HALF], F32, "late_res%d" % b, *((23, 0), (8, 1))[b])
+                late_res[b] = in_slot([P, PACK, HALF], F32, "late_res%d" % b, (23, 8)[b])
                 late_gated[b] = in_slot([P, PACK, HALF], F32, "late_gated%d" % b, (22, 15)[b])
             res[i] = late_res[b][:, 2 * u : 2 * u + 2, :]
             gated[i] = late_gated[b][:, 2 * u : 2 * u + 2, :]
@@ -239,6 +238,7 @@ def tile_list_coil_trust_weighting_kernel(
         def mask(*slices):
             for i, e in slices:
                 square(i, e)
+            for i, e in slices:
                 gate(i, e)
 
         def residuals(i):
@@ -248,7 +248,7 @@ def tile_list_coil_trust_weighting_kernel(
         def multiply(i):
             b, u, h = order[i]
             if u == 0:
-                zpairs[b] = in_slot([P, 2, HALF, 2], BF16, "zpairs%d" % b, (14, 8)[b])
+                zpairs[b] = in_slot([P, 2, HALF, 2], BF16, "zpairs%d" % b, *((14, 0), (8, 3))[b])
             nc.vector.scalar_tensor_tensor(
                 zpairs[b][:, u],
                 gated[i].rearrange("p e c -> p c e"),
@@ -275,17 +275,17 @@ def tile_list_coil_trust_weighting_kernel(
             zc[b, 0] = codes[:]
             zs[b, 0] = scales[:]
 
-        def keep_positive(b):
-            positive[b] = late_gated[b] if b == 1 else in_slot([P, PACK, HALF], F32, "positive", 14)
-            nc.scalar.activation(positive[b][:], late_gated[b][:], ACT.Relu)
-
         def late_product(tile, b):
-            nc.gpsimd.tensor_tensor(
-                tile[:, b, :].rearrange("p (c i t) -> p c t i", i=RUN, t=PACK),
-                positive[b][:].rearrange("p t (c i) -> p c t i", i=RUN),
-                late_res[b][:].rearrange("p t (c i) -> p c t i", i=RUN),
-                ALU.mult,
-            )
+            positive = late_gated[b] if b == 1 else in_slot([P, PACK, HALF], F32, "positive", 9)
+            for lo in (0, EARLY):
+                cols = slice(lo, lo + EARLY)
+                nc.scalar.activation(positive[:, :, cols], late_gated[b][:, :, cols], ACT.Relu)
+                nc.gpsimd.tensor_tensor(
+                    tile[:, b, PACK * lo : PACK * (lo + EARLY)].rearrange("p (c i t) -> p c t i", i=RUN, t=PACK),
+                    positive[:, :, cols].rearrange("p t (c i) -> p c t i", i=RUN),
+                    late_res[b][:, :, cols].rearrange("p t (c i) -> p c t i", i=RUN),
+                    ALU.mult,
+                )
 
         def make_late_z(tile):
             codes = in_slot([P, S], U32, "late_zc", 13, 2)
@@ -309,7 +309,7 @@ def tile_list_coil_trust_weighting_kernel(
 
         def make_step(t, h, n, lo=0, hi=HALF):
             acc2 = bank(n)
-            passes = (0, 1) if t < 2 - h else (1, 0)
+            passes = (0, 1) if t == 0 else (1, 0)
             for b in passes:
                 nc.tensor.matmul_mx(
                     out=acc2[:, : hi - lo],
@@ -335,7 +335,8 @@ def tile_list_coil_trust_weighting_kernel(
             )
 
         quant_w1(0, 1)
-        mask((0, 0), (1, 0), (0, 1), (1, 1))
+        mask((0, 0), (1, 0))
+        mask((0, 1), (1, 1))
         residuals(0)
         multiply(0)
         round_w1(nc.vector.tensor_copy, 1, 1)
@@ -348,11 +349,13 @@ def tile_list_coil_trust_weighting_kernel(
         residuals(2)
         multiply(2)
         residuals(3)
-        mask((4, 0), (6, 0), (4, 1), (6, 1))
+        mask((4, 0), (6, 0))
+        mask((4, 1), (6, 1))
         residuals(4)
         multiply(4)
         mask((5, 0), (5, 1))
         square(7, 1, (18, 4))
+        square(7, 0, (18, 2))
         gate(7, 1, (17, 2))
         residuals(5)
         multiply(5)
@@ -360,16 +363,13 @@ def tile_list_coil_trust_weighting_kernel(
         load_gain(2)
         weave_z(0)
         quant_z(0)
-        square(7, 0, (18, 2))
-        keep_positive(0)
         weave_z(1)
         quant_z(1)
-        gate(7, 0, (8, 0))
+        gate(7, 0, (21, 2))
         late_zbf = in_slot([P, 2, PACK * HALF], BF16, "late_zbf", 3)
         late_product(late_zbf, 0)
         residuals(6)
         residuals(7)
-        keep_positive(1)
         late_product(late_zbf, 1)
 
         steps = {t: in_slot([P, S], F32, "step%d" % t, *((6, 0), (6, 2), (15, 0), (7, 0))[t]) for t in range(PACK)}
@@ -384,8 +384,8 @@ def tile_list_coil_trust_weighting_kernel(
             nc.vector.tensor_copy(pages[t][:].indirect(place[:, : widths[t] // 16]), gained[t][:])
 
         apply_gain(0)
-        apply_gain(1)
         place_gained(0)
+        apply_gain(1)
         apply_gain(2)
         place_gained(1)
         place_gained(2)

@@ -269,7 +269,7 @@ def tile_list_coil_trust_weighting_kernel(
             weave(zpairs[b], zbf[b])
 
         def quant_z(b):
-            codes = in_slot([P, HALF], U32, "zc%d" % b, *((17, 2, 2 * N), (13, 1))[b])
+            codes = in_slot([P, HALF], U32, "zc%d" % b, *((17, 2, 2 * N), (13, 2))[b])
             scales = keep.tile([P, HALF], U8, name="zs%d" % b, align_bytes=64)
             nc.vector.quantize_mx(out=codes[:].bitcast(E4M3), scales=scales[:], in_=zbf[b][:])
             zc[b, 0] = codes[:]
@@ -288,7 +288,7 @@ def tile_list_coil_trust_weighting_kernel(
                 )
 
         def make_late_z(tile):
-            codes = in_slot([P, S], U32, "late_zc", 13, 2)
+            codes = in_slot([P, S], U32, "late_zc", 13)
             scales = keep.tile([P, S], U8, name="late_zs", align_bytes=64)
             for b in range(2):
                 zc[b, 1] = codes[:, HALF * b : HALF * (b + 1)]

@@ -55,7 +55,7 @@ def tile_list_coil_trust_weighting_kernel(
         moved = keep.tile([P, S], U8, name="moved", align_bytes=64)
         w2sc_raw = keep.tile([P, N], U8, name="w2sc_raw", align_bytes=64)
         w2sc = in_slot([P, N], U8, "w2sc", 17, 2, N)
-        w2raw = in_slot([P, 2, N], I32, "w2raw", 4)
+        w2raw = keep.tile([P, 2, N], I32, name="w2raw", align_bytes=64)
         w2w = in_slot([P, 2, N], I32, "w2w", 17, 0, N)
         tgt = keep.tile([P, 2, PACK], F32, name="tgt")
         ntgt = keep.tile([P, 2 * PACK], F32, name="ntgt")
@@ -301,11 +301,14 @@ def tile_list_coil_trust_weighting_kernel(
                     )
 
         gain = {}
-        wgo_v = wgo.rearrange("(r t) s -> r t s", t=PACK)
+        wgo_v = wgo.rearrange("(r u e) s -> u r e s", u=2, e=2)
 
-        def load_gain(t):
-            gain[t] = in_slot([P, S], F32, "gain%d" % t, *((5, 0), (5, 2), (4, 0), (4, 2))[t])
-            nc.sync.dma_start(gain[t][:], wgo_v[:, t, :].partition_broadcast(4))
+        def load_gains(u):
+            tile = in_slot([P, 2, S], F32, "gains%d" % u, 4 + u)
+            for q in (0, 2, 1, 3):
+                nc.sync.dma_start(tile[32 * q : 32 * (q + 1)], wgo_v[u])
+            for e in range(2):
+                gain[2 * u + e] = tile[:, e, :]
 
         def make_step(t, h, n, lo=0, hi=HALF):
             acc2 = bank(n)
@@ -341,8 +344,8 @@ def tile_list_coil_trust_weighting_kernel(
         multiply(0)
         round_w1(nc.vector.tensor_copy, 1, 1)
         quant_w1(1, 1)
-        for t in (3, 0, 1):
-            load_gain(t)
+        for u in range(2):
+            load_gains(u)
         mask((2, 0), (3, 0))
         residuals(1)
         mask((2, 1), (3, 1))
@@ -360,7 +363,6 @@ def tile_list_coil_trust_weighting_kernel(
         residuals(5)
         multiply(5)
         sort_w2()
-        load_gain(2)
         weave_z(0)
         quant_z(0)
         weave_z(1)

@@ -301,14 +301,14 @@ def tile_list_coil_trust_weighting_kernel(
                     )
 
         gain = {}
-        wgo_v = wgo.rearrange("(r u e) s -> u r e s", u=2, e=2)
+        wgo_v = wgo.rearrange("(r t) s -> r t s", t=PACK)
 
-        def load_gains(u):
-            tile = in_slot([P, 2, S], F32, "gains%d" % u, 4 + u)
+        def load_gains(name, place, slices, cols):
+            tile = in_slot([P, slices.stop - slices.start, cols.stop - cols.start], F32, name, *place)
             for q in (0, 2, 1, 3):
-                nc.sync.dma_start(tile[32 * q : 32 * (q + 1)], wgo_v[u])
-            for e in range(2):
-                gain[2 * u + e] = tile[:, e, :]
+                nc.sync.dma_start(tile[32 * q : 32 * (q + 1)], wgo_v[:, slices, cols])
+            for t in range(slices.start, slices.stop):
+                gain[t, cols.start] = tile[:, t - slices.start, :]
 
         def make_step(t, h, n, lo=0, hi=HALF):
             acc2 = bank(n)
@@ -326,7 +326,8 @@ def tile_list_coil_trust_weighting_kernel(
             return acc2
 
         def place_step(t, lo, hi, step):
-            nc.vector.tensor_tensor(pages[t][:].indirect(place[:, lo // 16 : hi // 16]), step, gain[t][:, lo:hi], ALU.mult)
+            first = lo // HALF * HALF
+            nc.vector.tensor_tensor(pages[t][:].indirect(place[:, lo // 16 : hi // 16]), step, gain[t, first][:, lo - first : hi - first], ALU.mult)
 
         def sort_w2():
             nc.vector.tensor_copy(
@@ -344,8 +345,9 @@ def tile_list_coil_trust_weighting_kernel(
         multiply(0)
         round_w1(nc.vector.tensor_copy, 1, 1)
         quant_w1(1, 1)
-        for u in range(2):
-            load_gains(u)
+        load_gains("gains_early", (4, 0), slice(0, 3), slice(0, HALF))
+        load_gains("gains_late", (5, 1), slice(0, 3), slice(HALF, S))
+        load_gains("gains_last", (4, 3), slice(3, 4), slice(0, S))
         mask((2, 0), (3, 0))
         residuals(1)
         mask((2, 1), (3, 1))
@@ -374,13 +376,13 @@ def tile_list_coil_trust_weighting_kernel(
         residuals(7)
         late_product(late_zbf, 1)
 
-        steps = {t: in_slot([P, S], F32, "step%d" % t, *((6, 0), (6, 2), (15, 0), (7, 0))[t]) for t in range(PACK)}
+        steps = {t: in_slot([P, S], F32, "step%d" % t, *((6, 0), (6, 2), (15, 0), (23, 0))[t]) for t in range(PACK)}
         widths = (HALF, HALF, EARLY)
         gained = [in_slot([P, widths[t]], F32, "gained%d" % t, *((0, 2), (0, 3), (13, 0))[t]) for t in range(3)]
         banks = [make_step(t, 0, (0, 2, 4, 5)[t]) for t in range(PACK)]
 
         def apply_gain(t):
-            nc.vector.tensor_tensor(gained[t][:], banks[t][:, : widths[t]], gain[t][:, : widths[t]], ALU.mult)
+            nc.vector.tensor_tensor(gained[t][:], banks[t][:, : widths[t]], gain[t, 0][:, : widths[t]], ALU.mult)
 
         def place_gained(t):
             nc.vector.tensor_copy(pages[t][:].indirect(place[:, : widths[t] // 16]), gained[t][:])
@@ -416,8 +418,8 @@ def tile_list_coil_trust_weighting_kernel(
                     nc.scalar.copy(pairs[c][:, 1], src.unsqueeze(2).to_broadcast([P, cols.stop - cols.start, 2]))
                 elif t < 3:
                     nc.scalar.copy(pairs[c][:, t // 2, :, t % 2], src)
-                if t == 1 and c < ON_VECTOR:
-                    weave(pairs[c], ybf[c])
+                if t == 1 and 0 < c <= ON_VECTOR:
+                    weave(pairs[c - 1], ybf[c - 1])
 
         words_v = out_1[0].rearrange("p m t -> p (m t)").bitcast(I32)
         for c, cols in enumerate(chunks):
@@ -425,7 +427,9 @@ def tile_list_coil_trust_weighting_kernel(
                 nc.vector.tensor_copy(ybf[c][:].rearrange("p (m t) -> p m t", t=PACK)[:, :, 3], pages[3][:, cols])
             else:
                 nc.scalar.copy(pairs[c][:, 1, :, 1], pages[3][:, cols])
-                weave(pairs[c], ybf[c])
+                if c > ON_VECTOR:
+                    weave(pairs[c - 1], ybf[c - 1])
+        weave(pairs[-1], ybf[-1])
         for c, cols in enumerate(chunks):
             nc.vector.quantize_mx(out=ycodes[:, cols].bitcast(E4M3), scales=yscales[:, cols], in_=ybf[c][:])
             nc.sync.dma_start(words_v[:, cols], ycodes[:, cols].bitcast(I32))

@@ -55,7 +55,7 @@ def tile_list_coil_trust_weighting_kernel(
         moved = keep.tile([P, S], U8, name="moved", align_bytes=64)
         w2sc_raw = keep.tile([P, N], U8, name="w2sc_raw", align_bytes=64)
         w2sc = in_slot([P, N], U8, "w2sc", 17, 2, N)
-        w2raw = keep.tile([P, 2, N], I32, name="w2raw", align_bytes=64)
+        w2raw = in_slot([P, 2, N], I32, "w2raw", 4)
         w2w = in_slot([P, 2, N], I32, "w2w", 17, 0, N)
         tgt = keep.tile([P, 2, PACK], F32, name="tgt")
         ntgt = keep.tile([P, 2 * PACK], F32, name="ntgt")
@@ -138,7 +138,7 @@ def tile_list_coil_trust_weighting_kernel(
                 if a + b < 2:
                     w1bf[a, b] = grouped("w1bf%d%d" % (a, b), 2 * b + a)
                 else:
-                    w1bf[a, b] = in_slot([P, PACK * HALF], BF16, "w1bf11", 16)
+                    w1bf[a, b] = in_slot([P, PACK * HALF], BF16, "w1bf11", 24)
                 if b == 0:
                     w1c[a, b] = in_slot([P, KP], U32, "w1c%d0" % a, *((18, 1), (0, 0))[a])
                 elif a == 0:
@@ -179,6 +179,7 @@ def tile_list_coil_trust_weighting_kernel(
         res = {}
         acc = {}
         squares = {}
+        trust = {}
         gated = {}
         zpairs = {}
         zbf = {}
@@ -207,13 +208,16 @@ def tile_list_coil_trust_weighting_kernel(
             res[i] = late_res[b][:, 2 * u : 2 * u + 2, :]
             gated[i] = late_gated[b][:, 2 * u : 2 * u + 2, :]
 
-        def square(i, e, place=None):
+        def own_squares(i, e, *place):
+            return in_slot([P, HALF], F32, "squares%d%d" % (i, e), *place)[:]
+
+        def square(i, e, dst=None):
             b, u, h = order[i]
             t = 2 * u + e
             n = len(acc) % 8
             if i not in res:
                 open_pair(i)
-            acc[i, e] = bank(n)
+            acc[i, e] = bank(2 * (0, 1, 2, 3, 0, 1, 2, 0)[i] + e)
             for a in range(2):
                 nc.tensor.matmul_mx(
                     out=acc[i, e][:],
@@ -224,26 +228,39 @@ def tile_list_coil_trust_weighting_kernel(
                     start=(a == 0),
                     stop=(a == 1),
                 )
-            squares[i, e] = in_slot([P, HALF], F32, "squares%d%d" % (i, e), *(place or (16, n)))
-            leave_bank(ACT.Square, squares[i, e][:], i, e)
+            squares[i, e] = own_squares(i, e, 16, n) if dst is None else dst
+            leave_bank(ACT.Square, squares[i, e], i, e)
 
-        def gate(i, e, place=None):
+        def weigh(i, e, place=None):
+            trust[i, e] = squares[i, e] if place is None else in_slot([P, HALF], F32, "trust%d%d" % (i, e), *place)[:]
+            nc.scalar.activation(trust[i, e], squares[i, e], ACT.Exp, scale=-1.0)
+
+        def gather(i, e):
             b, u, h = order[i]
-            trust = squares[i, e] if place is None else in_slot([P, HALF], F32, "trust%d%d" % (i, e), *place)
-            nc.scalar.activation(trust[:], squares[i, e][:], ACT.Exp, scale=-1.0)
             nc.vector.tensor_tensor(
-                gated[i][:, e, :], margins[b, 2 * u + e][:].indirect(half_list(pick, h)), trust[:], ALU.mult
+                gated[i][:, e, :], margins[b, 2 * u + e][:].indirect(half_list(pick, h)), trust[i, e], ALU.mult
             )
 
-        def mask(*slices):
-            for i, e in slices:
-                square(i, e)
-            for i, e in slices:
-                gate(i, e)
+        def gate(i, e, place=None):
+            weigh(i, e, place)
+            gather(i, e)
+
+        def mask(first, second, between):
+            both = in_slot([P, 2, HALF], F32, "squares%d%d" % first, 16, len(acc) % 8)
+            for k, (i, e) in enumerate((first, second)):
+                square(i, e, both[:, k, :])
+                trust[i, e] = both[:, k, :]
+            residual(*between)
+            nc.scalar.activation(both[:], both[:], ACT.Exp, scale=-1.0)
+            for i, e in (first, second):
+                gather(i, e)
+
+        def residual(i, e):
+            leave_bank(ACT.Identity, res[i][:, e, :], i, e)
 
         def residuals(i):
             for e in range(2):
-                leave_bank(ACT.Identity, res[i][:, e, :], i, e)
+                residual(i, e)
 
         def multiply(i):
             b, u, h = order[i]
@@ -339,34 +356,41 @@ def tile_list_coil_trust_weighting_kernel(
             )
 
         quant_w1(0, 1)
-        mask((0, 0), (1, 0))
-        mask((0, 1), (1, 1))
-        residuals(0)
+        square(0, 0)
+        square(0, 1)
+        gate(0, 0)
+        square(1, 0)
+        weigh(0, 1)
+        gate(1, 0)
+        gather(0, 1)
+        square(1, 1)
+        residual(0, 0)
+        gate(1, 1)
+        residual(0, 1)
         multiply(0)
         round_w1(nc.vector.tensor_copy, 1, 1)
         quant_w1(1, 1)
-        load_gains("gains_early", (4, 0), slice(0, 3), slice(0, HALF))
+        load_gains("gains_early", (4, 2), slice(0, 3), slice(0, HALF))
         load_gains("gains_late", (5, 1), slice(0, 3), slice(HALF, S))
-        load_gains("gains_last", (4, 3), slice(3, 4), slice(0, S))
-        mask((2, 0), (3, 0))
-        residuals(1)
-        mask((2, 1), (3, 1))
-        residuals(2)
+        load_gains("gains_last", (24, 0), slice(3, 4), slice(0, S))
+        mask((2, 0), (3, 0), (1, 0))
+        mask((2, 1), (3, 1), (2, 0))
+        residual(2, 1)
         multiply(2)
-        residuals(3)
-        mask((4, 0), (6, 0))
-        mask((4, 1), (6, 1))
-        residuals(4)
+        mask((4, 0), (6, 0), (1, 1))
+        mask((4, 1), (6, 1), (4, 0))
+        residual(4, 1)
         multiply(4)
-        mask((5, 0), (5, 1))
-        square(7, 1, (18, 4))
-        square(7, 0, (18, 2))
+        mask((5, 0), (5, 1), (3, 0))
+        square(7, 1, own_squares(7, 1, 18, 4))
+        square(7, 0, own_squares(7, 0, 18, 2))
         gate(7, 1, (17, 2))
         residuals(5)
         multiply(5)
         sort_w2()
         weave_z(0)
         quant_z(0)
+        residual(3, 1)
         weave_z(1)
         quant_z(1)
         gate(7, 0, (21, 2))
@@ -379,7 +403,7 @@ def tile_list_coil_trust_weighting_kernel(
         steps = {t: in_slot([P, S], F32, "step%d" % t, *((6, 0), (6, 2), (15, 0), (23, 0))[t]) for t in range(PACK)}
         widths = (HALF, HALF, EARLY)
         gained = [in_slot([P, widths[t]], F32, "gained%d" % t, *((0, 2), (0, 3), (13, 0))[t]) for t in range(3)]
-        banks = [make_step(t, 0, (0, 2, 4, 5)[t]) for t in range(PACK)]
+        banks = [make_step(t, 0, (2, 3, 6, 7)[t]) for t in range(PACK)]
 
         def apply_gain(t):
             nc.vector.tensor_tensor(gained[t][:], banks[t][:, : widths[t]], gain[t, 0][:, : widths[t]], ALU.mult)
@@ -399,10 +423,10 @@ def tile_list_coil_trust_weighting_kernel(
         clear_page(3, 3)
         place_step(2, EARLY, HALF, steps[2][:, EARLY:HALF])
         for lo in (0, EARLY):
-            first = make_step(0, 1, 1 + 2 * (lo // EARLY), lo, lo + EARLY)
+            first = make_step(0, 1, lo // EARLY, lo, lo + EARLY)
             nc.scalar.copy(steps[0][:, HALF + lo : HALF + lo + EARLY], first[:, :EARLY])
         for t in (2, 1, 3):
-            nc.scalar.copy(steps[t][:, HALF:], make_step(t, 1, (None, 7, 6, 1)[t])[:])
+            nc.scalar.copy(steps[t][:, HALF:], make_step(t, 1, (None, 5, 4, 0)[t])[:])
 
         out_v = out_0.rearrange("(p t) m -> p t m", t=PACK)
         chunks = [slice(lo, hi) for lo, hi in zip(EDGES, EDGES[1:])]

@@ -28,6 +28,7 @@ SPLIT = 64
 EDGES = (0, 512, 1024, 1536, 1792, 2048)
 ON_VECTOR = 2
 RUN = 4
+SHARE = 80
 EARLY = 256
 
 
@@ -182,7 +183,6 @@ def tile_list_coil_trust_weighting_kernel(
         trust = {}
         gated = {}
         zpairs = {}
-        zbf = {}
         late_res = {}
         late_gated = {}
         zc = {}
@@ -217,7 +217,7 @@ def tile_list_coil_trust_weighting_kernel(
             n = len(acc) % 8
             if i not in res:
                 open_pair(i)
-            acc[i, e] = bank(2 * (0, 1, 2, 3, 0, 1, 2, 0)[i] + e)
+            acc[i, e] = bank(2 * (0, 1, 2, 3, 0, 0, 2, 1)[i] + e)
             for a in range(2):
                 nc.tensor.matmul_mx(
                     out=acc[i, e][:],
@@ -245,13 +245,14 @@ def tile_list_coil_trust_weighting_kernel(
             weigh(i, e, place)
             gather(i, e)
 
-        def mask(first, second, between):
-            both = in_slot([P, 2, HALF], F32, "squares%d%d" % first, 16, len(acc) % 8)
+        def mask(first, second, between, place=None):
+            both = in_slot([P, 2, HALF], F32, "trust%d%d" % first, 16, len(acc) % 8)
+            raw = both if place is None else in_slot([P, 2, HALF], F32, "squares%d%d" % first, *place)
             for k, (i, e) in enumerate((first, second)):
-                square(i, e, both[:, k, :])
+                square(i, e, raw[:, k, :])
                 trust[i, e] = both[:, k, :]
-            residual(*between)
-            nc.scalar.activation(both[:], both[:], ACT.Exp, scale=-1.0)
+            between()
+            nc.scalar.activation(both[:], raw[:], ACT.Exp, scale=-1.0)
             for i, e in (first, second):
                 gather(i, e)
 
@@ -281,14 +282,15 @@ def tile_list_coil_trust_weighting_kernel(
                 pair_tile[:].rearrange("p u c e -> p u (c e)").bitcast(F32).rearrange("p u c -> p c u"),
             )
 
-        def weave_z(b):
-            zbf[b] = grouped("zbf%d" % b, 1 + b)
-            weave(zpairs[b], zbf[b])
-
-        def quant_z(b):
-            codes = in_slot([P, HALF], U32, "zc%d" % b, *((17, 2, 2 * N), (13, 2))[b])
-            scales = keep.tile([P, HALF], U8, name="zs%d" % b, align_bytes=64)
-            nc.vector.quantize_mx(out=codes[:].bitcast(E4M3), scales=scales[:], in_=zbf[b][:])
+        def make_z(b, tiles):
+            width = HALF // len(tiles)
+            codes = in_slot([P, HALF], U32, "zc%d" % b, *((24, 2), (13, 2))[b])
+            scales = in_slot([P, HALF], U8, "zs%d" % b, *((17, 2, 2 * N), (24, 3))[b])
+            words = zpairs[b][:].rearrange("p u c e -> p u (c e)").bitcast(F32).rearrange("p u c -> p c u")
+            for k, tile in enumerate(tiles):
+                cols = slice(width * k, width * (k + 1))
+                nc.scalar.copy(tile[:].bitcast(F32).rearrange("p (c u) -> p c u", u=2), words[:, cols])
+                nc.vector.quantize_mx(out=codes[:, cols].bitcast(E4M3), scales=scales[:, cols], in_=tile[:])
             zc[b, 0] = codes[:]
             zs[b, 0] = scales[:]
 
@@ -368,33 +370,34 @@ def tile_list_coil_trust_weighting_kernel(
         gate(1, 1)
         residual(0, 1)
         multiply(0)
-        round_w1(nc.vector.tensor_copy, 1, 1)
+        round_w1(nc.vector.tensor_copy, 1, 1, 0, SHARE)
+        mask((2, 0), (3, 0), lambda: round_w1(nc.scalar.copy, 1, 1, SHARE, P))
         quant_w1(1, 1)
+        mask((2, 1), (3, 1), lambda: residual(2, 0), (5, 2))
         load_gains("gains_early", (4, 2), slice(0, 3), slice(0, HALF))
         load_gains("gains_late", (5, 1), slice(0, 3), slice(HALF, S))
         load_gains("gains_last", (24, 0), slice(3, 4), slice(0, S))
-        mask((2, 0), (3, 0), (1, 0))
-        mask((2, 1), (3, 1), (2, 0))
-        residual(2, 1)
+        mask((4, 0), (6, 0), lambda: residual(2, 1))
         multiply(2)
-        mask((4, 0), (6, 0), (1, 1))
-        mask((4, 1), (6, 1), (4, 0))
+        mask((4, 1), (6, 1), lambda: residual(4, 0), (23, 0))
         residual(4, 1)
         multiply(4)
-        mask((5, 0), (5, 1), (3, 0))
+        residuals(1)
+        for e in range(2):
+            square(5, e)
+        for e in range(2):
+            gate(5, e)
         square(7, 1, own_squares(7, 1, 18, 4))
         square(7, 0, own_squares(7, 0, 18, 2))
         gate(7, 1, (17, 2))
         residuals(5)
         multiply(5)
         sort_w2()
-        weave_z(0)
-        quant_z(0)
-        residual(3, 1)
-        weave_z(1)
-        quant_z(1)
+        make_z(0, [grouped("zbf0", 1)])
+        residuals(3)
+        make_z(1, [in_slot([P, PACK * EARLY], BF16, "zbf1%d" % k, 2, 2 + k) for k in range(2)])
         gate(7, 0, (21, 2))
-        late_zbf = in_slot([P, 2, PACK * HALF], BF16, "late_zbf", 3)
+        late_zbf = in_slot([P, 2, PACK * HALF], BF16, "late_zbf", 2, 2)
         late_product(late_zbf, 0)
         residuals(6)
         residuals(7)
@@ -403,7 +406,7 @@ def tile_list_coil_trust_weighting_kernel(
         steps = {t: in_slot([P, S], F32, "step%d" % t, *((6, 0), (6, 2), (15, 0), (23, 0))[t]) for t in range(PACK)}
         widths = (HALF, HALF, EARLY)
         gained = [in_slot([P, widths[t]], F32, "gained%d" % t, *((0, 2), (0, 3), (13, 0))[t]) for t in range(3)]
-        banks = [make_step(t, 0, (2, 3, 6, 7)[t]) for t in range(PACK)]
+        banks = [make_step(t, 0, (0, 1, 6, 7)[t]) for t in range(PACK)]
 
         def apply_gain(t):
             nc.vector.tensor_tensor(gained[t][:], banks[t][:, : widths[t]], gain[t, 0][:, : widths[t]], ALU.mult)
@@ -423,10 +426,10 @@ def tile_list_coil_trust_weighting_kernel(
         clear_page(3, 3)
         place_step(2, EARLY, HALF, steps[2][:, EARLY:HALF])
         for lo in (0, EARLY):
-            first = make_step(0, 1, lo // EARLY, lo, lo + EARLY)
+            first = make_step(0, 1, 2 + lo // EARLY, lo, lo + EARLY)
             nc.scalar.copy(steps[0][:, HALF + lo : HALF + lo + EARLY], first[:, :EARLY])
         for t in (2, 1, 3):
-            nc.scalar.copy(steps[t][:, HALF:], make_step(t, 1, (None, 5, 4, 0)[t])[:])
+            nc.scalar.copy(steps[t][:, HALF:], make_step(t, 1, (None, 5, 4, 2)[t])[:])
 
         out_v = out_0.rearrange("(p t) m -> p t m", t=PACK)
         chunks = [slice(lo, hi) for lo, hi in zip(EDGES, EDGES[1:])]

@@ -28,7 +28,7 @@ SPLIT = 64
 EDGES = (0, 512, 1024, 1536, 1792, 2048)
 ON_VECTOR = 2
 RUN = 4
-SHARE = 80
+SHARE = 104
 EARLY = 256
 
 
@@ -58,8 +58,8 @@ def tile_list_coil_trust_weighting_kernel(
         w2sc = in_slot([P, N], U8, "w2sc", 17, 2, N)
         w2raw = in_slot([P, 2, N], I32, "w2raw", 4)
         w2w = in_slot([P, 2, N], I32, "w2w", 17, 0, N)
-        tgt = keep.tile([P, 2, PACK], F32, name="tgt")
-        ntgt = keep.tile([P, 2 * PACK], F32, name="ntgt")
+        tgt = [keep.tile([P, PACK], F32, name="tgt%d" % b) for b in range(2)]
+        ntgt = [keep.tile([P, PACK], F32, name="ntgt%d" % b) for b in range(2)]
         ycodes = keep.tile([P, T2], U32, name="ycodes", align_bytes=64)
         yscales = keep.tile([P, T2], U8, name="yscales", align_bytes=64)
 
@@ -95,13 +95,13 @@ def tile_list_coil_trust_weighting_kernel(
             margins[b, t] = in_slot([P, T], F32, "margins%d%d" % (b, t), 6 + t if b == 0 else (13, 2, 3, 1)[t])
             nc.sync.dma_start(margins[b, t][:], sT_v[b, t])
 
+        target_v = target.rearrange("(b p t) -> b p t", b=2, t=PACK)
         load_w1(0, 0)
         nc.sync.dma_start(pick[:], offs)
         load_scales()
         load_w1(1, 0, 0, SPLIT)
         load_tab(0)
-        nc.sync.dma_start(tgt[:], target.rearrange("(b p t) -> p b t", b=2, t=PACK))
-        nc.sync.dma_start(place[:], offs2)
+        nc.sync.dma_start(tgt[0][:], target_v[0])
         load_w1(1, 0, SPLIT, P)
         load_tab(1)
         load_w1(0, 1)
@@ -110,6 +110,8 @@ def tile_list_coil_trust_weighting_kernel(
         load_w1(1, 1)
         load_margins(0, 2)
         load_margins(0, 3)
+        nc.sync.dma_start(tgt[1][:], target_v[1])
+        nc.sync.dma_start(place[:], offs2)
         for t in range(PACK):
             load_margins(1, t)
         nc.sync.dma_start(w2raw[:], w2_words.rearrange("a p c i -> p a (c i)").bitcast(I32))
@@ -139,7 +141,7 @@ def tile_list_coil_trust_weighting_kernel(
                 if a + b < 2:
                     w1bf[a, b] = grouped("w1bf%d%d" % (a, b), 2 * b + a)
                 else:
-                    w1bf[a, b] = in_slot([P, PACK * HALF], BF16, "w1bf11", 24)
+                    w1bf[a, b] = in_slot([P, PACK * HALF], BF16, "w1bf11", 16)
                 if b == 0:
                     w1c[a, b] = in_slot([P, KP], U32, "w1c%d0" % a, *((18, 1), (0, 0))[a])
                 elif a == 0:
@@ -169,7 +171,7 @@ def tile_list_coil_trust_weighting_kernel(
             gather_words(0, h)
         round_w1(nc.scalar.copy, 1, 0, 0, SPLIT)
         round_w1(nc.scalar.copy, 1, 0, SPLIT, P, SPLIT)
-        nc.scalar.mul(ntgt[:], tgt[:].rearrange("p b t -> p (b t)"), -1.0)
+        nc.scalar.mul(ntgt[0][:], tgt[0][:], -1.0)
         quant_w1(1, 0)
         for h in range(2):
             gather_words(1, h)
@@ -193,8 +195,8 @@ def tile_list_coil_trust_weighting_kernel(
 
         def leave_bank(func, dst, i, e):
             b, u, h = order[i]
-            column = PACK * b + 2 * u + e
-            nc.scalar.activation(dst, acc[i, e][:], func, bias=ntgt[:, column : column + 1])
+            t = 2 * u + e
+            nc.scalar.activation(dst, acc[i, e][:], func, bias=ntgt[b][:, t : t + 1])
 
         def open_pair(i):
             b, u, h = order[i]
@@ -245,8 +247,8 @@ def tile_list_coil_trust_weighting_kernel(
             weigh(i, e, place)
             gather(i, e)
 
-        def mask(first, second, between, place=None):
-            both = in_slot([P, 2, HALF], F32, "trust%d%d" % first, 16, len(acc) % 8)
+        def mask(first, second, between, place=None, home=None):
+            both = in_slot([P, 2, HALF], F32, "trust%d%d" % first, *(home or (16, len(acc) % 8)))
             raw = both if place is None else in_slot([P, 2, HALF], F32, "squares%d%d" % first, *place)
             for k, (i, e) in enumerate((first, second)):
                 square(i, e, raw[:, k, :])
@@ -371,12 +373,13 @@ def tile_list_coil_trust_weighting_kernel(
         residual(0, 1)
         multiply(0)
         round_w1(nc.vector.tensor_copy, 1, 1, 0, SHARE)
-        mask((2, 0), (3, 0), lambda: round_w1(nc.scalar.copy, 1, 1, SHARE, P))
+        mask((2, 0), (3, 0), lambda: round_w1(nc.scalar.copy, 1, 1, SHARE, P), home=(24, 0))
         quant_w1(1, 1)
         mask((2, 1), (3, 1), lambda: residual(2, 0), (5, 2))
         load_gains("gains_early", (4, 2), slice(0, 3), slice(0, HALF))
         load_gains("gains_late", (5, 1), slice(0, 3), slice(HALF, S))
         load_gains("gains_last", (24, 0), slice(3, 4), slice(0, S))
+        nc.scalar.mul(ntgt[1][:], tgt[1][:], -1.0)
         mask((4, 0), (6, 0), lambda: residual(2, 1))
         multiply(2)
         mask((4, 1), (6, 1), lambda: residual(4, 0), (23, 0))

@@ -309,7 +309,7 @@ def tile_list_coil_trust_weighting_kernel(
                 )
 
         def make_late_z(tile):
-            codes = in_slot([P, S], U32, "late_zc", 13)
+            codes = in_slot([P, S], U32, "late_zc", 0, 2)
             scales = keep.tile([P, S], U8, name="late_zs", align_bytes=64)
             for b in range(2):
                 zc[b, 1] = codes[:, HALF * b : HALF * (b + 1)]

@@ -28,7 +28,7 @@ SPLIT = 64
 EDGES = (0, 512, 1024, 1536, 1792, 2048)
 ON_VECTOR = 2
 RUN = 4
-SHARE = 104
+SHARE = 88
 EARLY = 256
 
 

@@ -28,7 +28,7 @@ SPLIT = 64
 EDGES = (0, 512, 1024, 1536, 1792, 2048)
 ON_VECTOR = 2
 RUN = 4
-SHARE = 88
+SHARE = 72
 EARLY = 256
 
 

from contextlib import ExitStack

import concourse.mybir as mybir

K, T, S, H, N, T2 = 1024, 2048, 1024, 1024, 512, 2048
FLOPS = 2 * K * H * S + 2 * H * N * S

F32 = mybir.dt.float32
BF16 = mybir.dt.bfloat16
I32 = mybir.dt.int32
U32 = mybir.dt.uint32
U16 = mybir.dt.uint16
U8 = mybir.dt.uint8
E4M3 = mybir.dt.float8_e4m3fn_x4
E5M2 = mybir.dt.float8_e5m2_x4
ACT = mybir.ActivationFunctionType
ALU = mybir.AluOpType

P = 128
PACK = 4
KP = P * PACK
HALF = 512
LCOL = HALF // 16
CHUNK = 512
SLOT = 8192
QUARTER = SLOT // 4
SPLIT = 64
EDGES = (0, 512, 1024, 1536, 1792, 2048)
ON_VECTOR = 2
RUN = 4
SHARE = 72
EARLY = 256


def tile_list_coil_trust_weighting_kernel(
    tc, tab_words, tab_scales, offs, w1, target, sT, w2_words, w2_scales, wgo, offs2, out_0, out_1, out_2
):
    nc = tc.nc
    with ExitStack() as ctx:
        keep = ctx.enter_context(tc.tile_pool(name="keep", bufs=1))
        slots = ctx.enter_context(tc.tile_pool(name="slots", bufs=1))
        psum = ctx.enter_context(tc.psum_pool(name="psum", bufs=1))

        def in_slot(shape, dtype, name, slot, quarter=0, extra=0):
            return slots.tile(shape, dtype, name=name, align_bytes=64, offset=SLOT * slot + QUARTER * quarter + extra)

        def grouped(name, cell):
            return in_slot([P, PACK * HALF], BF16, name, 18, 2 + 2 * cell)

        def half_list(offsets, h):
            return offsets[:, LCOL * h : LCOL * (h + 1)]

        pick = keep.tile([P, S // 16], U16, name="pick")
        place = keep.tile([P, S // 16], U16, name="place")
        tsc = in_slot([P, T], U8, "tsc", 18, 1)
        moved = keep.tile([P, S], U8, name="moved", align_bytes=64)
        w2sc_raw = keep.tile([P, N], U8, name="w2sc_raw", align_bytes=64)
        w2sc = in_slot([P, N], U8, "w2sc", 17, 2, N)
        w2raw = in_slot([P, 2, N], I32, "w2raw", 4)
        w2w = in_slot([P, 2, N], I32, "w2w", 17, 0, N)
        tgt = [keep.tile([P, PACK], F32, name="tgt%d" % b) for b in range(2)]
        ntgt = [keep.tile([P, PACK], F32, name="ntgt%d" % b) for b in range(2)]
        ycodes = keep.tile([P, T2], U32, name="ycodes", align_bytes=64)
        yscales = keep.tile([P, T2], U8, name="yscales", align_bytes=64)

        nc.vector.memset(tsc[:].bitcast(I32), 0)
        nc.vector.memset(moved[:].bitcast(I32), 0)
        nc.vector.memset(w2sc_raw[:].bitcast(I32), 0)
        pages = {t: in_slot([P, T2], F32, "page%d" % t, 10 + t) for t in range(3)}
        for t in range(3):
            nc.vector.memset(pages[t][:], 0.0)

        tabw = {}
        w1raw = {}
        margins = {}

        def load_tab(a):
            tabw[a] = in_slot([P, T], U32, "tabw%d" % a, a)
            nc.sync.dma_start(tabw[a][:].bitcast(I32), tab_words[a].rearrange("p t i -> p (t i)").bitcast(I32))

        def load_scales():
            rows = tab_scales.rearrange("a (q r) t -> r q a t", r=4)
            for r in range(4):
                nc.sync.dma_start(tsc[r:P:16, :].bitcast(I32), rows[r].bitcast(I32))

        def load_w1(a, b, lo=0, hi=P):
            tile = in_slot([P, PACK, PACK * (hi - lo)], F32, "w1raw%d%d%d" % (a, b, lo), 2 + 2 * b + a, lo // 32)
            w1raw[a, b, lo] = tile
            rows = w1[KP * a : KP * (a + 1), KP * b + PACK * lo : KP * b + PACK * hi]
            nc.sync.dma_start(tile[:], rows.rearrange("(p j) c -> p j c", j=PACK))

        sT_v = sT.rearrange("(b p t) c -> b t p c", b=2, t=PACK)

        def load_margins(b, t):
            margins[b, t] = in_slot([P, T], F32, "margins%d%d" % (b, t), 6 + t if b == 0 else (13, 2, 3, 1)[t])
            nc.sync.dma_start(margins[b, t][:], sT_v[b, t])

        target_v = target.rearrange("(b p t) -> b p t", b=2, t=PACK)
        load_w1(0, 0)
        nc.sync.dma_start(pick[:], offs)
        load_scales()
        load_w1(1, 0, 0, SPLIT)
        load_tab(0)
        nc.sync.dma_start(tgt[0][:], target_v[0])
        load_w1(1, 0, SPLIT, P)
        load_tab(1)
        load_w1(0, 1)
        load_margins(0, 0)
        load_margins(0, 1)
        load_w1(1, 1)
        load_margins(0, 2)
        load_margins(0, 3)
        nc.sync.dma_start(tgt[1][:], target_v[1])
        nc.sync.dma_start(place[:], offs2)
        for t in range(PACK):
            load_margins(1, t)
        nc.sync.dma_start(w2raw[:], w2_words.rearrange("a p c i -> p a (c i)").bitcast(I32))
        for q in range(4):
            nc.sync.dma_start(
                w2sc_raw[32 * q : 32 * q + 8, :].bitcast(I32), w2_scales[:, 4 * q : 4 * q + 4, :].bitcast(I32)
            )

        vw = {}
        vsc = {}

        def gather_words(a, h):
            vw[a, h] = keep.tile([P, HALF], U32, name="vw%d%d" % (a, h), align_bytes=64)
            nc.vector.tensor_copy(vw[a, h][:], tabw[a][:].indirect(half_list(pick, h)))

        def gather_scales():
            vsc[0] = keep.tile([P, S], U8, name="vsc", align_bytes=64)
            nc.vector.tensor_copy(vsc[0][:], tsc[:].indirect(pick[:]))
            vsc[1] = moved

        w1bf = {}
        w1c = {}
        w1s = {}

        def round_w1(copy, a, b, lo=0, hi=P, piece=0):
            if lo == 0:
                if a + b < 2:
                    w1bf[a, b] = grouped("w1bf%d%d" % (a, b), 2 * b + a)
                else:
                    w1bf[a, b] = in_slot([P, PACK * HALF], BF16, "w1bf11", 16)
                if b == 0:
                    w1c[a, b] = in_slot([P, KP], U32, "w1c%d0" % a, *((18, 1), (0, 0))[a])
                elif a == 0:
                    w1c[a, b] = keep.tile([P, KP], U32, name="w1c01", align_bytes=64)
                else:
                    w1c[a, b] = keep.tile([P, KP], U32, name="w1c11", align_bytes=64)
                w1s[a, b] = keep.tile([P, KP], U8, name="w1s%d%d" % (a, b), align_bytes=64)
            dst = w1bf[a, b][:].rearrange("p (u e m j) -> p u m j e", u=2, e=2, j=PACK)
            src = w1raw[a, b, piece][:].rearrange("p j (m u e) -> p u m j e", u=2, e=2)
            copy(dst[:, :, lo:hi], src[:, :, lo - piece : hi - piece])

        def quant_w1(a, b, lo=0, hi=KP):
            nc.vector.quantize_mx(
                out=w1c[a, b][:, lo:hi].bitcast(E4M3), scales=w1s[a, b][:, lo:hi], in_=w1bf[a, b][:, PACK * lo : PACK * hi]
            )

        def clear_page(t, slot):
            pages[t] = in_slot([P, T2], F32, "page%d" % t, slot)
            for c in range(T2 // CHUNK):
                nc.gpsimd.memset(pages[t][:, CHUNK * c : CHUNK * (c + 1)], 0.0)

        gather_scales()
        round_w1(nc.scalar.copy, 0, 0)
        nc.scalar.dma_start(moved[: P - 16, :].bitcast(I32), vsc[0][16:, :].bitcast(I32))
        quant_w1(0, 0)
        for h in range(2):
            gather_words(0, h)
        round_w1(nc.scalar.copy, 1, 0, 0, SPLIT)
        round_w1(nc.scalar.copy, 1, 0, SPLIT, P, SPLIT)
        nc.scalar.mul(ntgt[0][:], tgt[0][:], -1.0)
        quant_w1(1, 0)
        for h in range(2):
            gather_words(1, h)
        round_w1(nc.vector.tensor_copy, 0, 1)

        order = [(0, 0, 0), (0, 0, 1), (0, 1, 0), (0, 1, 1), (1, 0, 0), (1, 1, 0), (1, 0, 1), (1, 1, 1)]
        last = len(order) - 1
        res = {}
        acc = {}
        squares = {}
        trust = {}
        gated = {}
        zpairs = {}
        late_res = {}
        late_gated = {}
        zc = {}
        zs = {}

        def bank(n):
            return psum.tile([P, HALF], F32, name="bank%d" % n, tag="bank%d" % n, bufs=1)

        def leave_bank(func, dst, i, e):
            b, u, h = order[i]
            t = 2 * u + e
            nc.scalar.activation(dst, acc[i, e][:], func, bias=ntgt[b][:, t : t + 1])

        def open_pair(i):
            b, u, h = order[i]
            if h == 0:
                res[i] = in_slot([P, 2, HALF], F32, "res%d" % i, 20, 2 * u)[:]
                gated[i] = in_slot([P, 2, HALF], F32, "gated%d" % i, 21, 2 * u)[:]
                return
            if b not in late_res:
                late_res[b] = in_slot([P, PACK, HALF], F32, "late_res%d" % b, (23, 8)[b])
                late_gated[b] = in_slot([P, PACK, HALF], F32, "late_gated%d" % b, (22, 15)[b])
            res[i] = late_res[b][:, 2 * u : 2 * u + 2, :]
            gated[i] = late_gated[b][:, 2 * u : 2 * u + 2, :]

        def own_squares(i, e, *place):
            return in_slot([P, HALF], F32, "squares%d%d" % (i, e), *place)[:]

        def square(i, e, dst=None):
            b, u, h = order[i]
            t = 2 * u + e
            n = len(acc) % 8
            if i not in res:
                open_pair(i)
            acc[i, e] = bank(2 * (0, 1, 2, 3, 0, 0, 2, 1)[i] + e)
            for a in range(2):
                nc.tensor.matmul_mx(
                    out=acc[i, e][:],
                    lhsT=w1c[a, b][:, P * t : P * (t + 1)].bitcast(E4M3),
                    lhsT_scale=w1s[a, b][:, P * t : P * (t + 1)],
                    rhs=vw[a, h][:].bitcast(E5M2),
                    rhs_scale=vsc[a][:, HALF * h : HALF * (h + 1)],
                    start=(a == 0),
                    stop=(a == 1),
                )
            squares[i, e] = own_squares(i, e, 16, n) if dst is None else dst
            leave_bank(ACT.Square, squares[i, e], i, e)

        def weigh(i, e, place=None):
            trust[i, e] = squares[i, e] if place is None else in_slot([P, HALF], F32, "trust%d%d" % (i, e), *place)[:]
            nc.scalar.activation(trust[i, e], squares[i, e], ACT.Exp, scale=-1.0)

        def gather(i, e):
            b, u, h = order[i]
            nc.vector.tensor_tensor(
                gated[i][:, e, :], margins[b, 2 * u + e][:].indirect(half_list(pick, h)), trust[i, e], ALU.mult
            )

        def gate(i, e, place=None):
            weigh(i, e, place)
            gather(i, e)

        def mask(first, second, between, place=None, home=None):
            both = in_slot([P, 2, HALF], F32, "trust%d%d" % first, *(home or (16, len(acc) % 8)))
            raw = both if place is None else in_slot([P, 2, HALF], F32, "squares%d%d" % first, *place)
            for k, (i, e) in enumerate((first, second)):
                square(i, e, raw[:, k, :])
                trust[i, e] = both[:, k, :]
            between()
            nc.scalar.activation(both[:], raw[:], ACT.Exp, scale=-1.0)
            for i, e in (first, second):
                gather(i, e)

        def residual(i, e):
            leave_bank(ACT.Identity, res[i][:, e, :], i, e)

        def residuals(i):
            for e in range(2):
                residual(i, e)

        def multiply(i):
            b, u, h = order[i]
            if u == 0:
                zpairs[b] = in_slot([P, 2, HALF, 2], BF16, "zpairs%d" % b, *((14, 0), (8, 3))[b])
            nc.vector.scalar_tensor_tensor(
                zpairs[b][:, u],
                gated[i].rearrange("p e c -> p c e"),
                0.0,
                res[i].rearrange("p e c -> p c e"),
                ALU.max,
                ALU.mult,
            )

        def weave(pair_tile, tile):
            nc.scalar.copy(
                tile[:].bitcast(F32).rearrange("p (c u) -> p c u", u=2),
                pair_tile[:].rearrange("p u c e -> p u (c e)").bitcast(F32).rearrange("p u c -> p c u"),
            )

        def make_z(b, tiles):
            width = HALF // len(tiles)
            codes = in_slot([P, HALF], U32, "zc%d" % b, *((24, 2), (13, 2))[b])
            scales = in_slot([P, HALF], U8, "zs%d" % b, *((17, 2, 2 * N), (24, 3))[b])
            words = zpairs[b][:].rearrange("p u c e -> p u (c e)").bitcast(F32).rearrange("p u c -> p c u")
            for k, tile in enumerate(tiles):
                cols = slice(width * k, width * (k + 1))
                nc.scalar.copy(tile[:].bitcast(F32).rearrange("p (c u) -> p c u", u=2), words[:, cols])
                nc.vector.quantize_mx(out=codes[:, cols].bitcast(E4M3), scales=scales[:, cols], in_=tile[:])
            zc[b, 0] = codes[:]
            zs[b, 0] = scales[:]

        def late_product(tile, b):
            positive = late_gated[b] if b == 1 else in_slot([P, PACK, HALF], F32, "positive", 9)
            for lo in (0, EARLY):
                cols = slice(lo, lo + EARLY)
                nc.scalar.activation(positive[:, :, cols], late_gated[b][:, :, cols], ACT.Relu)
                nc.gpsimd.tensor_tensor(
                    tile[:, b, PACK * lo : PACK * (lo + EARLY)].rearrange("p (c i t) -> p c t i", i=RUN, t=PACK),
                    positive[:, :, cols].rearrange("p t (c i) -> p c t i", i=RUN),
                    late_res[b][:, :, cols].rearrange("p t (c i) -> p c t i", i=RUN),
                    ALU.mult,
                )

        def make_late_z(tile):
            codes = in_slot([P, S], U32, "late_zc", 0, 2)
            scales = keep.tile([P, S], U8, name="late_zs", align_bytes=64)
            for b in range(2):
                zc[b, 1] = codes[:, HALF * b : HALF * (b + 1)]
                zs[b, 1] = scales[:, HALF * b : HALF * (b + 1)]
                for lo, hi in ((0, HALF),) if b == 0 else ((0, EARLY), (EARLY, HALF)):
                    nc.vector.quantize_mx(
                        out=zc[b, 1][:, lo:hi].bitcast(E4M3),
                        scales=zs[b, 1][:, lo:hi],
                        in_=tile[:, b, PACK * lo : PACK * hi],
                    )

        gain = {}
        wgo_v = wgo.rearrange("(r t) s -> r t s", t=PACK)

        def load_gains(name, place, slices, cols):
            tile = in_slot([P, slices.stop - slices.start, cols.stop - cols.start], F32, name, *place)
            for q in (0, 2, 1, 3):
                nc.sync.dma_start(tile[32 * q : 32 * (q + 1)], wgo_v[:, slices, cols])
            for t in range(slices.start, slices.stop):
                gain[t, cols.start] = tile[:, t - slices.start, :]

        def make_step(t, h, n, lo=0, hi=HALF):
            acc2 = bank(n)
            passes = (0, 1) if t == 0 else (1, 0)
            for b in passes:
                nc.tensor.matmul_mx(
                    out=acc2[:, : hi - lo],
                    lhsT=w2w[:, b, P * t : P * (t + 1)].bitcast(E4M3),
                    lhsT_scale=w2sc[4 * b :, P * t : P * (t + 1)],
                    rhs=zc[b, h][:, lo:hi].bitcast(E4M3),
                    rhs_scale=zs[b, h][:, lo:hi],
                    start=(b == passes[0]),
                    stop=(b == passes[1]),
                )
            return acc2

        def place_step(t, lo, hi, step):
            first = lo // HALF * HALF
            nc.vector.tensor_tensor(pages[t][:].indirect(place[:, lo // 16 : hi // 16]), step, gain[t, first][:, lo - first : hi - first], ALU.mult)

        def sort_w2():
            nc.vector.tensor_copy(
                w2w[:].rearrange("p a (t m) -> p a m t", t=PACK),
                w2raw[:].rearrange("p a (m t) -> p a m t", t=PACK),
            )
            nc.vector.tensor_copy(
                w2sc[:].rearrange("p (t m) -> p m t", t=PACK), w2sc_raw[:].rearrange("p (m t) -> p m t", t=PACK)
            )

        quant_w1(0, 1)
        square(0, 0)
        square(0, 1)
        gate(0, 0)
        square(1, 0)
        weigh(0, 1)
        gate(1, 0)
        gather(0, 1)
        square(1, 1)
        residual(0, 0)
        gate(1, 1)
        residual(0, 1)
        multiply(0)
        round_w1(nc.vector.tensor_copy, 1, 1, 0, SHARE)
        mask((2, 0), (3, 0), lambda: round_w1(nc.scalar.copy, 1, 1, SHARE, P), home=(24, 0))
        quant_w1(1, 1)
        mask((2, 1), (3, 1), lambda: residual(2, 0), (5, 2))
        load_gains("gains_early", (4, 2), slice(0, 3), slice(0, HALF))
        load_gains("gains_late", (5, 1), slice(0, 3), slice(HALF, S))
        load_gains("gains_last", (24, 0), slice(3, 4), slice(0, S))
        nc.scalar.mul(ntgt[1][:], tgt[1][:], -1.0)
        mask((4, 0), (6, 0), lambda: residual(2, 1))
        multiply(2)
        mask((4, 1), (6, 1), lambda: residual(4, 0), (23, 0))
        residual(4, 1)
        multiply(4)
        residuals(1)
        for e in range(2):
            square(5, e)
        for e in range(2):
            gate(5, e)
        square(7, 1, own_squares(7, 1, 18, 4))
        square(7, 0, own_squares(7, 0, 18, 2))
        gate(7, 1, (17, 2))
        residuals(5)
        multiply(5)
        sort_w2()
        make_z(0, [grouped("zbf0", 1)])
        residuals(3)
        make_z(1, [in_slot([P, PACK * EARLY], BF16, "zbf1%d" % k, 2, 2 + k) for k in range(2)])
        gate(7, 0, (21, 2))
        late_zbf = in_slot([P, 2, PACK * HALF], BF16, "late_zbf", 2, 2)
        late_product(late_zbf, 0)
        residuals(6)
        residuals(7)
        late_product(late_zbf, 1)

        steps = {t: in_slot([P, S], F32, "step%d" % t, *((6, 0), (6, 2), (15, 0), (23, 0))[t]) for t in range(PACK)}
        widths = (HALF, HALF, EARLY)
        gained = [in_slot([P, widths[t]], F32, "gained%d" % t, *((0, 2), (0, 3), (13, 0))[t]) for t in range(3)]
        banks = [make_step(t, 0, (0, 1, 6, 7)[t]) for t in range(PACK)]

        def apply_gain(t):
            nc.vector.tensor_tensor(gained[t][:], banks[t][:, : widths[t]], gain[t, 0][:, : widths[t]], ALU.mult)

        def place_gained(t):
            nc.vector.tensor_copy(pages[t][:].indirect(place[:, : widths[t] // 16]), gained[t][:])

        apply_gain(0)
        place_gained(0)
        apply_gain(1)
        apply_gain(2)
        place_gained(1)
        place_gained(2)
        nc.scalar.copy(steps[2][:, EARLY:HALF], banks[2][:, EARLY:])
        nc.scalar.copy(steps[3][:, :HALF], banks[3][:])
        make_late_z(late_zbf)
        clear_page(3, 3)
        place_step(2, EARLY, HALF, steps[2][:, EARLY:HALF])
        for lo in (0, EARLY):
            first = make_step(0, 1, 2 + lo // EARLY, lo, lo + EARLY)
            nc.scalar.copy(steps[0][:, HALF + lo : HALF + lo + EARLY], first[:, :EARLY])
        for t in (2, 1, 3):
            nc.scalar.copy(steps[t][:, HALF:], make_step(t, 1, (None, 5, 4, 2)[t])[:])

        out_v = out_0.rearrange("(p t) m -> p t m", t=PACK)
        chunks = [slice(lo, hi) for lo, hi in zip(EDGES, EDGES[1:])]
        pairs = [in_slot([P, 2, c.stop - c.start, 2], BF16, "pairs%d" % c.start, 8, c.start // 256) for c in chunks]
        ybf = [in_slot([P, PACK * (c.stop - c.start)], BF16, "ybf%d" % c.start, 1, c.start // 256) for c in chunks]
        for t in (0, 2, 1, 3):
            lo = HALF if t < 3 else 0
            place_step(t, lo, S, steps[t][:, lo:])
            nc.sync.dma_start(out_v[:, t, :], pages[t][:])
            for c, cols in enumerate(chunks):
                src = pages[t][:, cols]
                if t == 2 and c < ON_VECTOR:
                    nc.scalar.copy(pairs[c][:, 1], src.unsqueeze(2).to_broadcast([P, cols.stop - cols.start, 2]))
                elif t < 3:
                    nc.scalar.copy(pairs[c][:, t // 2, :, t % 2], src)
                if t == 1 and 0 < c <= ON_VECTOR:
                    weave(pairs[c - 1], ybf[c - 1])

        words_v = out_1[0].rearrange("p m t -> p (m t)").bitcast(I32)
        for c, cols in enumerate(chunks):
            if c < ON_VECTOR:
                nc.vector.tensor_copy(ybf[c][:].rearrange("p (m t) -> p m t", t=PACK)[:, :, 3], pages[3][:, cols])
            else:
                nc.scalar.copy(pairs[c][:, 1, :, 1], pages[3][:, cols])
                if c > ON_VECTOR:
                    weave(pairs[c - 1], ybf[c - 1])
        weave(pairs[-1], ybf[-1])
        for c, cols in enumerate(chunks):
            nc.vector.quantize_mx(out=ycodes[:, cols].bitcast(E4M3), scales=yscales[:, cols], in_=ybf[c][:])
            nc.sync.dma_start(words_v[:, cols], ycodes[:, cols].bitcast(I32))
        for q in range(4):
            queue = nc.sync if q % 2 == 0 else nc.scalar
            queue.dma_start(out_2[0, 4 * q : 4 * q + 4, :].bitcast(I32), yscales[32 * q : 32 * q + 4, :].bitcast(I32))
